import numpy as np
import ml_dtypes


def mxq(x, axis, fmt="e4m3"):
    dtype, down = {"e4m3": (ml_dtypes.float8_e4m3fn, 7), "e5m2": (ml_dtypes.float8_e5m2, 14)}[fmt]
    v = np.moveaxis(np.asarray(x, np.float32).astype(ml_dtypes.bfloat16).astype(np.float64), axis, -1)
    blocks = v.reshape(v.shape[:-1] + (-1, 32))
    amax = np.abs(blocks).max(-1, keepdims=True)
    byte = np.maximum(np.where(amax > 0, np.frexp(amax)[1] - 1 + 127, 0) - down, 1)
    scale = np.exp2(byte - 127.0)
    codes = (blocks / scale).astype(np.float32).astype(dtype).astype(np.float64)
    return np.moveaxis((codes * scale).reshape(v.shape), -1, axis)


WIDE = False


def mx_kscale(k):
    if not WIDE:
        return np.ones(k)
    levels = np.array([24, -24, 12, -12, 0])
    if k % 512:
        return np.exp2(np.random.permutation(np.resize(levels, k // 32))).repeat(32)
    a = np.empty((k // 512, 16))
    for p in range(k // 512):
        a[p, :8] = np.random.permutation(np.resize(levels, 8))
        for g in range(8):
            far = levels[np.abs(levels - a[p, g]) >= 10]
            a[p, g + 8] = far[np.random.randint(len(far))]
    return np.exp2(a.ravel()).repeat(32)


def f64(x):
    return np.asarray(x).astype(np.float64)


def striped8(idx):
    return np.concatenate([v.reshape(-1, 16).T for v in idx]).astype(np.uint16)


def unstriped8(offs):
    return np.stack([offs[16 * g:16 * g + 16].T.reshape(-1) for g in range(8)]).astype(np.int64)


E2M1 = np.array([0.0, 0.5, 1.0, 1.5, 2.0, 3.0, 4.0, 6.0, -0.0, -0.5, -1.0, -1.5, -2.0, -3.0, -4.0, -6.0])


def pack_weight(w, fmt):
    k, n = w.shape
    w = f64(np.asarray(w, np.float32).astype(ml_dtypes.bfloat16)).reshape(k // 32, 32, n)
    amax = np.abs(w).max(1)
    if fmt == "e4m3":
        byte = np.frexp(amax)[1] - 1 + 127 - 7
    else:
        mant, ex = np.frexp(amax / 6.0)
        byte = np.where(mant > 0.5, ex, ex - 1) + 127
    byte = np.clip(np.where(amax > 0, byte, 1), 1, 254)
    scaled = (w * np.exp2(127.0 - byte)[:, None, :]).reshape(k, n).astype(np.float32)
    by_word = np.ascontiguousarray(scaled.reshape(k // 512, 128, 4, n).transpose(0, 1, 3, 2))
    if fmt == "e4m3":
        words = by_word.astype(ml_dtypes.float8_e4m3fn).view(np.uint8)
    else:
        c = by_word.astype(ml_dtypes.float4_e2m1fn).view(np.uint8) & 0xF
        words = (c[..., 0::2] | (c[..., 1::2] << 4)).reshape(k // 512, 128, 2 * n)
    return np.ascontiguousarray(words), np.ascontiguousarray(byte.astype(np.uint8).reshape(k // 512, 16, n))


def unpack_weight(words, scales, fmt):
    g, _, n = scales.shape
    words = np.ascontiguousarray(words).reshape(g, 128, n, -1)
    if fmt == "e4m3":
        vals = words.view(ml_dtypes.float8_e4m3fn).astype(np.float64)
    else:
        nib = np.empty((g, 128, n, 4), np.uint8)
        nib[..., 0::2] = words & 0xF
        nib[..., 1::2] = words >> 4
        vals = E2M1[nib]
    vals = vals * np.repeat(np.exp2(scales.astype(np.float64) - 127.0), 8, axis=1)[..., None]
    return vals.transpose(0, 1, 3, 2).reshape(g * 512, n)


K, R, N, T, J = 1024, 1024, 512, 2048, 1024


def setup_inputs():
    n = np.random.standard_normal
    s = mx_kscale(K)[:, None]
    u = mx_kscale(R)[:, None]
    wd = n((R, N)) / np.sqrt(R) / u
    p_wg = pack_weight(n((K, R)) / np.sqrt(K) / s, "e4m3")
    p_wd8 = pack_weight(wd[:512], "e4m3")
    p_wd4 = pack_weight(wd[512:], "e2m1")
    return {
        "xT": (n((K, T)) * s).astype(np.float32),
        "wgt": np.repeat(np.random.uniform(0.5, 2.0, (8, J)), 16, axis=0).astype(np.float32),
        "wg_words": p_wg[0],
        "wg_scales": p_wg[1],
        "wu": (n((K, R)) / np.sqrt(K) / s * u.T).astype(np.float32),
        "wd8_words": p_wd8[0],
        "wd8_scales": p_wd8[1],
        "wd4_words": p_wd4[0],
        "wd4_scales": p_wd4[1],
        "b": (0.3 * n(N)).astype(np.float32),
        "wgo": np.repeat(np.random.uniform(0.5, 2.0, (8, J)), 16, axis=0).astype(np.float32),
        "offs": striped8(np.stack([np.random.permutation(T)[:J] for _ in range(8)])),
        "offs2": striped8(np.stack([np.random.permutation(T)[:J] for _ in range(8)])),
    }


def reference(xT, wgt, wg_words, wg_scales, wu, wd8_words, wd8_scales, wd4_words, wd4_scales, b, wgo, offs, offs2):
    idx = unstriped8(offs)
    idx2 = unstriped8(offs2)
    rows = np.arange(K)
    xg = f64(wgt)[rows // 4 % 128] * f64(xT)[rows[:, None], idx[rows % 512 // 64]]
    xT_ = mxq(xg, 0, "e4m3")
    wg_ = unpack_weight(wg_words, wg_scales, "e4m3")
    wu_ = mxq(f64(wu), 0, "e4m3")
    ga = wg_.T @ xT_
    ub = wu_.T @ xT_
    h = np.tanh(ga) * ub
    h_ = mxq(h, 0, "e4m3")
    wd8_ = unpack_weight(wd8_words, wd8_scales, "e4m3")
    wd4_ = unpack_weight(wd4_words, wd4_scales, "e2m1")
    y = wd8_.T @ h_[:512] + wd4_.T @ h_[512:]
    out = np.zeros((N, T))
    rows = np.arange(N)
    out[rows[:, None], idx2[rows % 128 // 16]] = f64(wgo)[rows % 128] * (y + f64(b)[:, None])
    return out

@@ -1,0 +1,269 @@
+from contextlib import ExitStack
+
+import concourse.mybir as mybir
+
+K, R, N, T, J = 1024, 1024, 512, 2048, 1024
+FLOPS = 2 * J * (2 * K * R + R * N)
+
+F32 = mybir.dt.float32
+BF16 = mybir.dt.bfloat16
+I32 = mybir.dt.int32
+U16 = mybir.dt.uint16
+U8 = mybir.dt.uint8
+FP8X4 = mybir.dt.float8_e4m3fn_x4
+FP4X4 = mybir.dt.float4_e2m1fn_x4
+MULT = mybir.AluOpType.mult
+ACT = mybir.ActivationFunctionType
+
+P = 128
+PACK = 4
+PASS = P * PACK
+HALF = 512
+LIST_COLS = HALF // 16
+UNIT = 128
+
+
+def tile_list_tanh_mix_scatb_kernel(
+    tc, xT, wgt, wg_words, wg_scales, wu, wd8_words, wd8_scales, wd4_words, wd4_scales, b, wgo, offs, offs2, out
+):
+    nc = tc.nc
+    with ExitStack() as ctx:
+        keep = ctx.enter_context(tc.tile_pool(name="keep", bufs=1))
+        psum = ctx.enter_context(tc.psum_pool(name="psum", bufs=3))
+        psum_y = ctx.enter_context(tc.psum_pool(name="psum_y", bufs=2))
+
+        pick_list = keep.tile([P, J // 16], U16, name="pick_list")
+        place_list = keep.tile([P, J // 16], U16, name="place_list")
+        planes = [[keep.tile([P, T], F32, name=f"x{a}{i}") for i in range(PACK)] for a in range(2)]
+        pages = [keep.tile([P, T], F32, name=f"page{n}") for n in range(4)]
+        last_picked = keep.tile([P, PACK, HALF], F32, name="last_picked")
+        wgt_second = keep.tile([P, HALF], F32, name="wgt_second")
+        wgt_half = [last_picked[:, 2, :], wgt_second[:]]
+        wgo_sb = keep.tile([P, J], F32, name="wgo_sb")
+        bias = keep.tile([P, 4], F32, name="bias")
+        warm = keep.tile([P, 8], F32, name="warm")
+        wg_raw = keep.tile([P, 2 * R], I32, name="wg_raw", tag="wg_raw_hq", align_bytes=64)
+        wg_sc_raw = keep.tile([P, R], U8, name="wg_sc_raw", align_bytes=64)
+        wg_codes = keep.tile([P, 2 * R], I32, name="wg_codes", align_bytes=64)
+        wg_sc = keep.tile([P, R], U8, name="wg_sc", align_bytes=64)
+        wd8_codes = keep.tile([P, N], I32, name="wd8_codes", align_bytes=64)
+        wd4_codes = keep.tile([P, 2 * N], U8, name="wd4_codes", align_bytes=64)
+        wd8_sc = keep.tile([P, N], U8, name="wd8_sc", align_bytes=64)
+        wd4_sc = keep.tile([P, N], U8, name="wd4_sc", align_bytes=64)
+
+        def quantised(name):
+            codes = keep.tile([P, HALF], I32, name=name + "_codes", align_bytes=64)
+            scales = keep.tile([P, HALF], U8, name=name + "_scales", align_bytes=64)
+            return codes, scales
+
+        xq = {(a, c): quantised(f"xq{a}{c}") for a in range(2) for c in range(2)}
+        wuq = {(a, h): quantised(f"wuq{a}{h}") for a in range(2) for h in range(2)}
+
+        rounded = [keep.tile([P, PACK * HALF], BF16, name=f"rounded{s}", align_bytes=64) for s in range(6)]
+        x_slot = {(0, 0): 0, (0, 1): 1, (1, 0): 5, (1, 1): 0}
+        wu_slot = {(0, 0): 2, (1, 0): 3, (0, 1): 4, (1, 1): 1}
+        x_rows = xT.rearrange("(a p i) t -> a i p t", a=2, i=PACK)
+        wu_raw = {}
+
+        def load_x(a, i):
+            nc.sync.dma_start(out=planes[a][i][:], in_=x_rows[a, i])
+
+        def load_wu(a, h):
+            raw = keep.tile([P, PACK, HALF], F32, name=f"wu_raw{a}{h}")
+            rows = wu[a * PASS : (a + 1) * PASS, h * PASS : (h + 1) * PASS]
+            nc.sync.dma_start(out=raw[:], in_=rows.rearrange("(p i) r -> p i r", i=PACK))
+            wu_raw[a, h] = raw
+
+        def load_scale_rows(tile, first_row, rows):
+            for q in range(4):
+                nc.sync.dma_start(
+                    out=tile[32 * q + first_row : 32 * q + first_row + 4, :].bitcast(I32),
+                    in_=rows[4 * q : 4 * q + 4, :].bitcast(I32),
+                )
+
+        def quantise(dst, src):
+            codes, scales = dst
+            nc.vector.quantize_mx(out=codes[:].bitcast(FP8X4), scales=scales[:], in_=src[:])
+
+        for tile in (wg_sc_raw, wd8_sc, wd4_sc):
+            nc.vector.memset(tile[:].bitcast(I32), 0)
+        nc.vector.memset(warm[:], 0.0)
+        nc.scalar.activation(out=warm[:, 4:8], in_=warm[:, 0:4], func=ACT.Tanh)
+        for page in pages:
+            nc.gpsimd.memset(page[:], 0.0)
+
+        picked = {}
+        for a, c in ((0, 0), (0, 1), (1, 0)):
+            picked[a, c] = keep.tile([P, PACK, HALF], F32, name=f"picked{a}{c}")
+        picked[1, 1] = last_picked
+
+        nc.sync.dma_start(pick_list[:], offs)
+        load_x(0, 0)
+        nc.sync.dma_start(out=wgt_half[0], in_=wgt[:, 0:HALF])
+        nc.sync.dma_start(out=wgt_half[1], in_=wgt[:, HALF:J])
+        load_x(0, 1)
+        load_x(0, 2)
+        load_wu(0, 0)
+        load_x(0, 3)
+        load_wu(1, 0)
+        load_x(1, 0)
+        load_x(1, 1)
+        load_x(1, 2)
+        load_x(1, 3)
+        for a in range(2):
+            load_scale_rows(wg_sc_raw, 4 * a, wg_scales[a])
+        nc.sync.dma_start(
+            out=wg_raw[:].rearrange("p (a r) -> p a r", a=2),
+            in_=wg_words.rearrange("a p r i -> p a (r i)").bitcast(I32),
+        )
+        load_wu(0, 1)
+        load_wu(1, 1)
+        load_scale_rows(wd8_sc, 0, wd8_scales[0])
+        load_scale_rows(wd4_sc, 0, wd4_scales[0])
+        nc.sync.dma_start(out=wd8_codes[:], in_=wd8_words[0].rearrange("p n i -> p (n i)").bitcast(I32))
+        nc.sync.dma_start(out=wd4_codes[:].bitcast(I32), in_=wd4_words[0].bitcast(I32))
+        with nc.allow_non_contiguous_dma(reason="one bias value for each partition and output tile"):
+            nc.sync.dma_start(out=bias[:], in_=b.rearrange("(n p) -> p n", p=P))
+        nc.sync.dma_start(place_list[:], offs2)
+        nc.sync.dma_start(out=wgo_sb[:], in_=wgo)
+
+        def gather(a, i, c):
+            offsets = pick_list[:, c * LIST_COLS : (c + 1) * LIST_COLS]
+            nc.vector.tensor_tensor(picked[a, c][:, i, :], planes[a][i][:].indirect(offsets), wgt_half[c], MULT)
+
+        def round_x(a, c):
+            grouped = rounded[x_slot[a, c]]
+            nc.scalar.copy(
+                out=grouped[:].rearrange("p (g e i) -> p g i e", e=4, i=PACK),
+                in_=picked[a, c][:].rearrange("p i (g e) -> p g i e", e=4),
+            )
+            return grouped
+
+        def round_wu(a, h):
+            grouped = rounded[wu_slot[a, h]]
+            nc.scalar.copy(
+                out=grouped[:].rearrange("p (t q i) -> p q i t", t=PACK, i=PACK),
+                in_=wu_raw[a, h][:].rearrange("p i (q t) -> p q i t", t=PACK),
+            )
+            return grouped
+
+        def deal_wg():
+            nc.vector.tensor_copy(
+                out=wg_codes[:].rearrange("p (g t q) -> p g q t", t=PACK, q=P),
+                in_=wg_raw[:].rearrange("p (g q t) -> p g q t", t=PACK, q=P),
+            )
+            nc.vector.tensor_copy(
+                out=wg_sc[:].rearrange("p (g t q) -> p g t q", t=PACK, q=P),
+                in_=wg_sc_raw[:].rearrange("p (g q t) -> p g t q", t=PACK, q=P),
+            )
+
+        def hidden(c, h):
+            grouped = rounded[2 + 2 * c + h]
+            for u in range(HALF // UNIT):
+                cols = slice(u * UNIT, (u + 1) * UNIT)
+                gate = psum.tile([P, PACK, UNIT], F32, name="gate")
+                up = psum.tile([P, PACK, UNIT], F32, name="up")
+                for t in range(PACK):
+                    for a in range(2):
+                        lo = h * PASS + t * P
+                        nc.tensor.matmul_mx(
+                            out=gate[:, t, :],
+                            lhsT=wg_codes[:, a * R + lo : a * R + lo + P].bitcast(FP8X4),
+                            lhsT_scale=wg_sc[4 * a :, lo : lo + P],
+                            rhs=xq[a, c][0][:, cols].bitcast(FP8X4),
+                            rhs_scale=xq[a, c][1][:, cols],
+                            start=(a == 0),
+                            stop=(a == 1),
+                        )
+                for t in range(PACK):
+                    for a in range(2):
+                        nc.tensor.matmul_mx(
+                            out=up[:, t, :],
+                            lhsT=wuq[a, h][0][:, t * P : (t + 1) * P].bitcast(FP8X4),
+                            lhsT_scale=wuq[a, h][1][:, t * P : (t + 1) * P],
+                            rhs=xq[a, c][0][:, cols].bitcast(FP8X4),
+                            rhs_scale=xq[a, c][1][:, cols],
+                            start=(a == 0),
+                            stop=(a == 1),
+                        )
+                gated = wu_raw[h, 0][:, u, :].rearrange("p (j t) -> p j t", t=PACK)
+                nc.scalar.activation(out=gated, in_=gate[:].rearrange("p t j -> p j t"), func=ACT.Tanh)
+                nc.vector.tensor_tensor(
+                    grouped[:, u * PACK * UNIT : (u + 1) * PACK * UNIT].rearrange("p (j t) -> p j t", t=PACK),
+                    up[:].rearrange("p t j -> p j t"),
+                    gated,
+                    MULT,
+                )
+            return grouped
+
+        for i in range(PACK):
+            for c in range(2):
+                gather(0, i, c)
+            if i == 2:
+                quantise(wuq[0, 0], round_wu(0, 0))
+        g00 = round_x(0, 0)
+        g01 = round_x(0, 1)
+        w10 = round_wu(1, 0)
+        gather(1, 0, 0)
+        gather(1, 0, 1)
+        quantise(xq[0, 0], g00)
+        gather(1, 1, 0)
+        gather(1, 1, 1)
+        quantise(xq[0, 1], g01)
+        gather(1, 2, 0)
+        quantise(wuq[1, 0], w10)
+        gather(1, 3, 0)
+        g10 = round_x(1, 0)
+        gather(1, 2, 1)
+        gather(1, 3, 1)
+        quantise(xq[1, 0], g10)
+        deal_wg()
+        w01 = round_wu(0, 1)
+        w11 = round_wu(1, 1)
+        g11 = round_x(1, 1)
+
+        hq_codes = keep.tile([P, 4 * HALF], I32, name="hq_codes", tag="wg_raw_hq", align_bytes=64)
+        hq_scales = keep.tile([P, 4 * HALF], U8, name="hq_scales", align_bytes=64)
+
+        def hq(c, h):
+            lo = (2 * c + h) * HALF
+            return hq_codes[:, lo : lo + HALF], hq_scales[:, lo : lo + HALF]
+
+        def quantise_h(c, h, grouped):
+            codes, scales = hq(c, h)
+            nc.vector.quantize_mx(out=codes.bitcast(FP8X4), scales=scales, in_=grouped[:])
+
+        def output(c, n):
+            acc = psum_y.tile([P, HALF], F32, name="acc")
+            cols = slice(n * P, (n + 1) * P)
+            nc.tensor.matmul_mx(
+                out=acc[:], lhsT=wd8_codes[:, cols].bitcast(FP8X4), lhsT_scale=wd8_sc[:, cols],
+                rhs=hq(c, 0)[0].bitcast(FP8X4), rhs_scale=hq(c, 0)[1], start=True, stop=False,
+            )
+            nc.tensor.matmul_mx(
+                out=acc[:], lhsT=wd4_codes[:, 2 * n * P : 2 * (n + 1) * P].bitcast(FP4X4), lhsT_scale=wd4_sc[:, cols],
+                rhs=hq(c, 1)[0].bitcast(FP8X4), rhs_scale=hq(c, 1)[1], start=False, stop=True,
+            )
+            y = picked[0, c][:, n, :]
+            nc.scalar.activation(out=y, in_=acc[:], func=ACT.Identity, bias=bias[:, n : n + 1])
+            offsets = place_list[:, c * LIST_COLS : (c + 1) * LIST_COLS]
+            nc.vector.tensor_tensor(pages[n][:].indirect(offsets), y, wgo_sb[:, c * HALF : (c + 1) * HALF], MULT)
+
+        h00 = hidden(0, 0)
+        quantise(wuq[0, 1], w01)
+        quantise(wuq[1, 1], w11)
+        quantise(xq[1, 1], g11)
+        quantise_h(0, 0, h00)
+        h01 = hidden(0, 1)
+        quantise_h(0, 1, h01)
+        h10 = hidden(1, 0)
+        output(0, 0)
+        quantise_h(1, 0, h10)
+        output(0, 1)
+        h11 = hidden(1, 1)
+        output(0, 2)
+        quantise_h(1, 1, h11)
+        output(0, 3)
+        for n in range(4):
+            output(1, n)
+            nc.sync.dma_start(out=out[n * P : (n + 1) * P, :], in_=pages[n][:])

@@ -1,6 +1,7 @@
 from contextlib import ExitStack
 
 import concourse.mybir as mybir
+from concourse.masks import make_identity
 
 K, R, N, T, J = 1024, 1024, 512, 2048, 1024
 FLOPS = 2 * J * (2 * K * R + R * N)
@@ -19,8 +20,8 @@ P = 128
 PACK = 4
 PASS = P * PACK
 HALF = 512
-LIST_COLS = HALF // 16
 UNIT = 128
+CHUNKS = ((0, 256), (256, 512), (512, 1024))
 
 
 def tile_list_tanh_mix_scatb_kernel(
@@ -36,234 +37,282 @@ def tile_list_tanh_mix_scatb_kernel(
         place_list = keep.tile([P, J // 16], U16, name="place_list")
         planes = [[keep.tile([P, T], F32, name=f"x{a}{i}") for i in range(PACK)] for a in range(2)]
         pages = [keep.tile([P, T], F32, name=f"page{n}") for n in range(4)]
-        last_picked = keep.tile([P, PACK, HALF], F32, name="last_picked")
-        wgt_second = keep.tile([P, HALF], F32, name="wgt_second")
-        wgt_half = [last_picked[:, 2, :], wgt_second[:]]
+        picked = {(a, c): keep.tile([P, PACK, HALF], F32, name=f"picked{a}{c}") for a in range(2) for c in range(2)}
+        wu_raw = {(a, h): keep.tile([P, PACK, HALF], F32, name=f"wu_raw{a}{h}") for a in range(2) for h in range(2)}
+        wgt_half = [keep.tile([P, HALF], F32, name=f"wgt{c}") for c in range(2)]
         wgo_sb = keep.tile([P, J], F32, name="wgo_sb")
+        bias_rows = keep.tile([P, P], F32, name="bias_rows")
+        identity = keep.tile([P, P], F32, name="identity")
         bias = keep.tile([P, 4], F32, name="bias")
         warm = keep.tile([P, 8], F32, name="warm")
-        wg_raw = keep.tile([P, 2 * R], I32, name="wg_raw", tag="wg_raw_hq", align_bytes=64)
+        wg_raw = [keep.tile([P, 2 * PASS], I32, name=f"wg_raw{h}", align_bytes=64) for h in range(2)]
+        wg_codes = [keep.tile([P, 2 * PASS], I32, name=f"wg_codes{h}", align_bytes=64) for h in range(2)]
         wg_sc_raw = keep.tile([P, R], U8, name="wg_sc_raw", align_bytes=64)
-        wg_codes = keep.tile([P, 2 * R], I32, name="wg_codes", align_bytes=64)
         wg_sc = keep.tile([P, R], U8, name="wg_sc", align_bytes=64)
         wd8_codes = keep.tile([P, N], I32, name="wd8_codes", align_bytes=64)
         wd4_codes = keep.tile([P, 2 * N], U8, name="wd4_codes", align_bytes=64)
         wd8_sc = keep.tile([P, N], U8, name="wd8_sc", align_bytes=64)
         wd4_sc = keep.tile([P, N], U8, name="wd4_sc", align_bytes=64)
+        x_codes = [keep.tile([P, J], I32, name=f"x_codes{a}", align_bytes=64) for a in range(2)]
+        x_sc = [keep.tile([P, J], U8, name=f"x_sc{a}", align_bytes=64) for a in range(2)]
+        wu_codes = [keep.tile([P, R], I32, name=f"wu_codes{a}", align_bytes=64) for a in range(2)]
+        wu_sc = [keep.tile([P, R], U8, name=f"wu_sc{a}", align_bytes=64) for a in range(2)]
+        h_codes = wg_raw
+        h_sc = [keep.tile([P, J], U8, name=f"h_sc{h}", align_bytes=64) for h in range(2)]
+        rounded = [keep.tile([P, PACK * HALF], BF16, name=f"rounded{s}", align_bytes=64) for s in range(5)]
+        late_planes = picked[1, 1][:, 2:4, :].rearrange("p i j -> p (i j)").bitcast(BF16)
+        x_rounded = {(0, 0): rounded[0], (0, 1): rounded[1], (1, 0): late_planes, (1, 1): rounded[0]}
+        wu_rounded = {(0, 0): rounded[2], (1, 0): rounded[3], (0, 1): rounded[4], (1, 1): rounded[0]}
+        h_rounded = {(0, 0): rounded[2], (1, 0): rounded[3], (0, 1): rounded[1], (1, 1): rounded[4]}
 
-        def quantised(name):
-            codes = keep.tile([P, HALF], I32, name=name + "_codes", align_bytes=64)
-            scales = keep.tile([P, HALF], U8, name=name + "_scales", align_bytes=64)
-            return codes, scales
-
-        xq = {(a, c): quantised(f"xq{a}{c}") for a in range(2) for c in range(2)}
-        wuq = {(a, h): quantised(f"wuq{a}{h}") for a in range(2) for h in range(2)}
-
-        rounded = [keep.tile([P, PACK * HALF], BF16, name=f"rounded{s}", align_bytes=64) for s in range(6)]
-        x_slot = {(0, 0): 0, (0, 1): 1, (1, 0): 5, (1, 1): 0}
-        wu_slot = {(0, 0): 2, (1, 0): 3, (0, 1): 4, (1, 1): 1}
         x_rows = xT.rearrange("(a p i) t -> a i p t", a=2, i=PACK)
-        wu_raw = {}
 
         def load_x(a, i):
             nc.sync.dma_start(out=planes[a][i][:], in_=x_rows[a, i])
 
         def load_wu(a, h):
-            raw = keep.tile([P, PACK, HALF], F32, name=f"wu_raw{a}{h}")
             rows = wu[a * PASS : (a + 1) * PASS, h * PASS : (h + 1) * PASS]
-            nc.sync.dma_start(out=raw[:], in_=rows.rearrange("(p i) r -> p i r", i=PACK))
-            wu_raw[a, h] = raw
+            nc.sync.dma_start(out=wu_raw[a, h][:], in_=rows.rearrange("(p i) r -> p i r", i=PACK))
 
-        def load_scale_rows(tile, first_row, rows):
+        def load_wg(h):
+            words = wg_words[:, :, h * PASS : (h + 1) * PASS, :].rearrange("a p r i -> p a (r i)")
+            nc.sync.dma_start(out=wg_raw[h][:].rearrange("p (a r) -> p a r", a=2), in_=words.bitcast(I32))
+
+        def load_scale_rows(queue, tile, rows):
+            passes = rows.shape[0]
             for q in range(4):
-                nc.sync.dma_start(
-                    out=tile[32 * q + first_row : 32 * q + first_row + 4, :].bitcast(I32),
-                    in_=rows[4 * q : 4 * q + 4, :].bitcast(I32),
+                queue.dma_start(
+                    out=tile[32 * q : 32 * q + 4 * passes, :].bitcast(I32),
+                    in_=rows[:, 4 * q : 4 * q + 4, :].bitcast(I32),
                 )
 
-        def quantise(dst, src):
-            codes, scales = dst
-            nc.vector.quantize_mx(out=codes[:].bitcast(FP8X4), scales=scales[:], in_=src[:])
-
-        for tile in (wg_sc_raw, wd8_sc, wd4_sc):
-            nc.vector.memset(tile[:].bitcast(I32), 0)
         nc.vector.memset(warm[:], 0.0)
         nc.scalar.activation(out=warm[:, 4:8], in_=warm[:, 0:4], func=ACT.Tanh)
+        for tile in (wg_sc_raw, wd8_sc, wd4_sc):
+            nc.vector.memset(tile[:].bitcast(I32), 0)
+        nc.vector.memset(bias_rows[:], 0.0)
+        make_identity(nc, identity[:])
+        nc.gpsimd.dma_start(out=bias_rows[0:4, :], in_=b.rearrange("(n p) -> n p", p=P))
+        load_scale_rows(nc.gpsimd, wd8_sc, wd8_scales)
+        load_scale_rows(nc.gpsimd, wd4_sc, wd4_scales)
         for page in pages:
             nc.gpsimd.memset(page[:], 0.0)
 
-        picked = {}
-        for a, c in ((0, 0), (0, 1), (1, 0)):
-            picked[a, c] = keep.tile([P, PACK, HALF], F32, name=f"picked{a}{c}")
-        picked[1, 1] = last_picked
-
         nc.sync.dma_start(pick_list[:], offs)
         load_x(0, 0)
-        nc.sync.dma_start(out=wgt_half[0], in_=wgt[:, 0:HALF])
-        nc.sync.dma_start(out=wgt_half[1], in_=wgt[:, HALF:J])
+        nc.sync.dma_start(out=wgt_half[0][:], in_=wgt[:, 0:HALF])
+        nc.sync.dma_start(out=wgt_half[1][:], in_=wgt[:, HALF:J])
         load_x(0, 1)
         load_x(0, 2)
         load_wu(0, 0)
         load_x(0, 3)
+        load_scale_rows(nc.sync, wg_sc_raw, wg_scales)
         load_wu(1, 0)
-        load_x(1, 0)
-        load_x(1, 1)
-        load_x(1, 2)
-        load_x(1, 3)
-        for a in range(2):
-            load_scale_rows(wg_sc_raw, 4 * a, wg_scales[a])
-        nc.sync.dma_start(
-            out=wg_raw[:].rearrange("p (a r) -> p a r", a=2),
-            in_=wg_words.rearrange("a p r i -> p a (r i)").bitcast(I32),
-        )
+        for i in range(PACK):
+            load_x(1, i)
+        load_wg(0)
         load_wu(0, 1)
+        load_wg(1)
         load_wu(1, 1)
-        load_scale_rows(wd8_sc, 0, wd8_scales[0])
-        load_scale_rows(wd4_sc, 0, wd4_scales[0])
         nc.sync.dma_start(out=wd8_codes[:], in_=wd8_words[0].rearrange("p n i -> p (n i)").bitcast(I32))
         nc.sync.dma_start(out=wd4_codes[:].bitcast(I32), in_=wd4_words[0].bitcast(I32))
-        with nc.allow_non_contiguous_dma(reason="one bias value for each partition and output tile"):
-            nc.sync.dma_start(out=bias[:], in_=b.rearrange("(n p) -> p n", p=P))
         nc.sync.dma_start(place_list[:], offs2)
         nc.sync.dma_start(out=wgo_sb[:], in_=wgo)
 
-        def gather(a, i, c):
-            offsets = pick_list[:, c * LIST_COLS : (c + 1) * LIST_COLS]
-            nc.vector.tensor_tensor(picked[a, c][:, i, :], planes[a][i][:].indirect(offsets), wgt_half[c], MULT)
+        turned = psum_y.tile([P, HALF], F32, name="acc")
+        nc.tensor.transpose(turned[:, 0:P], bias_rows[:], identity[:])
+        nc.scalar.copy(out=bias[:], in_=turned[:, 0:4])
 
-        def round_x(a, c):
-            grouped = rounded[x_slot[a, c]]
-            nc.scalar.copy(
-                out=grouped[:].rearrange("p (g e i) -> p g i e", e=4, i=PACK),
-                in_=picked[a, c][:].rearrange("p i (g e) -> p g i e", e=4),
+        def gather(a, i, lo, hi):
+            c, first = divmod(lo, HALF)
+            cols = slice(first, first + hi - lo)
+            offsets = pick_list[:, lo // 16 : hi // 16]
+            nc.vector.tensor_tensor(
+                picked[a, c][:, i, cols], planes[a][i][:].indirect(offsets), wgt_half[c][:, cols], MULT
             )
-            return grouped
+
+        def round_x(a, lo, hi):
+            c, first = divmod(lo, HALF)
+            nc.scalar.copy(
+                out=x_rounded[a, c][:, PACK * first : PACK * (first + hi - lo)].rearrange(
+                    "p (g e i) -> p g i e", e=4, i=PACK
+                ),
+                in_=picked[a, c][:, :, first : first + hi - lo].rearrange("p i (g e) -> p g i e", e=4),
+            )
+
+        def quantise_tokens(codes, scales, grouped, lo, hi):
+            first = lo % HALF
+            nc.vector.quantize_mx(
+                out=codes[:, lo:hi].bitcast(FP8X4),
+                scales=scales[:, lo:hi],
+                in_=grouped[:, PACK * first : PACK * (first + hi - lo)],
+            )
+
+        def quantise_x(a, lo, hi):
+            quantise_tokens(x_codes[a], x_sc[a], x_rounded[a, lo // HALF], lo, hi)
+
+        def quantise_h(h, lo, hi):
+            quantise_tokens(h_codes[h], h_sc[h], h_rounded[h, lo // HALF], lo, hi)
 
         def round_wu(a, h):
-            grouped = rounded[wu_slot[a, h]]
             nc.scalar.copy(
-                out=grouped[:].rearrange("p (t q i) -> p q i t", t=PACK, i=PACK),
+                out=wu_rounded[a, h][:].rearrange("p (t q i) -> p q i t", t=PACK, i=PACK),
                 in_=wu_raw[a, h][:].rearrange("p i (q t) -> p q i t", t=PACK),
             )
-            return grouped
 
-        def deal_wg():
-            nc.vector.tensor_copy(
-                out=wg_codes[:].rearrange("p (g t q) -> p g q t", t=PACK, q=P),
-                in_=wg_raw[:].rearrange("p (g q t) -> p g q t", t=PACK, q=P),
+        def quantise_wu(a, h):
+            cols = slice(h * PASS, (h + 1) * PASS)
+            nc.vector.quantize_mx(
+                out=wu_codes[a][:, cols].bitcast(FP8X4), scales=wu_sc[a][:, cols], in_=wu_rounded[a, h][:]
             )
+
+        def deal_wg_words(h):
+            nc.vector.tensor_copy(
+                out=wg_codes[h][:].rearrange("p (a t q) -> p a q t", t=PACK, q=P),
+                in_=wg_raw[h][:].rearrange("p (a q t) -> p a q t", t=PACK, q=P),
+            )
+
+        def deal_wg_scales():
             nc.vector.tensor_copy(
                 out=wg_sc[:].rearrange("p (g t q) -> p g t q", t=PACK, q=P),
                 in_=wg_sc_raw[:].rearrange("p (g q t) -> p g t q", t=PACK, q=P),
             )
 
-        def hidden(c, h):
-            grouped = rounded[2 + 2 * c + h]
-            for u in range(HALF // UNIT):
-                cols = slice(u * UNIT, (u + 1) * UNIT)
-                gate = psum.tile([P, PACK, UNIT], F32, name="gate")
-                up = psum.tile([P, PACK, UNIT], F32, name="up")
-                for t in range(PACK):
-                    for a in range(2):
-                        lo = h * PASS + t * P
-                        nc.tensor.matmul_mx(
-                            out=gate[:, t, :],
-                            lhsT=wg_codes[:, a * R + lo : a * R + lo + P].bitcast(FP8X4),
-                            lhsT_scale=wg_sc[4 * a :, lo : lo + P],
-                            rhs=xq[a, c][0][:, cols].bitcast(FP8X4),
-                            rhs_scale=xq[a, c][1][:, cols],
-                            start=(a == 0),
-                            stop=(a == 1),
-                        )
-                for t in range(PACK):
-                    for a in range(2):
-                        nc.tensor.matmul_mx(
-                            out=up[:, t, :],
-                            lhsT=wuq[a, h][0][:, t * P : (t + 1) * P].bitcast(FP8X4),
-                            lhsT_scale=wuq[a, h][1][:, t * P : (t + 1) * P],
-                            rhs=xq[a, c][0][:, cols].bitcast(FP8X4),
-                            rhs_scale=xq[a, c][1][:, cols],
-                            start=(a == 0),
-                            stop=(a == 1),
-                        )
-                gated = wu_raw[h, 0][:, u, :].rearrange("p (j t) -> p j t", t=PACK)
-                nc.scalar.activation(out=gated, in_=gate[:].rearrange("p t j -> p j t"), func=ACT.Tanh)
-                nc.vector.tensor_tensor(
-                    grouped[:, u * PACK * UNIT : (u + 1) * PACK * UNIT].rearrange("p (j t) -> p j t", t=PACK),
-                    up[:].rearrange("p t j -> p j t"),
-                    gated,
-                    MULT,
-                )
-            return grouped
+        def gated(h, u):
+            return wu_raw[h, u // 4][:, u % 4, :].rearrange("p (j t) -> p j t", t=PACK)
 
-        for i in range(PACK):
-            for c in range(2):
-                gather(0, i, c)
-            if i == 2:
-                quantise(wuq[0, 0], round_wu(0, 0))
-        g00 = round_x(0, 0)
-        g01 = round_x(0, 1)
-        w10 = round_wu(1, 0)
-        gather(1, 0, 0)
-        gather(1, 0, 1)
-        quantise(xq[0, 0], g00)
-        gather(1, 1, 0)
-        gather(1, 1, 1)
-        quantise(xq[0, 1], g01)
-        gather(1, 2, 0)
-        quantise(wuq[1, 0], w10)
-        gather(1, 3, 0)
-        g10 = round_x(1, 0)
-        gather(1, 2, 1)
-        gather(1, 3, 1)
-        quantise(xq[1, 0], g10)
-        deal_wg()
-        w01 = round_wu(0, 1)
-        w11 = round_wu(1, 1)
-        g11 = round_x(1, 1)
+        def gate(h, u):
+            cols = slice(u * UNIT, (u + 1) * UNIT)
+            bank = psum.tile([P, PACK, UNIT], F32, name="gate")
+            for t in range(PACK):
+                for a in (1, 0):
+                    lo = h * PASS + t * P
+                    nc.tensor.matmul_mx(
+                        out=bank[:, t, :],
+                        lhsT=wg_codes[h][:, a * PASS + t * P : a * PASS + (t + 1) * P].bitcast(FP8X4),
+                        lhsT_scale=wg_sc[4 * a :, lo : lo + P],
+                        rhs=x_codes[a][:, cols].bitcast(FP8X4),
+                        rhs_scale=x_sc[a][:, cols],
+                        start=(a == 1),
+                        stop=(a == 0),
+                    )
+            nc.scalar.activation(out=gated(h, u), in_=bank[:].rearrange("p t j -> p j t"), func=ACT.Tanh)
 
-        hq_codes = keep.tile([P, 4 * HALF], I32, name="hq_codes", tag="wg_raw_hq", align_bytes=64)
-        hq_scales = keep.tile([P, 4 * HALF], U8, name="hq_scales", align_bytes=64)
+        def up(h, u):
+            cols = slice(u * UNIT, (u + 1) * UNIT)
+            bank = psum.tile([P, PACK, UNIT], F32, name="up")
+            for t in range(PACK):
+                for a in (1, 0):
+                    lo = h * PASS + t * P
+                    nc.tensor.matmul_mx(
+                        out=bank[:, t, :],
+                        lhsT=wu_codes[a][:, lo : lo + P].bitcast(FP8X4),
+                        lhsT_scale=wu_sc[a][:, lo : lo + P],
+                        rhs=x_codes[a][:, cols].bitcast(FP8X4),
+                        rhs_scale=x_sc[a][:, cols],
+                        start=(a == 1),
+                        stop=(a == 0),
+                    )
+            first = (u % 4) * PACK * UNIT
+            nc.vector.tensor_tensor(
+                h_rounded[h, u // 4][:, first : first + PACK * UNIT].rearrange("p (j t) -> p j t", t=PACK),
+                bank[:].rearrange("p t j -> p j t"),
+                gated(h, u),
+                MULT,
+            )
 
-        def hq(c, h):
-            lo = (2 * c + h) * HALF
-            return hq_codes[:, lo : lo + HALF], hq_scales[:, lo : lo + HALF]
+        def unit(h, u):
+            gate(h, u)
+            up(h, u)
 
-        def quantise_h(c, h, grouped):
-            codes, scales = hq(c, h)
-            nc.vector.quantize_mx(out=codes.bitcast(FP8X4), scales=scales, in_=grouped[:])
-
-        def output(c, n):
+        def output(chunk, n):
+            lo, hi = CHUNKS[chunk]
+            width = hi - lo
+            step = HALF if width == HALF else UNIT
             acc = psum_y.tile([P, HALF], F32, name="acc")
             cols = slice(n * P, (n + 1) * P)
-            nc.tensor.matmul_mx(
-                out=acc[:], lhsT=wd8_codes[:, cols].bitcast(FP8X4), lhsT_scale=wd8_sc[:, cols],
-                rhs=hq(c, 0)[0].bitcast(FP8X4), rhs_scale=hq(c, 0)[1], start=True, stop=False,
-            )
-            nc.tensor.matmul_mx(
-                out=acc[:], lhsT=wd4_codes[:, 2 * n * P : 2 * (n + 1) * P].bitcast(FP4X4), lhsT_scale=wd4_sc[:, cols],
-                rhs=hq(c, 1)[0].bitcast(FP8X4), rhs_scale=hq(c, 1)[1], start=False, stop=True,
-            )
-            y = picked[0, c][:, n, :]
-            nc.scalar.activation(out=y, in_=acc[:], func=ACT.Identity, bias=bias[:, n : n + 1])
-            offsets = place_list[:, c * LIST_COLS : (c + 1) * LIST_COLS]
-            nc.vector.tensor_tensor(pages[n][:].indirect(offsets), y, wgo_sb[:, c * HALF : (c + 1) * HALF], MULT)
+            for first in range(0, width, step):
+                tokens = slice(lo + first, lo + first + step)
+                nc.tensor.matmul_mx(
+                    out=acc[:, first : first + step],
+                    lhsT=wd8_codes[:, cols].bitcast(FP8X4),
+                    lhsT_scale=wd8_sc[:, cols],
+                    rhs=h_codes[0][:, tokens].bitcast(FP8X4),
+                    rhs_scale=h_sc[0][:, tokens],
+                    start=True,
+                    stop=False,
+                )
+                nc.tensor.matmul_mx(
+                    out=acc[:, first : first + step],
+                    lhsT=wd4_codes[:, 2 * n * P : 2 * (n + 1) * P].bitcast(FP4X4),
+                    lhsT_scale=wd4_sc[:, cols],
+                    rhs=h_codes[1][:, tokens].bitcast(FP8X4),
+                    rhs_scale=h_sc[1][:, tokens],
+                    start=False,
+                    stop=True,
+                )
+            c, first = divmod(lo, HALF)
+            y = picked[0, c][:, n, first : first + width]
+            nc.scalar.activation(out=y, in_=acc[:, 0:width], func=ACT.Identity, bias=bias[:, n : n + 1])
+            offsets = place_list[:, lo // 16 : hi // 16]
+            nc.vector.tensor_tensor(pages[n][:].indirect(offsets), y, wgo_sb[:, lo:hi], MULT)
 
-        h00 = hidden(0, 0)
-        quantise(wuq[0, 1], w01)
-        quantise(wuq[1, 1], w11)
-        quantise(xq[1, 1], g11)
-        quantise_h(0, 0, h00)
-        h01 = hidden(0, 1)
-        quantise_h(0, 1, h01)
-        h10 = hidden(1, 0)
+        for i in range(PACK):
+            gather(0, i, 0, HALF)
+            gather(0, i, HALF, J)
+        round_wu(0, 0)
+        quantise_wu(0, 0)
+        round_x(0, 0, HALF)
+        round_x(0, HALF, J)
+        round_wu(1, 0)
+        for i in range(2):
+            gather(1, i, 0, HALF)
+            gather(1, i, HALF, J)
+            quantise_x(0, i * HALF, (i + 1) * HALF)
+        deal_wg_scales()
+        gather(1, 2, 0, HALF)
+        quantise_wu(1, 0)
+        for lo, hi in CHUNKS[:2]:
+            gather(1, 3, lo, hi)
+            round_x(1, lo, hi)
+        deal_wg_words(0)
+        for lo, hi in CHUNKS[:2]:
+            quantise_x(1, lo, hi)
+        gather(1, 2, HALF, J)
+        gather(1, 3, HALF, J)
+        round_wu(0, 1)
+        quantise_wu(0, 1)
+        deal_wg_words(1)
+        round_wu(1, 1)
+        quantise_wu(1, 1)
+
+        unit(0, 0)
+        unit(0, 1)
+        quantise_h(0, *CHUNKS[0])
+        unit(0, 2)
+        gate(1, 0)
+        gate(1, 1)
+        unit(0, 3)
+        quantise_h(0, *CHUNKS[1])
+        up(1, 0)
+        up(1, 1)
+        quantise_h(1, *CHUNKS[0])
+        round_x(1, HALF, J)
+        unit(1, 2)
         output(0, 0)
-        quantise_h(1, 0, h10)
         output(0, 1)
-        h11 = hidden(1, 1)
+        unit(1, 3)
+        quantise_h(1, *CHUNKS[1])
+        quantise_x(1, HALF, J)
         output(0, 2)
-        quantise_h(1, 1, h11)
         output(0, 3)
         for n in range(4):
+            h, u = n // 2, 4 + 2 * (n % 2)
+            unit(h, u)
+            unit(h, u + 1)
+            if n % 2 == 1:
+                quantise_h(h, *CHUNKS[2])
             output(1, n)
+        for n in range(4):
+            output(2, n)
             nc.sync.dma_start(out=out[n * P : (n + 1) * P, :], in_=pages[n][:])

@@ -179,7 +179,8 @@ def tile_list_tanh_mix_scatb_kernel(
             )
 
         def gated(h, u):
-            return wu_raw[h, u // 4][:, u % 4, :].rearrange("p (j t) -> p j t", t=PACK)
+            slot = wu_raw[1, 1][:, 2 * h + u % 2, :] if u < 4 else wu_raw[h, 0][:, u % 4, :]
+            return slot.rearrange("p (j t) -> p j t", t=PACK)
 
         def gate(h, u):
             cols = slice(u * UNIT, (u + 1) * UNIT)
@@ -214,12 +215,20 @@ def tile_list_tanh_mix_scatb_kernel(
                         stop=(a == 0),
                     )
             first = (u % 4) * PACK * UNIT
-            nc.vector.tensor_tensor(
-                h_rounded[h, u // 4][:, first : first + PACK * UNIT].rearrange("p (j t) -> p j t", t=PACK),
-                bank[:].rearrange("p t j -> p j t"),
-                gated(h, u),
-                MULT,
-            )
+            product = h_rounded[h, u // 4][:, first : first + PACK * UNIT]
+            if 4 <= 4 * h + u < 11 and u >= 4:
+                moved = wu_raw[h, 1][:, u % 4, :]
+                nc.scalar.copy(
+                    out=moved.rearrange("p (j t) -> p j t", t=PACK), in_=bank[:].rearrange("p t j -> p j t")
+                )
+                nc.gpsimd.tensor_tensor(product, moved, wu_raw[h, 0][:, u % 4, :], MULT)
+            else:
+                nc.vector.tensor_tensor(
+                    product.rearrange("p (j t) -> p j t", t=PACK),
+                    bank[:].rearrange("p t j -> p j t"),
+                    gated(h, u),
+                    MULT,
+                )
 
         def unit(h, u):
             gate(h, u)
@@ -253,9 +262,16 @@ def tile_list_tanh_mix_scatb_kernel(
                 )
             c, first = divmod(lo, HALF)
             y = picked[0, c][:, n, first : first + width]
+            if chunk == 0 and n == 0:
+                y = x_rounded[1, 1][:].bitcast(F32)[:, 0:width]
             nc.scalar.activation(out=y, in_=acc[:, 0:width], func=ACT.Identity, bias=bias[:, n : n + 1])
             offsets = place_list[:, lo // 16 : hi // 16]
-            nc.vector.tensor_tensor(pages[n][:].indirect(offsets), y, wgo_sb[:, lo:hi], MULT)
+            if chunk < 2:
+                weighted = picked[1, 0][:, n, lo:hi]
+                nc.gpsimd.tensor_tensor(weighted, y, wgo_sb[:, lo:hi], MULT)
+                nc.vector.tensor_copy(pages[n][:].indirect(offsets), weighted)
+            else:
+                nc.vector.tensor_tensor(pages[n][:].indirect(offsets), y, wgo_sb[:, lo:hi], MULT)
 
         for i in range(PACK):
             gather(0, i, 0, HALF)
@@ -289,22 +305,20 @@ def tile_list_tanh_mix_scatb_kernel(
         unit(0, 0)
         unit(0, 1)
         quantise_h(0, *CHUNKS[0])
+        unit(1, 0)
+        unit(1, 1)
+        quantise_h(1, *CHUNKS[0])
         unit(0, 2)
-        gate(1, 0)
-        gate(1, 1)
+        output(0, 0)
+        round_x(1, HALF, J)
         unit(0, 3)
         quantise_h(0, *CHUNKS[1])
-        up(1, 0)
-        up(1, 1)
-        quantise_h(1, *CHUNKS[0])
-        round_x(1, HALF, J)
-        unit(1, 2)
-        output(0, 0)
         output(0, 1)
+        unit(1, 2)
+        output(0, 2)
+        quantise_x(1, HALF, J)
         unit(1, 3)
         quantise_h(1, *CHUNKS[1])
-        quantise_x(1, HALF, J)
-        output(0, 2)
         output(0, 3)
         for n in range(4):
             h, u = n // 2, 4 + 2 * (n % 2)

@@ -1,7 +1,6 @@
 from contextlib import ExitStack
 
 import concourse.mybir as mybir
-from concourse.masks import make_identity
 
 K, R, N, T, J = 1024, 1024, 512, 2048, 1024
 FLOPS = 2 * J * (2 * K * R + R * N)
@@ -14,6 +13,7 @@ U8 = mybir.dt.uint8
 FP8X4 = mybir.dt.float8_e4m3fn_x4
 FP4X4 = mybir.dt.float4_e2m1fn_x4
 MULT = mybir.AluOpType.mult
+ADD = mybir.AluOpType.add
 ACT = mybir.ActivationFunctionType
 
 P = 128
@@ -21,7 +21,8 @@ PACK = 4
 PASS = P * PACK
 HALF = 512
 UNIT = 128
-CHUNKS = ((0, 256), (256, 512), (512, 1024))
+CHUNK = 256
+CHUNKS = ((0, 256), (256, 512), (512, 768), (768, 1024))
 
 
 def tile_list_tanh_mix_scatb_kernel(
@@ -41,8 +42,6 @@ def tile_list_tanh_mix_scatb_kernel(
         wu_raw = {(a, h): keep.tile([P, PACK, HALF], F32, name=f"wu_raw{a}{h}") for a in range(2) for h in range(2)}
         wgt_half = [keep.tile([P, HALF], F32, name=f"wgt{c}") for c in range(2)]
         wgo_sb = keep.tile([P, J], F32, name="wgo_sb")
-        bias_rows = keep.tile([P, P], F32, name="bias_rows")
-        identity = keep.tile([P, P], F32, name="identity")
         bias = keep.tile([P, 4], F32, name="bias")
         warm = keep.tile([P, 8], F32, name="warm")
         wg_raw = [keep.tile([P, 2 * PASS], I32, name=f"wg_raw{h}", align_bytes=64) for h in range(2)]
@@ -63,7 +62,9 @@ def tile_list_tanh_mix_scatb_kernel(
         late_planes = picked[1, 1][:, 2:4, :].rearrange("p i j -> p (i j)").bitcast(BF16)
         x_rounded = {(0, 0): rounded[0], (0, 1): rounded[1], (1, 0): late_planes, (1, 1): rounded[0]}
         wu_rounded = {(0, 0): rounded[2], (1, 0): rounded[3], (0, 1): rounded[4], (1, 1): rounded[0]}
-        h_rounded = {(0, 0): rounded[2], (1, 0): rounded[3], (0, 1): rounded[1], (1, 1): rounded[4]}
+        h_rounded = [rounded[2], rounded[3], rounded[1], rounded[4]]
+        gated_tile = [wu_raw[1, 1], wu_raw[0, 0], wu_raw[1, 0], wu_raw[0, 0]]
+        moved_tile = [None, wu_raw[0, 1], wu_raw[1, 1], wu_raw[0, 1]]
 
         x_rows = xT.rearrange("(a p i) t -> a i p t", a=2, i=PACK)
 
@@ -90,9 +91,6 @@ def tile_list_tanh_mix_scatb_kernel(
         nc.scalar.activation(out=warm[:, 4:8], in_=warm[:, 0:4], func=ACT.Tanh)
         for tile in (wg_sc_raw, wd8_sc, wd4_sc):
             nc.vector.memset(tile[:].bitcast(I32), 0)
-        nc.vector.memset(bias_rows[:], 0.0)
-        make_identity(nc, identity[:])
-        nc.gpsimd.dma_start(out=bias_rows[0:4, :], in_=b.rearrange("(n p) -> n p", p=P))
         load_scale_rows(nc.gpsimd, wd8_sc, wd8_scales)
         load_scale_rows(nc.gpsimd, wd4_sc, wd4_scales)
         for page in pages:
@@ -104,24 +102,24 @@ def tile_list_tanh_mix_scatb_kernel(
         nc.sync.dma_start(out=wgt_half[1][:], in_=wgt[:, HALF:J])
         load_x(0, 1)
         load_x(0, 2)
-        load_wu(0, 0)
         load_x(0, 3)
+        load_wu(0, 0)
+        load_x(1, 0)
+        load_x(1, 1)
         load_scale_rows(nc.sync, wg_sc_raw, wg_scales)
         load_wu(1, 0)
-        for i in range(PACK):
-            load_x(1, i)
+        load_x(1, 2)
+        load_x(1, 3)
         load_wg(0)
         load_wu(0, 1)
-        load_wg(1)
         load_wu(1, 1)
+        load_wg(1)
         nc.sync.dma_start(out=wd8_codes[:], in_=wd8_words[0].rearrange("p n i -> p (n i)").bitcast(I32))
         nc.sync.dma_start(out=wd4_codes[:].bitcast(I32), in_=wd4_words[0].bitcast(I32))
         nc.sync.dma_start(place_list[:], offs2)
         nc.sync.dma_start(out=wgo_sb[:], in_=wgo)
-
-        turned = psum_y.tile([P, HALF], F32, name="acc")
-        nc.tensor.transpose(turned[:, 0:P], bias_rows[:], identity[:])
-        nc.scalar.copy(out=bias[:], in_=turned[:, 0:4])
+        with nc.allow_non_contiguous_dma(reason="one bias value for each partition and output tile"):
+            nc.sync.dma_start(out=bias[:], in_=b.rearrange("(n p) -> p n", p=P))
 
         def gather(a, i, lo, hi):
             c, first = divmod(lo, HALF)
@@ -151,8 +149,13 @@ def tile_list_tanh_mix_scatb_kernel(
         def quantise_x(a, lo, hi):
             quantise_tokens(x_codes[a], x_sc[a], x_rounded[a, lo // HALF], lo, hi)
 
-        def quantise_h(h, lo, hi):
-            quantise_tokens(h_codes[h], h_sc[h], h_rounded[h, lo // HALF], lo, hi)
+        def quantise_h(h, chunk):
+            lo, hi = CHUNKS[chunk]
+            nc.vector.quantize_mx(
+                out=h_codes[h][:, lo:hi].bitcast(FP8X4),
+                scales=h_sc[h][:, lo:hi],
+                in_=h_rounded[chunk][:, h * PACK * CHUNK : (h + 1) * PACK * CHUNK],
+            )
 
         def round_wu(a, h):
             nc.scalar.copy(
@@ -179,8 +182,7 @@ def tile_list_tanh_mix_scatb_kernel(
             )
 
         def gated(h, u):
-            slot = wu_raw[1, 1][:, 2 * h + u % 2, :] if u < 4 else wu_raw[h, 0][:, u % 4, :]
-            return slot.rearrange("p (j t) -> p j t", t=PACK)
+            return gated_tile[u // 2][:, 2 * h + u % 2, :]
 
         def gate(h, u):
             cols = slice(u * UNIT, (u + 1) * UNIT)
@@ -197,7 +199,7 @@ def tile_list_tanh_mix_scatb_kernel(
                         start=(a == 1),
                         stop=(a == 0),
                     )
-            nc.scalar.activation(out=gated(h, u), in_=bank[:].rearrange("p t j -> p j t"), func=ACT.Tanh)
+            nc.scalar.activation(out=gated(h, u).rearrange("p (j t) -> p j t", t=PACK), in_=bank[:].rearrange("p t j -> p j t"), func=ACT.Tanh)
 
         def up(h, u):
             cols = slice(u * UNIT, (u + 1) * UNIT)
@@ -214,19 +216,19 @@ def tile_list_tanh_mix_scatb_kernel(
                         start=(a == 1),
                         stop=(a == 0),
                     )
-            first = (u % 4) * PACK * UNIT
-            product = h_rounded[h, u // 4][:, first : first + PACK * UNIT]
-            if 4 <= 4 * h + u < 11 and u >= 4:
-                moved = wu_raw[h, 1][:, u % 4, :]
+            slot = 2 * h + u % 2
+            product = h_rounded[u // 2][:, slot * PACK * UNIT : (slot + 1) * PACK * UNIT]
+            if u >= 2 and slot < 3:
+                moved = moved_tile[u // 2][:, slot, :]
                 nc.scalar.copy(
                     out=moved.rearrange("p (j t) -> p j t", t=PACK), in_=bank[:].rearrange("p t j -> p j t")
                 )
-                nc.gpsimd.tensor_tensor(product, moved, wu_raw[h, 0][:, u % 4, :], MULT)
+                nc.gpsimd.tensor_tensor(product, moved, gated(h, u), MULT)
             else:
                 nc.vector.tensor_tensor(
                     product.rearrange("p (j t) -> p j t", t=PACK),
                     bank[:].rearrange("p t j -> p j t"),
-                    gated(h, u),
+                    gated(h, u).rearrange("p (j t) -> p j t", t=PACK),
                     MULT,
                 )
 
@@ -237,7 +239,7 @@ def tile_list_tanh_mix_scatb_kernel(
         def output(chunk, n):
             lo, hi = CHUNKS[chunk]
             width = hi - lo
-            step = HALF if width == HALF else UNIT
+            step = UNIT
             acc = psum_y.tile([P, HALF], F32, name="acc")
             cols = slice(n * P, (n + 1) * P)
             for first in range(0, width, step):
@@ -262,12 +264,20 @@ def tile_list_tanh_mix_scatb_kernel(
                 )
             c, first = divmod(lo, HALF)
             y = picked[0, c][:, n, first : first + width]
-            if chunk == 0 and n == 0:
+            if (chunk, n) == (0, 1):
                 y = x_rounded[1, 1][:].bitcast(F32)[:, 0:width]
-            nc.scalar.activation(out=y, in_=acc[:, 0:width], func=ACT.Identity, bias=bias[:, n : n + 1])
+            if (chunk, n) == (2, 3):
+                y = picked[0, 1][:, 1, CHUNK:HALF]
             offsets = place_list[:, lo // 16 : hi // 16]
-            if chunk < 2:
-                weighted = picked[1, 0][:, n, lo:hi]
+            weighted = picked[1, 0][:, n, first : first + width]
+            if chunk < 3 and n == 0:
+                nc.vector.scalar_tensor_tensor(
+                    weighted, acc[:, 0:width], bias[:, n : n + 1], wgo_sb[:, lo:hi], ADD, MULT
+                )
+                nc.vector.tensor_copy(pages[n][:].indirect(offsets), weighted)
+                return
+            nc.scalar.activation(out=y, in_=acc[:, 0:width], func=ACT.Identity, bias=bias[:, n : n + 1])
+            if 4 * chunk + n < 11:
                 nc.gpsimd.tensor_tensor(weighted, y, wgo_sb[:, lo:hi], MULT)
                 nc.vector.tensor_copy(pages[n][:].indirect(offsets), weighted)
             else:
@@ -285,8 +295,8 @@ def tile_list_tanh_mix_scatb_kernel(
             gather(1, i, 0, HALF)
             gather(1, i, HALF, J)
             quantise_x(0, i * HALF, (i + 1) * HALF)
-        deal_wg_scales()
         gather(1, 2, 0, HALF)
+        deal_wg_scales()
         quantise_wu(1, 0)
         for lo, hi in CHUNKS[:2]:
             gather(1, 3, lo, hi)
@@ -298,35 +308,35 @@ def tile_list_tanh_mix_scatb_kernel(
         gather(1, 3, HALF, J)
         round_wu(0, 1)
         quantise_wu(0, 1)
-        deal_wg_words(1)
         round_wu(1, 1)
+        deal_wg_words(1)
         quantise_wu(1, 1)
 
-        unit(0, 0)
-        unit(0, 1)
-        quantise_h(0, *CHUNKS[0])
-        unit(1, 0)
-        unit(1, 1)
-        quantise_h(1, *CHUNKS[0])
-        unit(0, 2)
-        output(0, 0)
-        round_x(1, HALF, J)
-        unit(0, 3)
-        quantise_h(0, *CHUNKS[1])
-        output(0, 1)
-        unit(1, 2)
-        output(0, 2)
-        quantise_x(1, HALF, J)
-        unit(1, 3)
-        quantise_h(1, *CHUNKS[1])
-        output(0, 3)
-        for n in range(4):
-            h, u = n // 2, 4 + 2 * (n % 2)
-            unit(h, u)
-            unit(h, u + 1)
-            if n % 2 == 1:
-                quantise_h(h, *CHUNKS[2])
-            output(1, n)
-        for n in range(4):
-            output(2, n)
+        def half_hidden(h, chunk):
+            unit(h, 2 * chunk)
+            unit(h, 2 * chunk + 1)
+            quantise_h(h, chunk)
+
+        def store(n):
             nc.sync.dma_start(out=out[n * P : (n + 1) * P, :], in_=pages[n][:])
+
+        half_hidden(0, 0)
+        half_hidden(1, 0)
+        for chunk in range(3):
+            output(chunk, 0)
+            output(chunk, 1)
+            if chunk == 0:
+                round_x(1, HALF, J)
+            half_hidden(0, chunk + 1)
+            if chunk < 2:
+                output(chunk, 2)
+            if chunk == 0:
+                quantise_x(1, HALF, J)
+            half_hidden(1, chunk + 1)
+            output(chunk, 3 if chunk < 2 else 2)
+        for n in range(3):
+            output(3, n)
+            store(n)
+        output(2, 3)
+        output(3, 3)
+        store(3)

@@ -19,10 +19,12 @@ ACT = mybir.ActivationFunctionType
 P = 128
 PACK = 4
 PASS = P * PACK
-HALF = 512
-UNIT = 128
+GROUP = 16
+HALF = J // 2
 CHUNK = 256
-CHUNKS = ((0, 256), (256, 512), (512, 768), (768, 1024))
+UNIT = 128
+CHUNKS = J // CHUNK
+PAGES = N // P
 
 
 def tile_list_tanh_mix_scatb_kernel(
@@ -34,18 +36,18 @@ def tile_list_tanh_mix_scatb_kernel(
         psum = ctx.enter_context(tc.psum_pool(name="psum", bufs=3))
         psum_y = ctx.enter_context(tc.psum_pool(name="psum_y", bufs=2))
 
-        pick_list = keep.tile([P, J // 16], U16, name="pick_list")
-        place_list = keep.tile([P, J // 16], U16, name="place_list")
+        pick_list = keep.tile([P, J // GROUP], U16, name="pick_list")
+        place_list = keep.tile([P, J // GROUP], U16, name="place_list")
         planes = [[keep.tile([P, T], F32, name=f"x{a}{i}") for i in range(PACK)] for a in range(2)]
-        pages = [keep.tile([P, T], F32, name=f"page{n}") for n in range(4)]
+        pages = [keep.tile([P, T], F32, name=f"page{n}") for n in range(PAGES)]
         picked = {(a, c): keep.tile([P, PACK, HALF], F32, name=f"picked{a}{c}") for a in range(2) for c in range(2)}
-        wu_raw = {(a, h): keep.tile([P, PACK, HALF], F32, name=f"wu_raw{a}{h}") for a in range(2) for h in range(2)}
+        wu_raw = {(a, s): keep.tile([P, PACK, PASS], F32, name=f"wu_raw{a}{s}") for a in range(2) for s in range(2)}
         wgt_half = [keep.tile([P, HALF], F32, name=f"wgt{c}") for c in range(2)]
         wgo_sb = keep.tile([P, J], F32, name="wgo_sb")
-        bias = keep.tile([P, 4], F32, name="bias")
-        warm = keep.tile([P, 8], F32, name="warm")
-        wg_raw = [keep.tile([P, 2 * PASS], I32, name=f"wg_raw{h}", align_bytes=64) for h in range(2)]
-        wg_codes = [keep.tile([P, 2 * PASS], I32, name=f"wg_codes{h}", align_bytes=64) for h in range(2)]
+        bias = keep.tile([P, PAGES], F32, name="bias")
+        zeros = keep.tile([P, 8], F32, name="zeros")
+        wg_raw = [keep.tile([P, 2 * PASS], I32, name=f"wg_raw{s}", align_bytes=64) for s in range(2)]
+        wg_codes = [keep.tile([P, 2 * PASS], I32, name=f"wg_codes{s}", align_bytes=64) for s in range(2)]
         wg_sc_raw = keep.tile([P, R], U8, name="wg_sc_raw", align_bytes=64)
         wg_sc = keep.tile([P, R], U8, name="wg_sc", align_bytes=64)
         wd8_codes = keep.tile([P, N], I32, name="wd8_codes", align_bytes=64)
@@ -56,28 +58,31 @@ def tile_list_tanh_mix_scatb_kernel(
         x_sc = [keep.tile([P, J], U8, name=f"x_sc{a}", align_bytes=64) for a in range(2)]
         wu_codes = [keep.tile([P, R], I32, name=f"wu_codes{a}", align_bytes=64) for a in range(2)]
         wu_sc = [keep.tile([P, R], U8, name=f"wu_sc{a}", align_bytes=64) for a in range(2)]
-        h_codes = wg_raw
-        h_sc = [keep.tile([P, J], U8, name=f"h_sc{h}", align_bytes=64) for h in range(2)]
-        rounded = [keep.tile([P, PACK * HALF], BF16, name=f"rounded{s}", align_bytes=64) for s in range(5)]
+        h_sc_tiles = [keep.tile([P, J], U8, name=f"h_sc{c}", align_bytes=64) for c in range(2)]
+        rounded = [keep.tile([P, PACK * HALF], BF16, name=f"rounded{v}", align_bytes=64) for v in range(5)]
+
         late_planes = picked[1, 1][:, 2:4, :].rearrange("p i j -> p (i j)").bitcast(BF16)
         x_rounded = {(0, 0): rounded[0], (0, 1): rounded[1], (1, 0): late_planes, (1, 1): rounded[0]}
         wu_rounded = {(0, 0): rounded[2], (1, 0): rounded[3], (0, 1): rounded[4], (1, 1): rounded[0]}
         h_rounded = [rounded[2], rounded[3], rounded[1], rounded[4]]
         gated_tile = [wu_raw[1, 1], wu_raw[0, 0], wu_raw[1, 0], wu_raw[0, 0]]
-        moved_tile = [None, wu_raw[0, 1], wu_raw[1, 1], wu_raw[0, 1]]
+        moved_tile = {1: wu_raw[0, 1], 2: wu_raw[1, 1], 3: wu_raw[0, 1]}
+        h_cols = [slice(chunk % 2 * 2 * CHUNK, (chunk % 2 + 1) * 2 * CHUNK) for chunk in range(CHUNKS)]
+        h_codes = [wg_raw[chunk // 2][:, h_cols[chunk]] for chunk in range(CHUNKS)]
+        h_sc = [h_sc_tiles[chunk // 2][:, h_cols[chunk]] for chunk in range(CHUNKS)]
 
         x_rows = xT.rearrange("(a p i) t -> a i p t", a=2, i=PACK)
 
         def load_x(a, i):
             nc.sync.dma_start(out=planes[a][i][:], in_=x_rows[a, i])
 
-        def load_wu(a, h):
-            rows = wu[a * PASS : (a + 1) * PASS, h * PASS : (h + 1) * PASS]
-            nc.sync.dma_start(out=wu_raw[a, h][:], in_=rows.rearrange("(p i) r -> p i r", i=PACK))
+        def load_wu(a, s):
+            rows = wu[a * PASS : (a + 1) * PASS, s * PASS : (s + 1) * PASS]
+            nc.sync.dma_start(out=wu_raw[a, s][:], in_=rows.rearrange("(p i) r -> p i r", i=PACK))
 
-        def load_wg(h):
-            words = wg_words[:, :, h * PASS : (h + 1) * PASS, :].rearrange("a p r i -> p a (r i)")
-            nc.sync.dma_start(out=wg_raw[h][:].rearrange("p (a r) -> p a r", a=2), in_=words.bitcast(I32))
+        def load_wg(s):
+            words = wg_words[:, :, s * PASS : (s + 1) * PASS, :].rearrange("a p r i -> p a (r i)")
+            nc.sync.dma_start(out=wg_raw[s][:].rearrange("p (a r) -> p a r", a=2), in_=words.bitcast(I32))
 
         def load_scale_rows(queue, tile, rows):
             passes = rows.shape[0]
@@ -87,8 +92,9 @@ def tile_list_tanh_mix_scatb_kernel(
                     in_=rows[:, 4 * q : 4 * q + 4, :].bitcast(I32),
                 )
 
-        nc.vector.memset(warm[:], 0.0)
-        nc.scalar.activation(out=warm[:, 4:8], in_=warm[:, 0:4], func=ACT.Tanh)
+        nc.vector.memset(zeros[:], 0.0)
+        nc.scalar.activation(out=zeros[:, 4:8], in_=zeros[:, 0:4], func=ACT.Tanh)
+        no_bias = zeros[:, 4:5]
         for tile in (wg_sc_raw, wd8_sc, wd4_sc):
             nc.vector.memset(tile[:].bitcast(I32), 0)
         load_scale_rows(nc.gpsimd, wd8_sc, wd8_scales)
@@ -118,13 +124,13 @@ def tile_list_tanh_mix_scatb_kernel(
         nc.sync.dma_start(out=wd4_codes[:].bitcast(I32), in_=wd4_words[0].bitcast(I32))
         nc.sync.dma_start(place_list[:], offs2)
         nc.sync.dma_start(out=wgo_sb[:], in_=wgo)
-        with nc.allow_non_contiguous_dma(reason="one bias value for each partition and output tile"):
+        with nc.allow_non_contiguous_dma(reason="one bias value for each partition and page"):
             nc.sync.dma_start(out=bias[:], in_=b.rearrange("(n p) -> p n", p=P))
 
         def gather(a, i, lo, hi):
             c, first = divmod(lo, HALF)
             cols = slice(first, first + hi - lo)
-            offsets = pick_list[:, lo // 16 : hi // 16]
+            offsets = pick_list[:, lo // GROUP : hi // GROUP]
             nc.vector.tensor_tensor(
                 picked[a, c][:, i, cols], planes[a][i][:].indirect(offsets), wgt_half[c][:, cols], MULT
             )
@@ -138,150 +144,144 @@ def tile_list_tanh_mix_scatb_kernel(
                 in_=picked[a, c][:, :, first : first + hi - lo].rearrange("p i (g e) -> p g i e", e=4),
             )
 
-        def quantise_tokens(codes, scales, grouped, lo, hi):
-            first = lo % HALF
-            nc.vector.quantize_mx(
-                out=codes[:, lo:hi].bitcast(FP8X4),
-                scales=scales[:, lo:hi],
-                in_=grouped[:, PACK * first : PACK * (first + hi - lo)],
-            )
-
         def quantise_x(a, lo, hi):
-            quantise_tokens(x_codes[a], x_sc[a], x_rounded[a, lo // HALF], lo, hi)
-
-        def quantise_h(h, chunk):
-            lo, hi = CHUNKS[chunk]
+            c, first = divmod(lo, HALF)
             nc.vector.quantize_mx(
-                out=h_codes[h][:, lo:hi].bitcast(FP8X4),
-                scales=h_sc[h][:, lo:hi],
-                in_=h_rounded[chunk][:, h * PACK * CHUNK : (h + 1) * PACK * CHUNK],
+                out=x_codes[a][:, lo:hi].bitcast(FP8X4),
+                scales=x_sc[a][:, lo:hi],
+                in_=x_rounded[a, c][:, PACK * first : PACK * (first + hi - lo)],
             )
 
-        def round_wu(a, h):
+        def round_wu(a, s):
             nc.scalar.copy(
-                out=wu_rounded[a, h][:].rearrange("p (t q i) -> p q i t", t=PACK, i=PACK),
-                in_=wu_raw[a, h][:].rearrange("p i (q t) -> p q i t", t=PACK),
+                out=wu_rounded[a, s][:].rearrange("p (t q i) -> p q i t", t=PACK, i=PACK),
+                in_=wu_raw[a, s][:].rearrange("p i (q t) -> p q i t", t=PACK),
             )
 
-        def quantise_wu(a, h):
-            cols = slice(h * PASS, (h + 1) * PASS)
+        def quantise_wu(a, s):
+            cols = slice(s * PASS, (s + 1) * PASS)
             nc.vector.quantize_mx(
-                out=wu_codes[a][:, cols].bitcast(FP8X4), scales=wu_sc[a][:, cols], in_=wu_rounded[a, h][:]
+                out=wu_codes[a][:, cols].bitcast(FP8X4), scales=wu_sc[a][:, cols], in_=wu_rounded[a, s][:]
             )
 
-        def deal_wg_words(h):
+        def deal_wg_words(s):
             nc.vector.tensor_copy(
-                out=wg_codes[h][:].rearrange("p (a t q) -> p a q t", t=PACK, q=P),
-                in_=wg_raw[h][:].rearrange("p (a q t) -> p a q t", t=PACK, q=P),
+                out=wg_codes[s][:].rearrange("p (a t q) -> p a q t", t=PACK, q=P),
+                in_=wg_raw[s][:].rearrange("p (a q t) -> p a q t", t=PACK, q=P),
             )
 
         def deal_wg_scales():
             nc.vector.tensor_copy(
-                out=wg_sc[:].rearrange("p (g t q) -> p g t q", t=PACK, q=P),
-                in_=wg_sc_raw[:].rearrange("p (g q t) -> p g t q", t=PACK, q=P),
+                out=wg_sc[:].rearrange("p (s t q) -> p s t q", t=PACK, q=P),
+                in_=wg_sc_raw[:].rearrange("p (s q t) -> p s t q", t=PACK, q=P),
             )
 
-        def gated(h, u):
-            return gated_tile[u // 2][:, 2 * h + u % 2, :]
-
-        def gate(h, u):
+        def first_products(bank, u, stationary):
             cols = slice(u * UNIT, (u + 1) * UNIT)
-            bank = psum.tile([P, PACK, UNIT], F32, name="gate")
             for t in range(PACK):
                 for a in (1, 0):
-                    lo = h * PASS + t * P
+                    codes, scales = stationary(a, t)
                     nc.tensor.matmul_mx(
                         out=bank[:, t, :],
-                        lhsT=wg_codes[h][:, a * PASS + t * P : a * PASS + (t + 1) * P].bitcast(FP8X4),
-                        lhsT_scale=wg_sc[4 * a :, lo : lo + P],
+                        lhsT=codes.bitcast(FP8X4),
+                        lhsT_scale=scales,
                         rhs=x_codes[a][:, cols].bitcast(FP8X4),
                         rhs_scale=x_sc[a][:, cols],
                         start=(a == 1),
                         stop=(a == 0),
                     )
-            nc.scalar.activation(out=gated(h, u).rearrange("p (j t) -> p j t", t=PACK), in_=bank[:].rearrange("p t j -> p j t"), func=ACT.Tanh)
 
-        def up(h, u):
-            cols = slice(u * UNIT, (u + 1) * UNIT)
-            bank = psum.tile([P, PACK, UNIT], F32, name="up")
-            for t in range(PACK):
-                for a in (1, 0):
-                    lo = h * PASS + t * P
-                    nc.tensor.matmul_mx(
-                        out=bank[:, t, :],
-                        lhsT=wu_codes[a][:, lo : lo + P].bitcast(FP8X4),
-                        lhsT_scale=wu_sc[a][:, lo : lo + P],
-                        rhs=x_codes[a][:, cols].bitcast(FP8X4),
-                        rhs_scale=x_sc[a][:, cols],
-                        start=(a == 1),
-                        stop=(a == 0),
-                    )
-            slot = 2 * h + u % 2
-            product = h_rounded[u // 2][:, slot * PACK * UNIT : (slot + 1) * PACK * UNIT]
-            if u >= 2 and slot < 3:
-                moved = moved_tile[u // 2][:, slot, :]
+        def hidden(s, u):
+            chunk, slot = u // 2, 2 * s + u % 2
+
+            def wg_part(a, t):
+                lo = s * PASS + t * P
+                return wg_codes[s][:, a * PASS + t * P : a * PASS + (t + 1) * P], wg_sc[4 * a :, lo : lo + P]
+
+            def wu_part(a, t):
+                lo = s * PASS + t * P
+                return wu_codes[a][:, lo : lo + P], wu_sc[a][:, lo : lo + P]
+
+            gated = gated_tile[chunk][:, slot, :]
+            gate = psum.tile([P, PACK, UNIT], F32, name="gate")
+            first_products(gate, u, wg_part)
+            nc.scalar.activation(
+                out=gated.rearrange("p (j t) -> p j t", t=PACK),
+                in_=gate[:].rearrange("p t j -> p j t"),
+                func=ACT.Tanh,
+                bias=no_bias,
+            )
+            up = psum.tile([P, PACK, UNIT], F32, name="up")
+            first_products(up, u, wu_part)
+            product = h_rounded[chunk][:, slot * PACK * UNIT : (slot + 1) * PACK * UNIT]
+            if chunk > 0:
+                moved = moved_tile[chunk][:, slot, :]
                 nc.scalar.copy(
-                    out=moved.rearrange("p (j t) -> p j t", t=PACK), in_=bank[:].rearrange("p t j -> p j t")
+                    out=moved.rearrange("p (j t) -> p j t", t=PACK), in_=up[:].rearrange("p t j -> p j t")
                 )
-                nc.gpsimd.tensor_tensor(product, moved, gated(h, u), MULT)
+                nc.gpsimd.tensor_tensor(product, moved, gated, MULT)
             else:
                 nc.vector.tensor_tensor(
                     product.rearrange("p (j t) -> p j t", t=PACK),
-                    bank[:].rearrange("p t j -> p j t"),
-                    gated(h, u).rearrange("p (j t) -> p j t", t=PACK),
+                    up[:].rearrange("p t j -> p j t"),
+                    gated.rearrange("p (j t) -> p j t", t=PACK),
                     MULT,
                 )
 
-        def unit(h, u):
-            gate(h, u)
-            up(h, u)
+        def hidden_half(s, chunk):
+            hidden(s, 2 * chunk)
+            hidden(s, 2 * chunk + 1)
 
-        def output(chunk, n):
-            lo, hi = CHUNKS[chunk]
-            width = hi - lo
-            step = UNIT
+        def quantise_h(chunk):
+            nc.vector.quantize_mx(out=h_codes[chunk].bitcast(FP8X4), scales=h_sc[chunk], in_=h_rounded[chunk][:])
+
+        def output(chunk, n, beside_gpsimd):
+            lo, hi = chunk * CHUNK, (chunk + 1) * CHUNK
             acc = psum_y.tile([P, HALF], F32, name="acc")
-            cols = slice(n * P, (n + 1) * P)
-            for first in range(0, width, step):
-                tokens = slice(lo + first, lo + first + step)
+            rows = slice(n * P, (n + 1) * P)
+            for first in range(0, CHUNK, UNIT):
+                below, above = slice(first, first + UNIT), slice(CHUNK + first, CHUNK + first + UNIT)
                 nc.tensor.matmul_mx(
-                    out=acc[:, first : first + step],
-                    lhsT=wd8_codes[:, cols].bitcast(FP8X4),
-                    lhsT_scale=wd8_sc[:, cols],
-                    rhs=h_codes[0][:, tokens].bitcast(FP8X4),
-                    rhs_scale=h_sc[0][:, tokens],
+                    out=acc[:, below],
+                    lhsT=wd8_codes[:, rows].bitcast(FP8X4),
+                    lhsT_scale=wd8_sc[:, rows],
+                    rhs=h_codes[chunk][:, below].bitcast(FP8X4),
+                    rhs_scale=h_sc[chunk][:, below],
                     start=True,
                     stop=False,
                 )
                 nc.tensor.matmul_mx(
-                    out=acc[:, first : first + step],
+                    out=acc[:, below],
                     lhsT=wd4_codes[:, 2 * n * P : 2 * (n + 1) * P].bitcast(FP4X4),
-                    lhsT_scale=wd4_sc[:, cols],
-                    rhs=h_codes[1][:, tokens].bitcast(FP8X4),
-                    rhs_scale=h_sc[1][:, tokens],
+                    lhsT_scale=wd4_sc[:, rows],
+                    rhs=h_codes[chunk][:, above].bitcast(FP8X4),
+                    rhs_scale=h_sc[chunk][:, above],
                     start=False,
                     stop=True,
                 )
             c, first = divmod(lo, HALF)
-            y = picked[0, c][:, n, first : first + width]
+            y = picked[0, c][:, n, first : first + CHUNK]
             if (chunk, n) == (0, 1):
-                y = x_rounded[1, 1][:].bitcast(F32)[:, 0:width]
+                y = x_rounded[1, 1][:].bitcast(F32)[:, 0:CHUNK]
             if (chunk, n) == (2, 3):
                 y = picked[0, 1][:, 1, CHUNK:HALF]
-            offsets = place_list[:, lo // 16 : hi // 16]
-            weighted = picked[1, 0][:, n, first : first + width]
-            if chunk < 3 and n == 0:
+            weighted = picked[1, 0][:, n, first : first + CHUNK]
+            places = pages[n][:].indirect(place_list[:, lo // GROUP : hi // GROUP])
+            if beside_gpsimd and n == 0:
                 nc.vector.scalar_tensor_tensor(
-                    weighted, acc[:, 0:width], bias[:, n : n + 1], wgo_sb[:, lo:hi], ADD, MULT
+                    weighted, acc[:, 0:CHUNK], bias[:, n : n + 1], wgo_sb[:, lo:hi], ADD, MULT
                 )
-                nc.vector.tensor_copy(pages[n][:].indirect(offsets), weighted)
+                nc.vector.tensor_copy(places, weighted)
                 return
-            nc.scalar.activation(out=y, in_=acc[:, 0:width], func=ACT.Identity, bias=bias[:, n : n + 1])
-            if 4 * chunk + n < 11:
+            nc.scalar.activation(out=y, in_=acc[:, 0:CHUNK], func=ACT.Identity, bias=bias[:, n : n + 1])
+            if beside_gpsimd:
                 nc.gpsimd.tensor_tensor(weighted, y, wgo_sb[:, lo:hi], MULT)
-                nc.vector.tensor_copy(pages[n][:].indirect(offsets), weighted)
+                nc.vector.tensor_copy(places, weighted)
             else:
-                nc.vector.tensor_tensor(pages[n][:].indirect(offsets), y, wgo_sb[:, lo:hi], MULT)
+                nc.vector.tensor_tensor(places, y, wgo_sb[:, lo:hi], MULT)
+
+        def store(n):
+            nc.sync.dma_start(out=out[n * P : (n + 1) * P, :], in_=pages[n][:])
 
         for i in range(PACK):
             gather(0, i, 0, HALF)
@@ -298,12 +298,12 @@ def tile_list_tanh_mix_scatb_kernel(
         gather(1, 2, 0, HALF)
         deal_wg_scales()
         quantise_wu(1, 0)
-        for lo, hi in CHUNKS[:2]:
-            gather(1, 3, lo, hi)
-            round_x(1, lo, hi)
+        for lo in range(0, HALF, CHUNK):
+            gather(1, 3, lo, lo + CHUNK)
+            round_x(1, lo, lo + CHUNK)
         deal_wg_words(0)
-        for lo, hi in CHUNKS[:2]:
-            quantise_x(1, lo, hi)
+        for lo in range(0, HALF, CHUNK):
+            quantise_x(1, lo, lo + CHUNK)
         gather(1, 2, HALF, J)
         gather(1, 3, HALF, J)
         round_wu(0, 1)
@@ -312,31 +312,31 @@ def tile_list_tanh_mix_scatb_kernel(
         deal_wg_words(1)
         quantise_wu(1, 1)
 
-        def half_hidden(h, chunk):
-            unit(h, 2 * chunk)
-            unit(h, 2 * chunk + 1)
-            quantise_h(h, chunk)
-
-        def store(n):
-            nc.sync.dma_start(out=out[n * P : (n + 1) * P, :], in_=pages[n][:])
-
-        half_hidden(0, 0)
-        half_hidden(1, 0)
-        for chunk in range(3):
-            output(chunk, 0)
-            output(chunk, 1)
+        hidden_half(0, 0)
+        hidden_half(1, 0)
+        quantise_h(0)
+        for chunk in range(CHUNKS - 2):
+            output(chunk, 0, True)
+            output(chunk, 1, True)
             if chunk == 0:
                 round_x(1, HALF, J)
-            half_hidden(0, chunk + 1)
-            if chunk < 2:
-                output(chunk, 2)
+            hidden_half(0, chunk + 1)
+            output(chunk, 2, True)
             if chunk == 0:
                 quantise_x(1, HALF, J)
-            half_hidden(1, chunk + 1)
-            output(chunk, 3 if chunk < 2 else 2)
-        for n in range(3):
-            output(3, n)
+            hidden_half(1, chunk + 1)
+            quantise_h(chunk + 1)
+            output(chunk, 3, True)
+        before_last, last = CHUNKS - 2, CHUNKS - 1
+        output(before_last, 0, True)
+        output(before_last, 1, True)
+        hidden_half(0, last)
+        hidden_half(1, last)
+        quantise_h(last)
+        output(before_last, 2, True)
+        for n in range(PAGES - 1):
+            output(last, n, False)
             store(n)
-        output(2, 3)
-        output(3, 3)
-        store(3)
+        output(before_last, PAGES - 1, False)
+        output(last, PAGES - 1, False)
+        store(PAGES - 1)

@@ -21,10 +21,12 @@ PACK = 4
 PASS = P * PACK
 GROUP = 16
 HALF = J // 2
-CHUNK = 256
 UNIT = 128
-CHUNKS = J // CHUNK
 PAGES = N // P
+CHUNKS = [(0, 128), (128, 256), (256, 512), (512, 768), (768, 1024)]
+LATE_PIECES = [(0, 256), (256, 512), (512, 1024)]
+SLOTS = 4
+SUM_BANKS = 5
 
 
 def tile_list_tanh_mix_scatb_kernel(
@@ -33,16 +35,23 @@ def tile_list_tanh_mix_scatb_kernel(
     nc = tc.nc
     with ExitStack() as ctx:
         keep = ctx.enter_context(tc.tile_pool(name="keep", bufs=1))
-        psum = ctx.enter_context(tc.psum_pool(name="psum", bufs=3))
-        psum_y = ctx.enter_context(tc.psum_pool(name="psum_y", bufs=2))
+        psum = ctx.enter_context(tc.psum_pool(name="psum", bufs=1))
+        sum_banks = [psum.tile([P, PACK, UNIT], F32, name=f"sum_bank{v}") for v in range(SUM_BANKS)]
+        vector_banks = [psum.tile([P, PASS], F32, name=f"vector_bank{v}") for v in range(2)]
+        scalar_bank = psum.tile([P, PASS], F32, name="scalar_bank")
 
         pick_list = keep.tile([P, J // GROUP], U16, name="pick_list")
         place_list = keep.tile([P, J // GROUP], U16, name="place_list")
         planes = [[keep.tile([P, T], F32, name=f"x{a}{i}") for i in range(PACK)] for a in range(2)]
         pages = [keep.tile([P, T], F32, name=f"page{n}") for n in range(PAGES)]
-        picked = {(a, c): keep.tile([P, PACK, HALF], F32, name=f"picked{a}{c}") for a in range(2) for c in range(2)}
-        wu_raw = {(a, s): keep.tile([P, PACK, PASS], F32, name=f"wu_raw{a}{s}") for a in range(2) for s in range(2)}
-        wgt_half = [keep.tile([P, HALF], F32, name=f"wgt{c}") for c in range(2)]
+        pieces = [[(0, HALF), (HALF, J)], LATE_PIECES]
+        picked = {
+            (a, lo): keep.tile([P, (PACK + a * lo // HALF) * (hi - lo)], F32, name=f"picked{a}_{lo}", align_bytes=64)
+            for a in range(2)
+            for lo, hi in pieces[a]
+        }
+        wu_raw = {(a, s): keep.tile([P, PACK * PASS], F32, name=f"wu_raw{a}{s}") for a in range(2) for s in range(2)}
+        wgt_sb = keep.tile([P, J], F32, name="wgt_sb")
         wgo_sb = keep.tile([P, J], F32, name="wgo_sb")
         bias = keep.tile([P, PAGES], F32, name="bias")
         zeros = keep.tile([P, 8], F32, name="zeros")
@@ -59,26 +68,55 @@ def tile_list_tanh_mix_scatb_kernel(
         wu_codes = [keep.tile([P, R], I32, name=f"wu_codes{a}", align_bytes=64) for a in range(2)]
         wu_sc = [keep.tile([P, R], U8, name=f"wu_sc{a}", align_bytes=64) for a in range(2)]
         h_sc_tiles = [keep.tile([P, J], U8, name=f"h_sc{c}", align_bytes=64) for c in range(2)]
-        rounded = [keep.tile([P, PACK * HALF], BF16, name=f"rounded{v}", align_bytes=64) for v in range(5)]
+        rounded = [keep.tile([P, PACK * HALF], BF16, name=f"rounded{v}", align_bytes=64) for v in range(4)]
 
-        late_planes = picked[1, 1][:, 2:4, :].rearrange("p i j -> p (i j)").bitcast(BF16)
-        x_rounded = {(0, 0): rounded[0], (0, 1): rounded[1], (1, 0): late_planes, (1, 1): rounded[0]}
-        wu_rounded = {(0, 0): rounded[2], (1, 0): rounded[3], (0, 1): rounded[4], (1, 1): rounded[0]}
-        h_rounded = [rounded[2], rounded[3], rounded[1], rounded[4]]
-        gated_tile = [wu_raw[1, 1], wu_raw[0, 0], wu_raw[1, 0], wu_raw[0, 0]]
-        moved_tile = {1: wu_raw[0, 1], 2: wu_raw[1, 1], 3: wu_raw[0, 1]}
-        h_cols = [slice(chunk % 2 * 2 * CHUNK, (chunk % 2 + 1) * 2 * CHUNK) for chunk in range(CHUNKS)]
-        h_codes = [wg_raw[chunk // 2][:, h_cols[chunk]] for chunk in range(CHUNKS)]
-        h_sc = [h_sc_tiles[chunk // 2][:, h_cols[chunk]] for chunk in range(CHUNKS)]
+        late_rounded = picked[0, 0][:].bitcast(BF16)
+        wu_rounded = {(0, 0): rounded[2], (1, 0): rounded[3], (0, 1): rounded[2], (1, 1): picked[1, HALF][:, 3 * HALF : 5 * HALF].bitcast(BF16)}
+        gated_ring, moved_ring = wu_raw[0, 0], wu_raw[1, 0]
+        spare = [picked[0, HALF], wu_raw[0, 1]]
+        taken = [0]
+        turn = [0]
+
+        def take(width):
+            v, first = divmod(taken[0], PACK * HALF)
+            taken.insert(0, taken[0] + width)
+            return spare[v][:, first : first + width]
+
+        def x_rounded(a, lo, hi):
+            if a == 1:
+                return late_rounded[:, PACK * lo : PACK * hi]
+            c, first = divmod(lo, HALF)
+            return rounded[c][:, PACK * first : PACK * (first + hi - lo)]
+
+        def h_rounded(chunk):
+            lo, hi = CHUNKS[chunk]
+            if chunk == 0:
+                return picked[1, HALF][:, 2 * HALF : 3 * HALF].bitcast(BF16)
+            return rounded[int(chunk == 1)][:, 0 : 2 * PACK * (hi - lo)]
+
+        def h_codes(chunk):
+            lo, hi = CHUNKS[chunk]
+            c, first = divmod(lo, HALF)
+            cols = slice(2 * first, 2 * (first + hi - lo))
+            return wg_raw[c][:, cols], h_sc_tiles[c][:, cols]
 
         x_rows = xT.rearrange("(a p i) t -> a i p t", a=2, i=PACK)
 
         def load_x(a, i):
             nc.sync.dma_start(out=planes[a][i][:], in_=x_rows[a, i])
 
-        def load_wu(a, s):
-            rows = wu[a * PASS : (a + 1) * PASS, s * PASS : (s + 1) * PASS]
-            nc.sync.dma_start(out=wu_raw[a, s][:], in_=rows.rearrange("(p i) r -> p i r", i=PACK))
+        def wu_part(a, s, part, parts):
+            width = PASS // parts
+            return wu_raw[a, s][:, part * PACK * width : (part + 1) * PACK * width]
+
+        def load_wu(a, s, part=0, parts=1):
+            width = PASS // parts
+            first = s * PASS + part * width
+            rows = wu[a * PASS : (a + 1) * PASS, first : first + width]
+            nc.sync.dma_start(
+                out=wu_part(a, s, part, parts).rearrange("p (i r) -> p i r", i=PACK),
+                in_=rows.rearrange("(p i) r -> p i r", i=PACK),
+            )
 
         def load_wg(s):
             words = wg_words[:, :, s * PASS : (s + 1) * PASS, :].rearrange("a p r i -> p a (r i)")
@@ -96,66 +134,68 @@ def tile_list_tanh_mix_scatb_kernel(
         nc.scalar.activation(out=zeros[:, 4:8], in_=zeros[:, 0:4], func=ACT.Tanh)
         no_bias = zeros[:, 4:5]
         for tile in (wg_sc_raw, wd8_sc, wd4_sc):
-            nc.vector.memset(tile[:].bitcast(I32), 0)
+            nc.gpsimd.memset(tile[:].bitcast(I32), 0)
         load_scale_rows(nc.gpsimd, wd8_sc, wd8_scales)
         load_scale_rows(nc.gpsimd, wd4_sc, wd4_scales)
         for page in pages:
             nc.gpsimd.memset(page[:], 0.0)
 
         nc.sync.dma_start(pick_list[:], offs)
+        nc.sync.dma_start(out=wgt_sb[:, 0:HALF], in_=wgt[:, 0:HALF])
         load_x(0, 0)
-        nc.sync.dma_start(out=wgt_half[0][:], in_=wgt[:, 0:HALF])
-        nc.sync.dma_start(out=wgt_half[1][:], in_=wgt[:, HALF:J])
         load_x(0, 1)
+        nc.sync.dma_start(out=wgt_sb[:, HALF:J], in_=wgt[:, HALF:J])
         load_x(0, 2)
-        load_x(0, 3)
         load_wu(0, 0)
+        load_x(0, 3)
         load_x(1, 0)
+        load_wu(1, 0)
         load_x(1, 1)
         load_scale_rows(nc.sync, wg_sc_raw, wg_scales)
-        load_wu(1, 0)
         load_x(1, 2)
+        load_wu(0, 1)
         load_x(1, 3)
         load_wg(0)
-        load_wu(0, 1)
-        load_wu(1, 1)
+        load_wu(1, 1, 0, 2)
+        load_wu(1, 1, 1, 2)
         load_wg(1)
         nc.sync.dma_start(out=wd8_codes[:], in_=wd8_words[0].rearrange("p n i -> p (n i)").bitcast(I32))
         nc.sync.dma_start(out=wd4_codes[:].bitcast(I32), in_=wd4_words[0].bitcast(I32))
-        nc.sync.dma_start(place_list[:], offs2)
-        nc.sync.dma_start(out=wgo_sb[:], in_=wgo)
         with nc.allow_non_contiguous_dma(reason="one bias value for each partition and page"):
             nc.sync.dma_start(out=bias[:], in_=b.rearrange("(n p) -> p n", p=P))
+        nc.sync.dma_start(place_list[:], offs2)
+        nc.sync.dma_start(out=wgo_sb[:, 0:256], in_=wgo[:, 0:256])
+        nc.sync.dma_start(out=wgo_sb[:, 256:J], in_=wgo[:, 256:J])
 
-        def gather(a, i, lo, hi):
-            c, first = divmod(lo, HALF)
-            cols = slice(first, first + hi - lo)
-            offsets = pick_list[:, lo // GROUP : hi // GROUP]
-            nc.vector.tensor_tensor(
-                picked[a, c][:, i, cols], planes[a][i][:].indirect(offsets), wgt_half[c][:, cols], MULT
-            )
+        def gather(a, i, which=slice(0, 3)):
+            for lo, hi in pieces[a][which]:
+                nc.vector.tensor_tensor(
+                    picked[a, lo][:, i * (hi - lo) : (i + 1) * (hi - lo)],
+                    planes[a][i][:].indirect(pick_list[:, lo // GROUP : hi // GROUP]),
+                    wgt_sb[:, lo:hi],
+                    MULT,
+                )
 
         def round_x(a, lo, hi):
-            c, first = divmod(lo, HALF)
+            start = max(first for first, last in pieces[a] if first <= lo)
+            width = dict(pieces[a])[start] - start
+            rows = picked[a, start][:, 0 : PACK * width].rearrange("p (i j) -> p i j", i=PACK)
             nc.scalar.copy(
-                out=x_rounded[a, c][:, PACK * first : PACK * (first + hi - lo)].rearrange(
-                    "p (g e i) -> p g i e", e=4, i=PACK
-                ),
-                in_=picked[a, c][:, :, first : first + hi - lo].rearrange("p i (g e) -> p g i e", e=4),
+                out=x_rounded(a, lo, hi).rearrange("p (g e i) -> p g i e", e=4, i=PACK),
+                in_=rows[:, :, lo - start : hi - start].rearrange("p i (g e) -> p g i e", e=4),
             )
 
         def quantise_x(a, lo, hi):
-            c, first = divmod(lo, HALF)
             nc.vector.quantize_mx(
-                out=x_codes[a][:, lo:hi].bitcast(FP8X4),
-                scales=x_sc[a][:, lo:hi],
-                in_=x_rounded[a, c][:, PACK * first : PACK * (first + hi - lo)],
+                out=x_codes[a][:, lo:hi].bitcast(FP8X4), scales=x_sc[a][:, lo:hi], in_=x_rounded(a, lo, hi)
             )
 
-        def round_wu(a, s):
+        def round_wu(a, s, part=0, parts=1):
+            width = P // parts
+            dealt = wu_rounded[a, s][:].rearrange("p (t q i) -> p q i t", t=PACK, i=PACK)
             nc.scalar.copy(
-                out=wu_rounded[a, s][:].rearrange("p (t q i) -> p q i t", t=PACK, i=PACK),
-                in_=wu_raw[a, s][:].rearrange("p i (q t) -> p q i t", t=PACK),
+                out=dealt[:, part * width : (part + 1) * width],
+                in_=wu_part(a, s, part, parts).rearrange("p (i q t) -> p q i t", i=PACK, t=PACK),
             )
 
         def quantise_wu(a, s):
@@ -176,7 +216,9 @@ def tile_list_tanh_mix_scatb_kernel(
                 in_=wg_sc_raw[:].rearrange("p (s q t) -> p s t q", t=PACK, q=P),
             )
 
-        def first_products(bank, u, stationary):
+        def first_products(u, stationary):
+            bank = sum_banks[turn[0] % SUM_BANKS]
+            turn.insert(0, turn[0] + 1)
             cols = slice(u * UNIT, (u + 1) * UNIT)
             for t in range(PACK):
                 for a in (1, 0):
@@ -190,63 +232,64 @@ def tile_list_tanh_mix_scatb_kernel(
                         start=(a == 1),
                         stop=(a == 0),
                     )
+            return bank[:].rearrange("p t j -> p j t")
 
-        def hidden(s, u):
-            chunk, slot = u // 2, 2 * s + u % 2
+        def hidden(chunk, s, u):
+            lo, hi = CHUNKS[chunk]
 
-            def wg_part(a, t):
-                lo = s * PASS + t * P
-                return wg_codes[s][:, a * PASS + t * P : a * PASS + (t + 1) * P], wg_sc[4 * a :, lo : lo + P]
+            def wg_stationary(a, t):
+                first = s * PASS + t * P
+                return wg_codes[s][:, a * PASS + t * P : a * PASS + (t + 1) * P], wg_sc[4 * a :, first : first + P]
 
-            def wu_part(a, t):
-                lo = s * PASS + t * P
-                return wu_codes[a][:, lo : lo + P], wu_sc[a][:, lo : lo + P]
+            def wu_stationary(a, t):
+                first = s * PASS + t * P
+                return wu_codes[a][:, first : first + P], wu_sc[a][:, first : first + P]
 
-            gated = gated_tile[chunk][:, slot, :]
-            gate = psum.tile([P, PACK, UNIT], F32, name="gate")
-            first_products(gate, u, wg_part)
+            slot = turn[0] // 2 % SLOTS
+            ring = slice(slot * PASS, (slot + 1) * PASS)
+            gated = gated_ring[:, ring]
+            gate = first_products(u, wg_stationary)
             nc.scalar.activation(
-                out=gated.rearrange("p (j t) -> p j t", t=PACK),
-                in_=gate[:].rearrange("p t j -> p j t"),
-                func=ACT.Tanh,
-                bias=no_bias,
+                out=gated.rearrange("p (j t) -> p j t", t=PACK), in_=gate, func=ACT.Tanh, bias=no_bias
             )
-            up = psum.tile([P, PACK, UNIT], F32, name="up")
-            first_products(up, u, wu_part)
-            product = h_rounded[chunk][:, slot * PACK * UNIT : (slot + 1) * PACK * UNIT]
-            if chunk > 0:
-                moved = moved_tile[chunk][:, slot, :]
-                nc.scalar.copy(
-                    out=moved.rearrange("p (j t) -> p j t", t=PACK), in_=up[:].rearrange("p t j -> p j t")
-                )
-                nc.gpsimd.tensor_tensor(product, moved, gated, MULT)
-            else:
+            up = first_products(u, wu_stationary)
+            first = PACK * (s * (hi - lo) + u * UNIT - lo)
+            product = h_rounded(chunk)[:, first : first + PACK * UNIT]
+            if chunk == 0:
                 nc.vector.tensor_tensor(
                     product.rearrange("p (j t) -> p j t", t=PACK),
-                    up[:].rearrange("p t j -> p j t"),
+                    up,
                     gated.rearrange("p (j t) -> p j t", t=PACK),
                     MULT,
                 )
+            else:
+                moved = moved_ring[:, ring]
+                nc.scalar.copy(out=moved.rearrange("p (j t) -> p j t", t=PACK), in_=up)
+                nc.gpsimd.tensor_tensor(product, moved, gated, MULT)
 
-        def hidden_half(s, chunk):
-            hidden(s, 2 * chunk)
-            hidden(s, 2 * chunk + 1)
+        def hidden_half(chunk, s):
+            lo, hi = CHUNKS[chunk]
+            for u in range(lo // UNIT, hi // UNIT):
+                hidden(chunk, s, u)
 
         def quantise_h(chunk):
-            nc.vector.quantize_mx(out=h_codes[chunk].bitcast(FP8X4), scales=h_sc[chunk], in_=h_rounded[chunk][:])
+            codes, scales = h_codes(chunk)
+            nc.vector.quantize_mx(out=codes.bitcast(FP8X4), scales=scales, in_=h_rounded(chunk))
 
-        def output(chunk, n, beside_gpsimd):
-            lo, hi = chunk * CHUNK, (chunk + 1) * CHUNK
-            acc = psum_y.tile([P, HALF], F32, name="acc")
+        def output_sums(chunk, n, bank, side):
+            lo, hi = CHUNKS[chunk]
+            width = hi - lo
+            codes, scales = h_codes(chunk)
             rows = slice(n * P, (n + 1) * P)
-            for first in range(0, CHUNK, UNIT):
-                below, above = slice(first, first + UNIT), slice(CHUNK + first, CHUNK + first + UNIT)
+            acc = bank[:, side * 256 : side * 256 + width]
+            for first in range(0, width, UNIT):
+                below, above = slice(first, first + UNIT), slice(width + first, width + first + UNIT)
                 nc.tensor.matmul_mx(
                     out=acc[:, below],
                     lhsT=wd8_codes[:, rows].bitcast(FP8X4),
                     lhsT_scale=wd8_sc[:, rows],
-                    rhs=h_codes[chunk][:, below].bitcast(FP8X4),
-                    rhs_scale=h_sc[chunk][:, below],
+                    rhs=codes[:, below].bitcast(FP8X4),
+                    rhs_scale=scales[:, below],
                     start=True,
                     stop=False,
                 )
@@ -254,89 +297,102 @@ def tile_list_tanh_mix_scatb_kernel(
                     out=acc[:, below],
                     lhsT=wd4_codes[:, 2 * n * P : 2 * (n + 1) * P].bitcast(FP4X4),
                     lhsT_scale=wd4_sc[:, rows],
-                    rhs=h_codes[chunk][:, above].bitcast(FP8X4),
-                    rhs_scale=h_sc[chunk][:, above],
+                    rhs=codes[:, above].bitcast(FP8X4),
+                    rhs_scale=scales[:, above],
                     start=False,
                     stop=True,
                 )
-            c, first = divmod(lo, HALF)
-            y = picked[0, c][:, n, first : first + CHUNK]
-            if (chunk, n) == (0, 1):
-                y = x_rounded[1, 1][:].bitcast(F32)[:, 0:CHUNK]
-            if (chunk, n) == (2, 3):
-                y = picked[0, 1][:, 1, CHUNK:HALF]
-            weighted = picked[1, 0][:, n, first : first + CHUNK]
-            places = pages[n][:].indirect(place_list[:, lo // GROUP : hi // GROUP])
-            if beside_gpsimd and n == 0:
-                nc.vector.scalar_tensor_tensor(
-                    weighted, acc[:, 0:CHUNK], bias[:, n : n + 1], wgo_sb[:, lo:hi], ADD, MULT
-                )
-                nc.vector.tensor_copy(places, weighted)
-                return
-            nc.scalar.activation(out=y, in_=acc[:, 0:CHUNK], func=ACT.Identity, bias=bias[:, n : n + 1])
-            if beside_gpsimd:
-                nc.gpsimd.tensor_tensor(weighted, y, wgo_sb[:, lo:hi], MULT)
-                nc.vector.tensor_copy(places, weighted)
-            else:
-                nc.vector.tensor_tensor(places, y, wgo_sb[:, lo:hi], MULT)
+            return acc
+
+        def places(chunk, n):
+            lo, hi = CHUNKS[chunk]
+            return pages[n][:].indirect(place_list[:, lo // GROUP : hi // GROUP])
+
+        def by_vector(chunk, n, acc, staged):
+            lo, hi = CHUNKS[chunk]
+            nc.vector.scalar_tensor_tensor(staged, acc, bias[:, n : n + 1], wgo_sb[:, lo:hi], ADD, MULT)
+            nc.vector.tensor_copy(places(chunk, n), staged)
+
+        def by_gpsimd(chunk, n, acc, staged):
+            lo, hi = CHUNKS[chunk]
+            nc.scalar.activation(out=staged, in_=acc, func=ACT.Identity, bias=bias[:, n : n + 1])
+            nc.gpsimd.tensor_tensor(staged, staged, wgo_sb[:, lo:hi], MULT)
+            nc.vector.tensor_copy(places(chunk, n), staged)
+
+        def fused(chunk, n, acc, staged):
+            lo, hi = CHUNKS[chunk]
+            nc.scalar.activation(out=staged, in_=acc, func=ACT.Identity, bias=bias[:, n : n + 1])
+            nc.vector.tensor_tensor(places(chunk, n), staged, wgo_sb[:, lo:hi], MULT)
+
+        def held_place(chunk):
+            lo, hi = CHUNKS[chunk]
+            words = h_rounded(chunk + 1).bitcast(F32)
+            return words[:, words.shape[1] - (hi - lo) :]
 
         def store(n):
             nc.sync.dma_start(out=out[n * P : (n + 1) * P, :], in_=pages[n][:])
 
-        for i in range(PACK):
-            gather(0, i, 0, HALF)
-            gather(0, i, HALF, J)
+        gather(0, 0)
+        gather(0, 1)
+        gather(0, 2)
         round_wu(0, 0)
+        gather(0, 3)
         quantise_wu(0, 0)
         round_x(0, 0, HALF)
         round_x(0, HALF, J)
+        gather(1, 0)
+        quantise_x(0, 0, HALF)
         round_wu(1, 0)
-        for i in range(2):
-            gather(1, i, 0, HALF)
-            gather(1, i, HALF, J)
-            quantise_x(0, i * HALF, (i + 1) * HALF)
-        gather(1, 2, 0, HALF)
+        gather(1, 1)
+        quantise_x(0, HALF, J)
         deal_wg_scales()
+        gather(1, 2, slice(0, 2))
         quantise_wu(1, 0)
-        for lo in range(0, HALF, CHUNK):
-            gather(1, 3, lo, lo + CHUNK)
-            round_x(1, lo, lo + CHUNK)
-        deal_wg_words(0)
-        for lo in range(0, HALF, CHUNK):
-            quantise_x(1, lo, lo + CHUNK)
-        gather(1, 2, HALF, J)
-        gather(1, 3, HALF, J)
         round_wu(0, 1)
+        gather(1, 3, slice(0, 2))
         quantise_wu(0, 1)
-        round_wu(1, 1)
+        round_x(1, 0, 256)
+        deal_wg_words(0)
+        quantise_x(1, 0, 256)
+        round_wu(1, 1, 0, 2)
+        round_wu(1, 1, 1, 2)
+        hidden_half(0, 0)
         deal_wg_words(1)
         quantise_wu(1, 1)
-
-        hidden_half(0, 0)
-        hidden_half(1, 0)
+        gather(1, 3, slice(2, 3))
+        hidden_half(0, 1)
         quantise_h(0)
-        for chunk in range(CHUNKS - 2):
-            output(chunk, 0, True)
-            output(chunk, 1, True)
-            if chunk == 0:
-                round_x(1, HALF, J)
-            hidden_half(0, chunk + 1)
-            output(chunk, 2, True)
-            if chunk == 0:
-                quantise_x(1, HALF, J)
-            hidden_half(1, chunk + 1)
+        gather(1, 2, slice(2, 3))
+
+        last = len(CHUNKS) - 1
+        for chunk in range(last):
+            width = CHUNKS[chunk][1] - CHUNKS[chunk][0]
+            held = 3 if chunk < last - 1 else 2
+            middle = [n for n in (1, 2) if n != held]
+            bank = vector_banks[chunk % 2]
+            first_sums = output_sums(chunk, 0, bank, 0)
+            held_sums = output_sums(chunk, held, bank, 1)
+            middle_sums = [output_sums(chunk, n, scalar_bank, side) for side, n in enumerate(middle)]
+            by_vector(chunk, 0, first_sums, take(width))
+            for n, acc in zip(middle, middle_sums):
+                (by_gpsimd if chunk > 0 else by_vector)(chunk, n, acc, take(width))
+            hidden_half(chunk + 1, 0)
+            hidden_half(chunk + 1, 1)
+            if chunk < 3:
+                lo = 256 * (chunk + 1)
+                round_x(1, lo, lo + 256)
+                quantise_x(1, lo, lo + 256)
             quantise_h(chunk + 1)
-            output(chunk, 3, True)
-        before_last, last = CHUNKS - 2, CHUNKS - 1
-        output(before_last, 0, True)
-        output(before_last, 1, True)
-        hidden_half(0, last)
-        hidden_half(1, last)
-        quantise_h(last)
-        output(before_last, 2, True)
-        for n in range(PAGES - 1):
-            output(last, n, False)
+            by_vector(chunk, held, held_sums, held_place(chunk))
+        sums = [output_sums(last, n, scalar_bank, n) for n in range(2)]
+        staged = [take(256) for n in range(PAGES)]
+        for n in range(2):
+            fused(last, n, sums[n], staged[n])
             store(n)
-        output(before_last, PAGES - 1, False)
-        output(last, PAGES - 1, False)
-        store(PAGES - 1)
+        bank = vector_banks[last % 2]
+        sums = [output_sums(last, 2, bank, 0), output_sums(last - 1, 3, bank, 1)]
+        fused(last, 2, sums[0], staged[2])
+        store(2)
+        fused(last - 1, 3, sums[1], staged[1])
+        fused(last, 3, output_sums(last, 3, scalar_bank, 0), staged[3])
+        store(3)

@@ -23,8 +23,7 @@ GROUP = 16
 HALF = J // 2
 UNIT = 128
 PAGES = N // P
-CHUNKS = [(0, 128), (128, 256), (256, 512), (512, 768), (768, 1024)]
-LATE_PIECES = [(0, 256), (256, 512), (512, 1024)]
+CHUNKS = [(0, 256), (256, 512), (512, 768), (768, 1024)]
 SLOTS = 4
 SUM_BANKS = 5
 
@@ -36,21 +35,20 @@ def tile_list_tanh_mix_scatb_kernel(
     with ExitStack() as ctx:
         keep = ctx.enter_context(tc.tile_pool(name="keep", bufs=1))
         psum = ctx.enter_context(tc.psum_pool(name="psum", bufs=1))
-        sum_banks = [psum.tile([P, PACK, UNIT], F32, name=f"sum_bank{v}") for v in range(SUM_BANKS)]
-        vector_banks = [psum.tile([P, PASS], F32, name=f"vector_bank{v}") for v in range(2)]
-        scalar_bank = psum.tile([P, PASS], F32, name="scalar_bank")
+        banks = [psum.tile([P, PASS], F32, name=f"bank{v}") for v in range(8)]
+        bank_a, bank_b, bank_c = banks[SUM_BANKS:]
 
         pick_list = keep.tile([P, J // GROUP], U16, name="pick_list")
         place_list = keep.tile([P, J // GROUP], U16, name="place_list")
         planes = [[keep.tile([P, T], F32, name=f"x{a}{i}") for i in range(PACK)] for a in range(2)]
         pages = [keep.tile([P, T], F32, name=f"page{n}") for n in range(PAGES)]
-        pieces = [[(0, HALF), (HALF, J)], LATE_PIECES]
+        pieces = [[(0, HALF), (HALF, J)]] * 2
         picked = {
-            (a, lo): keep.tile([P, (PACK + a * lo // HALF) * (hi - lo)], F32, name=f"picked{a}_{lo}", align_bytes=64)
+            (a, lo): keep.tile([P, PACK * (hi - lo)], F32, name=f"picked{a}_{lo}", align_bytes=64)
             for a in range(2)
             for lo, hi in pieces[a]
         }
-        wu_raw = {(a, s): keep.tile([P, PACK * PASS], F32, name=f"wu_raw{a}{s}") for a in range(2) for s in range(2)}
+        wu_raw = [keep.tile([P, PACK * R], F32, name=f"wu_raw{a}") for a in range(2)]
         wgt_sb = keep.tile([P, J], F32, name="wgt_sb")
         wgo_sb = keep.tile([P, J], F32, name="wgo_sb")
         bias = keep.tile([P, PAGES], F32, name="bias")
@@ -64,16 +62,16 @@ def tile_list_tanh_mix_scatb_kernel(
         wd8_sc = keep.tile([P, N], U8, name="wd8_sc", align_bytes=64)
         wd4_sc = keep.tile([P, N], U8, name="wd4_sc", align_bytes=64)
         x_codes = [keep.tile([P, J], I32, name=f"x_codes{a}", align_bytes=64) for a in range(2)]
-        x_sc = [keep.tile([P, J], U8, name=f"x_sc{a}", align_bytes=64) for a in range(2)]
+        x_sc = keep.tile([P, J], U8, name="x_sc", align_bytes=64)
         wu_codes = [keep.tile([P, R], I32, name=f"wu_codes{a}", align_bytes=64) for a in range(2)]
         wu_sc = [keep.tile([P, R], U8, name=f"wu_sc{a}", align_bytes=64) for a in range(2)]
         h_sc_tiles = [keep.tile([P, J], U8, name=f"h_sc{c}", align_bytes=64) for c in range(2)]
         rounded = [keep.tile([P, PACK * HALF], BF16, name=f"rounded{v}", align_bytes=64) for v in range(4)]
 
         late_rounded = picked[0, 0][:].bitcast(BF16)
-        wu_rounded = {(0, 0): rounded[2], (1, 0): rounded[3], (0, 1): rounded[2], (1, 1): picked[1, HALF][:, 3 * HALF : 5 * HALF].bitcast(BF16)}
-        gated_ring, moved_ring = wu_raw[0, 0], wu_raw[1, 0]
-        spare = [picked[0, HALF], wu_raw[0, 1]]
+        wu_rounded = {(0, 0): rounded[2], (0, 1): rounded[3], (1, 0): rounded[2], (1, 1): rounded[3]}
+        gated_ring, moved_ring = wu_raw[0][:, 0 : 2 * R], wu_raw[0][:, 2 * R : 4 * R]
+        spare = [picked[0, HALF], picked[1, 0]]
         taken = [0]
         turn = [0]
 
@@ -83,16 +81,19 @@ def tile_list_tanh_mix_scatb_kernel(
             return spare[v][:, first : first + width]
 
         def x_rounded(a, lo, hi):
-            if a == 1:
+            if a == 1 and lo == 0:
                 return late_rounded[:, PACK * lo : PACK * hi]
+            if a == 1 and hi < J:
+                first = (lo // 256 - 1) * R + PASS
+                return wu_raw[1][:, first : first + PASS].bitcast(BF16)
+            if a == 1:
+                return rounded[3][:, 0 : PACK * 256]
             c, first = divmod(lo, HALF)
             return rounded[c][:, PACK * first : PACK * (first + hi - lo)]
 
         def h_rounded(chunk):
             lo, hi = CHUNKS[chunk]
-            if chunk == 0:
-                return picked[1, HALF][:, 2 * HALF : 3 * HALF].bitcast(BF16)
-            return rounded[int(chunk == 1)][:, 0 : 2 * PACK * (hi - lo)]
+            return rounded[min(chunk, 1)][:, 0 : 2 * PACK * (hi - lo)]
 
         def h_codes(chunk):
             lo, hi = CHUNKS[chunk]
@@ -105,22 +106,12 @@ def tile_list_tanh_mix_scatb_kernel(
         def load_x(a, i):
             nc.sync.dma_start(out=planes[a][i][:], in_=x_rows[a, i])
 
-        def wu_part(a, s, part, parts):
-            width = PASS // parts
-            return wu_raw[a, s][:, part * PACK * width : (part + 1) * PACK * width]
+        def load_wu(a, half):
+            rows = wu[a * PASS : (a + 1) * PASS, :].rearrange("(p h i) r -> h p (i r)", h=2, i=2)
+            nc.sync.dma_start(out=wu_raw[a][:, half * 2 * R : (half + 1) * 2 * R], in_=rows[half])
 
-        def load_wu(a, s, part=0, parts=1):
-            width = PASS // parts
-            first = s * PASS + part * width
-            rows = wu[a * PASS : (a + 1) * PASS, first : first + width]
-            nc.sync.dma_start(
-                out=wu_part(a, s, part, parts).rearrange("p (i r) -> p i r", i=PACK),
-                in_=rows.rearrange("(p i) r -> p i r", i=PACK),
-            )
-
-        def load_wg(s):
-            words = wg_words[:, :, s * PASS : (s + 1) * PASS, :].rearrange("a p r i -> p a (r i)")
-            nc.sync.dma_start(out=wg_raw[s][:].rearrange("p (a r) -> p a r", a=2), in_=words.bitcast(I32))
+        def load_wg(a):
+            nc.sync.dma_start(out=wg_raw[a][:], in_=wg_words[a].rearrange("p r i -> p (r i)").bitcast(I32))
 
         def load_scale_rows(queue, tile, rows):
             passes = rows.shape[0]
@@ -130,72 +121,71 @@ def tile_list_tanh_mix_scatb_kernel(
                     in_=rows[:, 4 * q : 4 * q + 4, :].bitcast(I32),
                 )
 
-        nc.vector.memset(zeros[:], 0.0)
+        nc.gpsimd.memset(wg_sc_raw[:].bitcast(I32), 0)
+        nc.gpsimd.memset(zeros[:], 0.0)
         nc.scalar.activation(out=zeros[:, 4:8], in_=zeros[:, 0:4], func=ACT.Tanh)
         no_bias = zeros[:, 4:5]
-        for tile in (wg_sc_raw, wd8_sc, wd4_sc):
+        for page in pages:
+            nc.gpsimd.memset(page[:], 0.0)
+        for tile in (wd8_sc, wd4_sc):
             nc.gpsimd.memset(tile[:].bitcast(I32), 0)
         load_scale_rows(nc.gpsimd, wd8_sc, wd8_scales)
         load_scale_rows(nc.gpsimd, wd4_sc, wd4_scales)
-        for page in pages:
-            nc.gpsimd.memset(page[:], 0.0)
 
         nc.sync.dma_start(pick_list[:], offs)
-        nc.sync.dma_start(out=wgt_sb[:, 0:HALF], in_=wgt[:, 0:HALF])
         load_x(0, 0)
+        nc.sync.dma_start(out=wgt_sb[:], in_=wgt)
         load_x(0, 1)
-        nc.sync.dma_start(out=wgt_sb[:, HALF:J], in_=wgt[:, HALF:J])
         load_x(0, 2)
+        load_scale_rows(nc.sync, wg_sc_raw, wg_scales)
         load_wu(0, 0)
         load_x(0, 3)
         load_x(1, 0)
-        load_wu(1, 0)
-        load_x(1, 1)
-        load_scale_rows(nc.sync, wg_sc_raw, wg_scales)
-        load_x(1, 2)
         load_wu(0, 1)
+        load_x(1, 1)
+        load_x(1, 2)
         load_x(1, 3)
+        load_wu(1, 0)
+        load_wu(1, 1)
         load_wg(0)
-        load_wu(1, 1, 0, 2)
-        load_wu(1, 1, 1, 2)
         load_wg(1)
         nc.sync.dma_start(out=wd8_codes[:], in_=wd8_words[0].rearrange("p n i -> p (n i)").bitcast(I32))
         nc.sync.dma_start(out=wd4_codes[:].bitcast(I32), in_=wd4_words[0].bitcast(I32))
         with nc.allow_non_contiguous_dma(reason="one bias value for each partition and page"):
             nc.sync.dma_start(out=bias[:], in_=b.rearrange("(n p) -> p n", p=P))
         nc.sync.dma_start(place_list[:], offs2)
-        nc.sync.dma_start(out=wgo_sb[:, 0:256], in_=wgo[:, 0:256])
-        nc.sync.dma_start(out=wgo_sb[:, 256:J], in_=wgo[:, 256:J])
+        nc.sync.dma_start(out=wgo_sb[:], in_=wgo)
 
-        def gather(a, i, which=slice(0, 3)):
-            for lo, hi in pieces[a][which]:
-                nc.vector.tensor_tensor(
-                    picked[a, lo][:, i * (hi - lo) : (i + 1) * (hi - lo)],
-                    planes[a][i][:].indirect(pick_list[:, lo // GROUP : hi // GROUP]),
-                    wgt_sb[:, lo:hi],
-                    MULT,
-                )
+        def piece(a, lo):
+            start, stop = [part for part in pieces[a] if part[0] <= lo][-1]
+            return picked[a, start][:, 0 : PACK * (stop - start)].rearrange("p (i j) -> p i j", i=PACK), start
 
-        def round_x(a, lo, hi):
-            start = max(first for first, last in pieces[a] if first <= lo)
-            width = dict(pieces[a])[start] - start
-            rows = picked[a, start][:, 0 : PACK * width].rearrange("p (i j) -> p i j", i=PACK)
-            nc.scalar.copy(
+        def gather(a, i, lo, hi):
+            rows, start = piece(a, lo)
+            nc.vector.tensor_tensor(
+                rows[:, i, lo - start : hi - start],
+                planes[a][i][:].indirect(pick_list[:, lo // GROUP : hi // GROUP]),
+                wgt_sb[:, lo:hi],
+                MULT,
+            )
+
+        def round_x(a, lo, hi, copy=nc.scalar.copy):
+            rows, start = piece(a, lo)
+            copy(
                 out=x_rounded(a, lo, hi).rearrange("p (g e i) -> p g i e", e=4, i=PACK),
                 in_=rows[:, :, lo - start : hi - start].rearrange("p i (g e) -> p g i e", e=4),
             )
 
         def quantise_x(a, lo, hi):
             nc.vector.quantize_mx(
-                out=x_codes[a][:, lo:hi].bitcast(FP8X4), scales=x_sc[a][:, lo:hi], in_=x_rounded(a, lo, hi)
+                out=x_codes[a][:, lo:hi].bitcast(FP8X4), scales=x_sc[4 * a :, lo:hi], in_=x_rounded(a, lo, hi)
             )
 
-        def round_wu(a, s, part=0, parts=1):
-            width = P // parts
-            dealt = wu_rounded[a, s][:].rearrange("p (t q i) -> p q i t", t=PACK, i=PACK)
-            nc.scalar.copy(
-                out=dealt[:, part * width : (part + 1) * width],
-                in_=wu_part(a, s, part, parts).rearrange("p (i q t) -> p q i t", i=PACK, t=PACK),
+        def round_wu(a, s, copy):
+            rows = wu_raw[a][:].rearrange("p (i r) -> p i r", i=PACK)[:, :, s * PASS : (s + 1) * PASS]
+            copy(
+                out=wu_rounded[a, s][:].rearrange("p (t q i) -> p q i t", t=PACK, i=PACK),
+                in_=rows.rearrange("p i (q t) -> p q i t", t=PACK),
             )
 
         def quantise_wu(a, s):
@@ -204,10 +194,10 @@ def tile_list_tanh_mix_scatb_kernel(
                 out=wu_codes[a][:, cols].bitcast(FP8X4), scales=wu_sc[a][:, cols], in_=wu_rounded[a, s][:]
             )
 
-        def deal_wg_words(s):
+        def deal_wg_words(a):
             nc.vector.tensor_copy(
-                out=wg_codes[s][:].rearrange("p (a t q) -> p a q t", t=PACK, q=P),
-                in_=wg_raw[s][:].rearrange("p (a q t) -> p a q t", t=PACK, q=P),
+                out=wg_codes[a][:].rearrange("p (s t q) -> p s q t", t=PACK, q=P),
+                in_=wg_raw[a][:].rearrange("p (s q t) -> p s q t", t=PACK, q=P),
             )
 
         def deal_wg_scales():
@@ -217,29 +207,29 @@ def tile_list_tanh_mix_scatb_kernel(
             )
 
         def first_products(u, stationary):
-            bank = sum_banks[turn[0] % SUM_BANKS]
+            bank = banks[turn[0] if turn[0] < 8 else (turn[0] - 8) % SUM_BANKS][:].rearrange("p (t j) -> p t j", t=PACK)
             turn.insert(0, turn[0] + 1)
             cols = slice(u * UNIT, (u + 1) * UNIT)
-            for t in range(PACK):
-                for a in (1, 0):
+            for a in range(2):
+                for t in range(PACK):
                     codes, scales = stationary(a, t)
                     nc.tensor.matmul_mx(
                         out=bank[:, t, :],
                         lhsT=codes.bitcast(FP8X4),
                         lhsT_scale=scales,
                         rhs=x_codes[a][:, cols].bitcast(FP8X4),
-                        rhs_scale=x_sc[a][:, cols],
-                        start=(a == 1),
-                        stop=(a == 0),
+                        rhs_scale=x_sc[4 * a :, cols],
+                        start=(a == 0 and t == 0),
+                        stop=(a == 1 and t == PACK - 1),
                     )
-            return bank[:].rearrange("p t j -> p j t")
+            return bank.rearrange("p t j -> p j t")
 
         def hidden(chunk, s, u):
             lo, hi = CHUNKS[chunk]
 
             def wg_stationary(a, t):
                 first = s * PASS + t * P
-                return wg_codes[s][:, a * PASS + t * P : a * PASS + (t + 1) * P], wg_sc[4 * a :, first : first + P]
+                return wg_codes[a][:, first : first + P], wg_sc[4 * a :, first : first + P]
 
             def wu_stationary(a, t):
                 first = s * PASS + t * P
@@ -324,75 +314,75 @@ def tile_list_tanh_mix_scatb_kernel(
             nc.scalar.activation(out=staged, in_=acc, func=ACT.Identity, bias=bias[:, n : n + 1])
             nc.vector.tensor_tensor(places(chunk, n), staged, wgo_sb[:, lo:hi], MULT)
 
-        def held_place(chunk):
+        def held_place(chunk, n):
             lo, hi = CHUNKS[chunk]
             words = h_rounded(chunk + 1).bitcast(F32)
-            return words[:, words.shape[1] - (hi - lo) :]
+            first = words.shape[1] - (PAGES - n) * (hi - lo)
+            return words[:, first : first + hi - lo]
 
         def store(n):
             nc.sync.dma_start(out=out[n * P : (n + 1) * P, :], in_=pages[n][:])
 
-        gather(0, 0)
-        gather(0, 1)
-        gather(0, 2)
-        round_wu(0, 0)
-        gather(0, 3)
-        quantise_wu(0, 0)
+        for i in range(PACK):
+            gather(0, i, 0, HALF)
+            gather(0, i, HALF, J)
+        deal_wg_scales()
         round_x(0, 0, HALF)
         round_x(0, HALF, J)
-        gather(1, 0)
         quantise_x(0, 0, HALF)
-        round_wu(1, 0)
-        gather(1, 1)
         quantise_x(0, HALF, J)
-        deal_wg_scales()
-        gather(1, 2, slice(0, 2))
-        quantise_wu(1, 0)
-        round_wu(0, 1)
-        gather(1, 3, slice(0, 2))
-        quantise_wu(0, 1)
-        round_x(1, 0, 256)
+        for s in range(2):
+            round_wu(0, s, nc.scalar.copy)
+            quantise_wu(0, s)
+        for i in range(PACK):
+            gather(1, i, 0, HALF)
+            gather(1, i, HALF, J)
+        round_wu(1, 0, nc.vector.tensor_copy)
+        round_wu(1, 1, nc.scalar.copy)
         deal_wg_words(0)
-        quantise_x(1, 0, 256)
-        round_wu(1, 1, 0, 2)
-        round_wu(1, 1, 1, 2)
-        hidden_half(0, 0)
+        quantise_wu(1, 0)
         deal_wg_words(1)
         quantise_wu(1, 1)
-        gather(1, 3, slice(2, 3))
+        for lo in range(0, 768, 256):
+            round_x(1, lo, lo + 256)
+            quantise_x(1, lo, lo + 256)
+        round_x(1, 768, J, nc.vector.tensor_copy)
+        quantise_x(1, 768, J)
+        hidden_half(0, 0)
         hidden_half(0, 1)
         quantise_h(0)
-        gather(1, 2, slice(2, 3))
 
-        last = len(CHUNKS) - 1
-        for chunk in range(last):
-            width = CHUNKS[chunk][1] - CHUNKS[chunk][0]
-            held = 3 if chunk < last - 1 else 2
-            middle = [n for n in (1, 2) if n != held]
-            bank = vector_banks[chunk % 2]
-            first_sums = output_sums(chunk, 0, bank, 0)
-            held_sums = output_sums(chunk, held, bank, 1)
-            middle_sums = [output_sums(chunk, n, scalar_bank, side) for side, n in enumerate(middle)]
-            by_vector(chunk, 0, first_sums, take(width))
-            for n, acc in zip(middle, middle_sums):
-                (by_gpsimd if chunk > 0 else by_vector)(chunk, n, acc, take(width))
-            hidden_half(chunk + 1, 0)
-            hidden_half(chunk + 1, 1)
-            if chunk < 3:
-                lo = 256 * (chunk + 1)
-                round_x(1, lo, lo + 256)
-                quantise_x(1, lo, lo + 256)
-            quantise_h(chunk + 1)
-            by_vector(chunk, held, held_sums, held_place(chunk))
-        sums = [output_sums(last, n, scalar_bank, n) for n in range(2)]
-        staged = [take(256) for n in range(PAGES)]
+        def next_hidden(chunk):
+            hidden_half(chunk, 0)
+            hidden_half(chunk, 1)
+            quantise_h(chunk)
+
+        sums = [output_sums(0, 0, bank_a, 0), output_sums(0, 1, bank_c, 0)]
+        sums = sums + [output_sums(0, n, bank_b, n % 2) for n in (2, 3)]
+        for n in range(3):
+            by_vector(0, n, sums[n], take(256))
+        next_hidden(1)
+        by_vector(0, 3, sums[3], held_place(0, 3))
+        sums = [output_sums(1, 0, bank_c, 0), output_sums(1, 1, bank_a, 0)]
+        sums = sums + [output_sums(1, n, bank_b, n % 2) for n in (2, 3)]
+        by_vector(1, 0, sums[0], take(256))
+        by_gpsimd(1, 1, sums[1], take(256))
+        next_hidden(2)
+        for n in (2, 3):
+            by_vector(1, n, sums[n], held_place(1, n))
+        sums = [output_sums(2, n, bank_c, n) for n in range(2)] + [output_sums(2, 2, bank_a, 0)]
         for n in range(2):
-            fused(last, n, sums[n], staged[n])
+            by_gpsimd(2, n, sums[n], take(256))
+        next_hidden(3)
+        by_vector(2, 2, sums[2], held_place(2, 3))
+        staged = [spare[1][:, n * 256 : (n + 1) * 256] for n in range(PAGES)]
+        sums = [output_sums(3, n, bank_b, n) for n in range(2)]
+        for n in range(2):
+            fused(3, n, sums[n], staged[n])
             store(n)
-        bank = vector_banks[last % 2]
-        sums = [output_sums(last, 2, bank, 0), output_sums(last - 1, 3, bank, 1)]
-        fused(last, 2, sums[0], staged[2])
+        sums = [output_sums(3, 2, bank_c, 0), output_sums(2, 3, bank_c, 1)]
+        fused(3, 2, sums[0], staged[2])
         store(2)
-        fused(last - 1, 3, sums[1], staged[1])
-        fused(last, 3, output_sums(last, 3, scalar_bank, 0), staged[3])
+        fused(2, 3, sums[1], staged[1])
+        fused(3, 3, output_sums(3, 3, bank_a, 0), staged[3])
         store(3)

@@ -62,7 +62,7 @@ def tile_list_tanh_mix_scatb_kernel(
         wd8_sc = keep.tile([P, N], U8, name="wd8_sc", align_bytes=64)
         wd4_sc = keep.tile([P, N], U8, name="wd4_sc", align_bytes=64)
         x_codes = [keep.tile([P, J], I32, name=f"x_codes{a}", align_bytes=64) for a in range(2)]
-        x_sc = keep.tile([P, J], U8, name="x_sc", align_bytes=64)
+        x_sc = [keep.tile([P, J], U8, name=f"x_sc{a}", align_bytes=64) for a in range(2)]
         wu_codes = [keep.tile([P, R], I32, name=f"wu_codes{a}", align_bytes=64) for a in range(2)]
         wu_sc = [keep.tile([P, R], U8, name=f"wu_sc{a}", align_bytes=64) for a in range(2)]
         h_sc_tiles = [keep.tile([P, J], U8, name=f"h_sc{c}", align_bytes=64) for c in range(2)]
@@ -82,12 +82,11 @@ def tile_list_tanh_mix_scatb_kernel(
 
         def x_rounded(a, lo, hi):
             if a == 1 and lo == 0:
+                return picked[1, HALF][:, 3 * HALF : 4 * HALF].bitcast(BF16)
+            if a == 1 and lo < HALF:
                 return late_rounded[:, PACK * lo : PACK * hi]
-            if a == 1 and hi < J:
-                first = (lo // 256 - 1) * R + PASS
-                return wu_raw[1][:, first : first + PASS].bitcast(BF16)
             if a == 1:
-                return rounded[3][:, 0 : PACK * 256]
+                return picked[1, 0][:, PASS : 3 * PASS].bitcast(BF16)[:, PACK * (lo - HALF) : PACK * (hi - HALF)]
             c, first = divmod(lo, HALF)
             return rounded[c][:, PACK * first : PACK * (first + hi - lo)]
 
@@ -106,9 +105,12 @@ def tile_list_tanh_mix_scatb_kernel(
         def load_x(a, i):
             nc.sync.dma_start(out=planes[a][i][:], in_=x_rows[a, i])
 
-        def load_wu(a, half):
-            rows = wu[a * PASS : (a + 1) * PASS, :].rearrange("(p h i) r -> h p (i r)", h=2, i=2)
-            nc.sync.dma_start(out=wu_raw[a][:, half * 2 * R : (half + 1) * 2 * R], in_=rows[half])
+        def load_wu(a, s):
+            cols = slice(s * PASS, (s + 1) * PASS)
+            nc.sync.dma_start(
+                out=wu_raw[a][:].rearrange("p (i r) -> p i r", i=PACK)[:, :, cols],
+                in_=wu[a * PASS : (a + 1) * PASS, cols].rearrange("(p i) r -> p i r", i=PACK),
+            )
 
         def load_wg(a):
             nc.sync.dma_start(out=wg_raw[a][:], in_=wg_words[a].rearrange("p r i -> p (r i)").bitcast(I32))
@@ -144,10 +146,10 @@ def tile_list_tanh_mix_scatb_kernel(
         load_wu(0, 1)
         load_x(1, 1)
         load_x(1, 2)
-        load_x(1, 3)
         load_wu(1, 0)
-        load_wu(1, 1)
+        load_x(1, 3)
         load_wg(0)
+        load_wu(1, 1)
         load_wg(1)
         nc.sync.dma_start(out=wd8_codes[:], in_=wd8_words[0].rearrange("p n i -> p (n i)").bitcast(I32))
         nc.sync.dma_start(out=wd4_codes[:].bitcast(I32), in_=wd4_words[0].bitcast(I32))
@@ -178,7 +180,7 @@ def tile_list_tanh_mix_scatb_kernel(
 
         def quantise_x(a, lo, hi):
             nc.vector.quantize_mx(
-                out=x_codes[a][:, lo:hi].bitcast(FP8X4), scales=x_sc[4 * a :, lo:hi], in_=x_rounded(a, lo, hi)
+                out=x_codes[a][:, lo:hi].bitcast(FP8X4), scales=x_sc[a][:, lo:hi], in_=x_rounded(a, lo, hi)
             )
 
         def round_wu(a, s, copy):
@@ -218,7 +220,7 @@ def tile_list_tanh_mix_scatb_kernel(
                         lhsT=codes.bitcast(FP8X4),
                         lhsT_scale=scales,
                         rhs=x_codes[a][:, cols].bitcast(FP8X4),
-                        rhs_scale=x_sc[4 * a :, cols],
+                        rhs_scale=x_sc[a][:, cols],
                         start=(a == 0 and t == 0),
                         stop=(a == 1 and t == PACK - 1),
                     )
@@ -237,7 +239,7 @@ def tile_list_tanh_mix_scatb_kernel(
 
             slot = turn[0] // 2 % SLOTS
             ring = slice(slot * PASS, (slot + 1) * PASS)
-            gated = gated_ring[:, ring]
+            gated = (gated_ring if chunk > 0 else picked[1, 0])[:, ring]
             gate = first_products(u, wg_stationary)
             nc.scalar.activation(
                 out=gated.rearrange("p (j t) -> p j t", t=PACK), in_=gate, func=ACT.Tanh, bias=no_bias
@@ -334,23 +336,28 @@ def tile_list_tanh_mix_scatb_kernel(
         for s in range(2):
             round_wu(0, s, nc.scalar.copy)
             quantise_wu(0, s)
-        for i in range(PACK):
+        for i in range(PACK - 1):
             gather(1, i, 0, HALF)
             gather(1, i, HALF, J)
-        round_wu(1, 0, nc.vector.tensor_copy)
-        round_wu(1, 1, nc.scalar.copy)
-        deal_wg_words(0)
+        round_wu(1, 0, nc.scalar.copy)
         quantise_wu(1, 0)
+        gather(1, 3, 0, 256)
+        round_x(1, 0, 256)
+        gather(1, 3, 256, HALF)
+        round_wu(1, 1, nc.scalar.copy)
+        quantise_x(1, 0, 256)
+        deal_wg_words(0)
+        gather(1, 3, HALF, J)
+        round_x(1, 256, HALF)
+        quantise_x(1, 256, HALF)
         deal_wg_words(1)
         quantise_wu(1, 1)
-        for lo in range(0, 768, 256):
-            round_x(1, lo, lo + 256)
-            quantise_x(1, lo, lo + 256)
-        round_x(1, 768, J, nc.vector.tensor_copy)
-        quantise_x(1, 768, J)
         hidden_half(0, 0)
         hidden_half(0, 1)
         quantise_h(0)
+        round_x(1, HALF, 768)
+        round_x(1, 768, J)
+        quantise_x(1, HALF, J)
 
         def next_hidden(chunk):
             hidden_half(chunk, 0)

@@ -48,7 +48,7 @@ def tile_list_tanh_mix_scatb_kernel(
             for a in range(2)
             for lo, hi in pieces[a]
         }
-        wu_raw = [keep.tile([P, PACK * R], F32, name=f"wu_raw{a}") for a in range(2)]
+        wu_raw = {(a, s): keep.tile([P, PACK * PASS], F32, name=f"wu_raw{a}{s}") for a in range(2) for s in range(2)}
         wgt_sb = keep.tile([P, J], F32, name="wgt_sb")
         wgo_sb = keep.tile([P, J], F32, name="wgo_sb")
         bias = keep.tile([P, PAGES], F32, name="bias")
@@ -70,7 +70,7 @@ def tile_list_tanh_mix_scatb_kernel(
 
         late_rounded = picked[0, 0][:].bitcast(BF16)
         wu_rounded = {(0, 0): rounded[2], (0, 1): rounded[3], (1, 0): rounded[2], (1, 1): rounded[3]}
-        gated_ring, moved_ring = wu_raw[0][:, 0 : 2 * R], wu_raw[0][:, 2 * R : 4 * R]
+        gated_ring, moved_ring = wu_raw[0, 0], wu_raw[0, 1]
         spare = [picked[0, HALF], picked[1, 0]]
         taken = [0]
         turn = [0]
@@ -108,7 +108,7 @@ def tile_list_tanh_mix_scatb_kernel(
         def load_wu(a, s):
             cols = slice(s * PASS, (s + 1) * PASS)
             nc.sync.dma_start(
-                out=wu_raw[a][:].rearrange("p (i r) -> p i r", i=PACK)[:, :, cols],
+                out=wu_raw[a, s][:].rearrange("p (i r) -> p i r", i=PACK),
                 in_=wu[a * PASS : (a + 1) * PASS, cols].rearrange("(p i) r -> p i r", i=PACK),
             )
 
@@ -184,10 +184,9 @@ def tile_list_tanh_mix_scatb_kernel(
             )
 
         def round_wu(a, s, copy):
-            rows = wu_raw[a][:].rearrange("p (i r) -> p i r", i=PACK)[:, :, s * PASS : (s + 1) * PASS]
             copy(
                 out=wu_rounded[a, s][:].rearrange("p (t q i) -> p q i t", t=PACK, i=PACK),
-                in_=rows.rearrange("p i (q t) -> p q i t", t=PACK),
+                in_=wu_raw[a, s][:].rearrange("p (i q t) -> p q i t", i=PACK, t=PACK),
             )
 
         def quantise_wu(a, s):

@@ -1,6 +1,7 @@
 from contextlib import ExitStack
 
 import concourse.mybir as mybir
+from concourse.masks import make_identity
 
 K, R, N, T, J = 1024, 1024, 512, 2048, 1024
 FLOPS = 2 * J * (2 * K * R + R * N)
@@ -25,6 +26,7 @@ UNIT = 128
 PAGES = N // P
 CHUNKS = [(0, 256), (256, 512), (512, 768), (768, 1024)]
 SLOTS = 4
+RUN = 64
 SUM_BANKS = 5
 
 
@@ -49,8 +51,10 @@ def tile_list_tanh_mix_scatb_kernel(
             for lo, hi in pieces[a]
         }
         wu_raw = {(a, s): keep.tile([P, PACK * PASS], F32, name=f"wu_raw{a}{s}") for a in range(2) for s in range(2)}
-        wgt_sb = keep.tile([P, J], F32, name="wgt_sb")
-        wgo_sb = keep.tile([P, J], F32, name="wgo_sb")
+        weights = keep.tile([P, 2 * J], F32, name="weights")
+        wgt_sb, wgo_sb = weights[:, 0:J], weights[:, J : 2 * J]
+        packed = keep.tile([P, P], F32, name="packed")
+        identity = keep.tile([P, P], F32, name="identity")
         bias = keep.tile([P, PAGES], F32, name="bias")
         zeros = keep.tile([P, 8], F32, name="zeros")
         wg_raw = [keep.tile([P, 2 * PASS], I32, name=f"wg_raw{s}", align_bytes=64) for s in range(2)]
@@ -64,7 +68,8 @@ def tile_list_tanh_mix_scatb_kernel(
         x_codes = [keep.tile([P, J], I32, name=f"x_codes{a}", align_bytes=64) for a in range(2)]
         x_sc = [keep.tile([P, J], U8, name=f"x_sc{a}", align_bytes=64) for a in range(2)]
         wu_codes = [keep.tile([P, R], I32, name=f"wu_codes{a}", align_bytes=64) for a in range(2)]
-        wu_sc = [keep.tile([P, R], U8, name=f"wu_sc{a}", align_bytes=64) for a in range(2)]
+        wu_sc_tiles = [keep.tile([P, PASS], U8, name=f"wu_sc{v}", align_bytes=64) for v in range(3)]
+        wu_sc = {(0, 0): wu_sc_tiles[0][:], (1, 0): wu_sc_tiles[0][4:, :], (0, 1): wu_sc_tiles[1][:], (1, 1): wu_sc_tiles[2][:]}
         h_sc_tiles = [keep.tile([P, J], U8, name=f"h_sc{c}", align_bytes=64) for c in range(2)]
         rounded = [keep.tile([P, PACK * HALF], BF16, name=f"rounded{v}", align_bytes=64) for v in range(4)]
 
@@ -82,7 +87,7 @@ def tile_list_tanh_mix_scatb_kernel(
 
         def x_rounded(a, lo, hi):
             if a == 1 and lo == 0:
-                return picked[1, HALF][:, 3 * HALF : 4 * HALF].bitcast(BF16)
+                return late_rounded[:, 0 : PACK * hi]
             if a == 1 and lo < HALF:
                 return late_rounded[:, PACK * lo : PACK * hi]
             if a == 1:
@@ -112,8 +117,9 @@ def tile_list_tanh_mix_scatb_kernel(
                 in_=wu[a * PASS : (a + 1) * PASS, cols].rearrange("(p i) r -> p i r", i=PACK),
             )
 
-        def load_wg(a):
-            nc.sync.dma_start(out=wg_raw[a][:], in_=wg_words[a].rearrange("p r i -> p (r i)").bitcast(I32))
+        def load_wg(a, lo, hi):
+            words = wg_words[a, :, lo:hi, :].rearrange("p r i -> p (r i)")
+            nc.sync.dma_start(out=wg_raw[a][:, lo:hi], in_=words.bitcast(I32))
 
         def load_scale_rows(queue, tile, rows):
             passes = rows.shape[0]
@@ -123,6 +129,7 @@ def tile_list_tanh_mix_scatb_kernel(
                     in_=rows[:, 4 * q : 4 * q + 4, :].bitcast(I32),
                 )
 
+        make_identity(nc, identity[:])
         nc.gpsimd.memset(wg_sc_raw[:].bitcast(I32), 0)
         nc.gpsimd.memset(zeros[:], 0.0)
         nc.scalar.activation(out=zeros[:, 4:8], in_=zeros[:, 0:4], func=ACT.Tanh)
@@ -134,9 +141,12 @@ def tile_list_tanh_mix_scatb_kernel(
         load_scale_rows(nc.gpsimd, wd8_sc, wd8_scales)
         load_scale_rows(nc.gpsimd, wd4_sc, wd4_scales)
 
+        for w, rows in enumerate((wgt, wgo)):
+            nc.sync.dma_start(
+                out=packed[:, w * RUN : (w + 1) * RUN], in_=rows[0:P:GROUP, :].rearrange("g (b c) -> g b c", c=RUN)
+            )
         nc.sync.dma_start(pick_list[:], offs)
         load_x(0, 0)
-        nc.sync.dma_start(out=wgt_sb[:], in_=wgt)
         load_x(0, 1)
         load_x(0, 2)
         load_scale_rows(nc.sync, wg_sc_raw, wg_scales)
@@ -147,16 +157,37 @@ def tile_list_tanh_mix_scatb_kernel(
         load_x(1, 1)
         load_x(1, 2)
         load_wu(1, 0)
+        load_wg(0, 0, R)
         load_x(1, 3)
-        load_wg(0)
+        load_wg(1, 0, PASS)
         load_wu(1, 1)
-        load_wg(1)
+        load_wg(1, PASS, R)
         nc.sync.dma_start(out=wd8_codes[:], in_=wd8_words[0].rearrange("p n i -> p (n i)").bitcast(I32))
         nc.sync.dma_start(out=wd4_codes[:].bitcast(I32), in_=wd4_words[0].bitcast(I32))
         with nc.allow_non_contiguous_dma(reason="one bias value for each partition and page"):
             nc.sync.dma_start(out=bias[:], in_=b.rearrange("(n p) -> p n", p=P))
         nc.sync.dma_start(place_list[:], offs2)
-        nc.sync.dma_start(out=wgo_sb[:], in_=wgo)
+
+        def spread_weights():
+            repeated = picked[1, 0][:]
+            copies = [nc.scalar.copy, nc.vector.tensor_copy, nc.scalar.copy, nc.scalar.copy]
+            for v in range(2):
+                nc.tensor.transpose(banks[v][:, 0:P], packed[:], identity[:])
+            for v in range(4):
+                by_run = banks[int(v == 1)][:, 0:P].rearrange("p (g b) -> p b g", b=GROUP)
+                copies[v](
+                    out=repeated[:, v * PASS : (v + 1) * PASS].rearrange("p (b g r) -> p b g r", g=8, r=GROUP),
+                    in_=by_run[:, 4 * v : 4 * v + 4, :].unsqueeze(3).to_broadcast([P, 4, 8, GROUP]),
+                )
+                for k in range(4):
+                    run = repeated[:, (4 * v + k) * P : (4 * v + k + 1) * P]
+                    nc.tensor.transpose(banks[2 + v][:, k * P : (k + 1) * P], run, identity[:])
+            for w, rows in enumerate((wgt_sb, wgo_sb)):
+                for v in range(4):
+                    (copies[v] if w == 0 else nc.scalar.copy)(
+                        out=rows[:, v * 256 : (v + 1) * 256].rearrange("p (k c) -> p k c", c=RUN),
+                        in_=banks[2 + v][:].rearrange("p (k w c) -> p w k c", k=4, w=2)[:, w],
+                    )
 
         def piece(a, lo):
             start, stop = [part for part in pieces[a] if part[0] <= lo][-1]
@@ -183,22 +214,22 @@ def tile_list_tanh_mix_scatb_kernel(
                 out=x_codes[a][:, lo:hi].bitcast(FP8X4), scales=x_sc[a][:, lo:hi], in_=x_rounded(a, lo, hi)
             )
 
-        def round_wu(a, s, copy):
+        def round_wu(a, s, copy, first=0, last=PACK):
             copy(
-                out=wu_rounded[a, s][:].rearrange("p (t q i) -> p q i t", t=PACK, i=PACK),
-                in_=wu_raw[a, s][:].rearrange("p (i q t) -> p q i t", i=PACK, t=PACK),
+                out=wu_rounded[a, s][:, first * PASS : last * PASS].rearrange("p (t q i) -> p q i t", q=P, i=PACK),
+                in_=wu_raw[a, s][:].rearrange("p (i q t) -> p q i t", i=PACK, t=PACK)[:, :, :, first:last],
             )
 
         def quantise_wu(a, s):
             cols = slice(s * PASS, (s + 1) * PASS)
             nc.vector.quantize_mx(
-                out=wu_codes[a][:, cols].bitcast(FP8X4), scales=wu_sc[a][:, cols], in_=wu_rounded[a, s][:]
+                out=wu_codes[a][:, cols].bitcast(FP8X4), scales=wu_sc[a, s], in_=wu_rounded[a, s][:]
             )
 
-        def deal_wg_words(a):
+        def deal_wg_words(a, lo, hi):
             nc.vector.tensor_copy(
-                out=wg_codes[a][:].rearrange("p (s t q) -> p s q t", t=PACK, q=P),
-                in_=wg_raw[a][:].rearrange("p (s q t) -> p s q t", t=PACK, q=P),
+                out=wg_codes[a][:, lo:hi].rearrange("p (s t q) -> p s q t", t=PACK, q=P),
+                in_=wg_raw[a][:, lo:hi].rearrange("p (s q t) -> p s q t", t=PACK, q=P),
             )
 
         def deal_wg_scales():
@@ -234,7 +265,7 @@ def tile_list_tanh_mix_scatb_kernel(
 
             def wu_stationary(a, t):
                 first = s * PASS + t * P
-                return wu_codes[a][:, first : first + P], wu_sc[a][:, first : first + P]
+                return wu_codes[a][:, first : first + P], wu_sc[a, s][:, t * P : (t + 1) * P]
 
             slot = turn[0] // 2 % SLOTS
             ring = slice(slot * PASS, (slot + 1) * PASS)
@@ -299,10 +330,13 @@ def tile_list_tanh_mix_scatb_kernel(
             lo, hi = CHUNKS[chunk]
             return pages[n][:].indirect(place_list[:, lo // GROUP : hi // GROUP])
 
-        def by_vector(chunk, n, acc, staged):
+        def weigh(chunk, n, acc, staged):
             lo, hi = CHUNKS[chunk]
             nc.vector.scalar_tensor_tensor(staged, acc, bias[:, n : n + 1], wgo_sb[:, lo:hi], ADD, MULT)
-            nc.vector.tensor_copy(places(chunk, n), staged)
+            return staged
+
+        def by_vector(chunk, n, acc, staged):
+            nc.vector.tensor_copy(places(chunk, n), weigh(chunk, n, acc, staged))
 
         def by_gpsimd(chunk, n, acc, staged):
             lo, hi = CHUNKS[chunk]
@@ -324,6 +358,7 @@ def tile_list_tanh_mix_scatb_kernel(
         def store(n):
             nc.sync.dma_start(out=out[n * P : (n + 1) * P, :], in_=pages[n][:])
 
+        spread_weights()
         for i in range(PACK):
             gather(0, i, 0, HALF)
             gather(0, i, HALF, J)
@@ -340,23 +375,24 @@ def tile_list_tanh_mix_scatb_kernel(
             gather(1, i, HALF, J)
         round_wu(1, 0, nc.scalar.copy)
         quantise_wu(1, 0)
+        deal_wg_words(0, 0, R)
         gather(1, 3, 0, 256)
         round_x(1, 0, 256)
         gather(1, 3, 256, HALF)
-        round_wu(1, 1, nc.scalar.copy)
-        quantise_x(1, 0, 256)
-        deal_wg_words(0)
         gather(1, 3, HALF, J)
+        round_wu(1, 1, nc.scalar.copy, 0, 2)
+        round_wu(1, 1, nc.vector.tensor_copy, 2, 4)
+        quantise_x(1, 0, 256)
+        deal_wg_words(1, 0, PASS)
         round_x(1, 256, HALF)
         quantise_x(1, 256, HALF)
-        deal_wg_words(1)
+        deal_wg_words(1, PASS, R)
         quantise_wu(1, 1)
         hidden_half(0, 0)
         hidden_half(0, 1)
         quantise_h(0)
         round_x(1, HALF, 768)
-        round_x(1, 768, J)
-        quantise_x(1, HALF, J)
+        quantise_x(1, HALF, 768)
 
         def next_hidden(chunk):
             hidden_half(chunk, 0)
@@ -365,20 +401,25 @@ def tile_list_tanh_mix_scatb_kernel(
 
         sums = [output_sums(0, 0, bank_a, 0), output_sums(0, 1, bank_c, 0)]
         sums = sums + [output_sums(0, n, bank_b, n % 2) for n in (2, 3)]
+        weighted = [weigh(0, n, sums[n], take(256)) for n in range(3)]
         for n in range(3):
-            by_vector(0, n, sums[n], take(256))
-        next_hidden(1)
+            nc.vector.tensor_copy(places(0, n), weighted[n])
+        hidden_half(1, 0)
+        hidden_half(1, 1)
+        round_x(1, 768, J)
+        quantise_x(1, 768, J)
+        quantise_h(1)
         by_vector(0, 3, sums[3], held_place(0, 3))
-        sums = [output_sums(1, 0, bank_c, 0), output_sums(1, 1, bank_a, 0)]
-        sums = sums + [output_sums(1, n, bank_b, n % 2) for n in (2, 3)]
+        sums = [output_sums(1, 0, bank_c, 0), output_sums(1, 1, bank_a, 0), output_sums(1, 2, bank_a, 1)]
+        sums = sums + [output_sums(1, 3, bank_b, 0)]
         by_vector(1, 0, sums[0], take(256))
-        by_gpsimd(1, 1, sums[1], take(256))
+        for n in (1, 2):
+            by_gpsimd(1, n, sums[n], take(256))
         next_hidden(2)
-        for n in (2, 3):
-            by_vector(1, n, sums[n], held_place(1, n))
+        by_vector(1, 3, sums[3], held_place(1, 3))
         sums = [output_sums(2, n, bank_c, n) for n in range(2)] + [output_sums(2, 2, bank_a, 0)]
         for n in range(2):
-            by_gpsimd(2, n, sums[n], take(256))
+            by_vector(2, n, sums[n], take(256))
         next_hidden(3)
         by_vector(2, 2, sums[2], held_place(2, 3))
         staged = [spare[1][:, n * 256 : (n + 1) * 256] for n in range(PAGES)]

@@ -132,7 +132,6 @@ def tile_list_tanh_mix_scatb_kernel(
         make_identity(nc, identity[:])
         nc.gpsimd.memset(wg_sc_raw[:].bitcast(I32), 0)
         nc.gpsimd.memset(zeros[:], 0.0)
-        nc.scalar.activation(out=zeros[:, 4:8], in_=zeros[:, 0:4], func=ACT.Tanh)
         no_bias = zeros[:, 4:5]
         for page in pages:
             nc.gpsimd.memset(page[:], 0.0)

@@ -420,15 +420,14 @@ def tile_list_tanh_mix_scatb_kernel(
         for n in range(2):
             by_vector(2, n, sums[n], take(256))
         next_hidden(3)
-        by_vector(2, 2, sums[2], held_place(2, 3))
+        fused(2, 2, sums[2], moved_ring[:, 3 * PASS : 3 * PASS + 256])
         staged = [spare[1][:, n * 256 : (n + 1) * 256] for n in range(PAGES)]
-        sums = [output_sums(3, n, bank_b, n) for n in range(2)]
-        for n in range(2):
-            fused(3, n, sums[n], staged[n])
+        for n, bank in enumerate((bank_b, banks[0])):
+            fused(3, n, output_sums(3, n, bank, 0), staged[n])
             store(n)
         sums = [output_sums(3, 2, bank_c, 0), output_sums(2, 3, bank_c, 1)]
         fused(3, 2, sums[0], staged[2])
         store(2)
         fused(2, 3, sums[1], staged[1])
-        fused(3, 3, output_sums(3, 3, bank_a, 0), staged[3])
+        fused(3, 3, output_sums(3, 3, banks[1], 0), staged[3])
         store(3)

@@ -276,7 +276,7 @@ def tile_list_tanh_mix_scatb_kernel(
             up = first_products(u, wu_stationary)
             first = PACK * (s * (hi - lo) + u * UNIT - lo)
             product = h_rounded(chunk)[:, first : first + PACK * UNIT]
-            if chunk == 0:
+            if chunk == 0 or (chunk, s, u) == (1, 1, 3):
                 nc.vector.tensor_tensor(
                     product.rearrange("p (j t) -> p j t", t=PACK),
                     up,
@@ -391,7 +391,8 @@ def tile_list_tanh_mix_scatb_kernel(
         hidden_half(0, 1)
         quantise_h(0)
         round_x(1, HALF, 768)
-        quantise_x(1, HALF, 768)
+        round_x(1, 768, J)
+        quantise_x(1, HALF, J)
 
         def next_hidden(chunk):
             hidden_half(chunk, 0)
@@ -400,25 +401,21 @@ def tile_list_tanh_mix_scatb_kernel(
 
         sums = [output_sums(0, 0, bank_a, 0), output_sums(0, 1, bank_c, 0)]
         sums = sums + [output_sums(0, n, bank_b, n % 2) for n in (2, 3)]
-        weighted = [weigh(0, n, sums[n], take(256)) for n in range(3)]
-        for n in range(3):
+        weighted = [weigh(0, n, sums[n], take(256)) for n in range(2)]
+        for n in range(2):
             nc.vector.tensor_copy(places(0, n), weighted[n])
-        hidden_half(1, 0)
-        hidden_half(1, 1)
-        round_x(1, 768, J)
-        quantise_x(1, 768, J)
-        quantise_h(1)
-        by_vector(0, 3, sums[3], held_place(0, 3))
-        sums = [output_sums(1, 0, bank_c, 0), output_sums(1, 1, bank_a, 0), output_sums(1, 2, bank_a, 1)]
-        sums = sums + [output_sums(1, 3, bank_b, 0)]
-        by_vector(1, 0, sums[0], take(256))
-        for n in (1, 2):
+        next_hidden(1)
+        for n in (2, 3):
+            by_vector(0, n, sums[n], held_place(0, n))
+        sums = [output_sums(1, n, (bank_c, bank_b)[n // 2], n % 2) for n in range(PAGES)]
+        for n in range(2):
             by_gpsimd(1, n, sums[n], take(256))
         next_hidden(2)
-        by_vector(1, 3, sums[3], held_place(1, 3))
+        for n in (2, 3):
+            by_vector(1, n, sums[n], held_place(1, n))
         sums = [output_sums(2, n, bank_c, n) for n in range(2)] + [output_sums(2, 2, bank_a, 0)]
         for n in range(2):
-            by_vector(2, n, sums[n], take(256))
+            by_gpsimd(2, n, sums[n], take(256))
         next_hidden(3)
         fused(2, 2, sums[2], moved_ring[:, 3 * PASS : 3 * PASS + 256])
         staged = [spare[1][:, n * 256 : (n + 1) * 256] for n in range(PAGES)]

@@ -21,13 +21,16 @@ P = 128
 PACK = 4
 PASS = P * PACK
 GROUP = 16
+GROUPS = P // GROUP
 HALF = J // 2
 UNIT = 128
 PAGES = N // P
-CHUNKS = [(0, 256), (256, 512), (512, 768), (768, 1024)]
-SLOTS = 4
-RUN = 64
+CHUNK = 2 * UNIT
+BANKS = 8
 SUM_BANKS = 5
+SLOTS = 4
+RUN = J // GROUP
+SCALE_SHIFT = 4
 
 
 def tile_list_tanh_mix_scatb_kernel(
@@ -37,18 +40,17 @@ def tile_list_tanh_mix_scatb_kernel(
     with ExitStack() as ctx:
         keep = ctx.enter_context(tc.tile_pool(name="keep", bufs=1))
         psum = ctx.enter_context(tc.psum_pool(name="psum", bufs=1))
-        banks = [psum.tile([P, PASS], F32, name=f"bank{v}") for v in range(8)]
+        banks = [psum.tile([P, PASS], F32, name=f"bank{v}") for v in range(BANKS)]
         bank_a, bank_b, bank_c = banks[SUM_BANKS:]
 
         pick_list = keep.tile([P, J // GROUP], U16, name="pick_list")
         place_list = keep.tile([P, J // GROUP], U16, name="place_list")
         planes = [[keep.tile([P, T], F32, name=f"x{a}{i}") for i in range(PACK)] for a in range(2)]
         pages = [keep.tile([P, T], F32, name=f"page{n}") for n in range(PAGES)]
-        pieces = [[(0, HALF), (HALF, J)]] * 2
         picked = {
-            (a, lo): keep.tile([P, PACK * (hi - lo)], F32, name=f"picked{a}_{lo}", align_bytes=64)
+            (a, start): keep.tile([P, PACK * HALF], F32, name=f"picked{a}_{start}", align_bytes=64)
             for a in range(2)
-            for lo, hi in pieces[a]
+            for start in (0, HALF)
         }
         wu_raw = {(a, s): keep.tile([P, PACK * PASS], F32, name=f"wu_raw{a}{s}") for a in range(2) for s in range(2)}
         weights = keep.tile([P, 2 * J], F32, name="weights")
@@ -56,9 +58,9 @@ def tile_list_tanh_mix_scatb_kernel(
         packed = keep.tile([P, P], F32, name="packed")
         identity = keep.tile([P, P], F32, name="identity")
         bias = keep.tile([P, PAGES], F32, name="bias")
-        zeros = keep.tile([P, 8], F32, name="zeros")
-        wg_raw = [keep.tile([P, 2 * PASS], I32, name=f"wg_raw{s}", align_bytes=64) for s in range(2)]
-        wg_codes = [keep.tile([P, 2 * PASS], I32, name=f"wg_codes{s}", align_bytes=64) for s in range(2)]
+        no_bias = keep.tile([P, 1], F32, name="no_bias")
+        wg_raw = [keep.tile([P, R], I32, name=f"wg_raw{a}", align_bytes=64) for a in range(2)]
+        wg_codes = [keep.tile([P, R], I32, name=f"wg_codes{a}", align_bytes=64) for a in range(2)]
         wg_sc_raw = keep.tile([P, R], U8, name="wg_sc_raw", align_bytes=64)
         wg_sc = keep.tile([P, R], U8, name="wg_sc", align_bytes=64)
         wd8_codes = keep.tile([P, N], I32, name="wd8_codes", align_bytes=64)
@@ -69,41 +71,41 @@ def tile_list_tanh_mix_scatb_kernel(
         x_sc = [keep.tile([P, J], U8, name=f"x_sc{a}", align_bytes=64) for a in range(2)]
         wu_codes = [keep.tile([P, R], I32, name=f"wu_codes{a}", align_bytes=64) for a in range(2)]
         wu_sc_tiles = [keep.tile([P, PASS], U8, name=f"wu_sc{v}", align_bytes=64) for v in range(3)]
-        wu_sc = {(0, 0): wu_sc_tiles[0][:], (1, 0): wu_sc_tiles[0][4:, :], (0, 1): wu_sc_tiles[1][:], (1, 1): wu_sc_tiles[2][:]}
         h_sc_tiles = [keep.tile([P, J], U8, name=f"h_sc{c}", align_bytes=64) for c in range(2)]
         rounded = [keep.tile([P, PACK * HALF], BF16, name=f"rounded{v}", align_bytes=64) for v in range(4)]
 
-        late_rounded = picked[0, 0][:].bitcast(BF16)
-        wu_rounded = {(0, 0): rounded[2], (0, 1): rounded[3], (1, 0): rounded[2], (1, 1): rounded[3]}
-        gated_ring, moved_ring = wu_raw[0, 0], wu_raw[0, 1]
-        spare = [picked[0, HALF], picked[1, 0]]
-        taken = [0]
-        turn = [0]
+        wu_sc = {
+            (0, 0): wu_sc_tiles[0][:],
+            (1, 0): wu_sc_tiles[0][SCALE_SHIFT:, :],
+            (0, 1): wu_sc_tiles[1][:],
+            (1, 1): wu_sc_tiles[2][:],
+        }
 
-        def take(width):
-            v, first = divmod(taken[0], PACK * HALF)
-            taken.insert(0, taken[0] + width)
-            return spare[v][:, first : first + width]
+        repeated = picked[1, 0]
+        first_gated = picked[1, 0]
+        last_staged = picked[1, 0]
+        early_staged = picked[0, HALF]
+        gated_slots, moved_slots = wu_raw[0, 0], wu_raw[0, 1]
+
+        def wu_rounded(s):
+            return rounded[2 + s]
 
         def x_rounded(a, lo, hi):
-            if a == 1 and lo == 0:
-                return late_rounded[:, 0 : PACK * hi]
-            if a == 1 and lo < HALF:
-                return late_rounded[:, PACK * lo : PACK * hi]
-            if a == 1:
-                return picked[1, 0][:, PASS : 3 * PASS].bitcast(BF16)[:, PACK * (lo - HALF) : PACK * (hi - HALF)]
-            c, first = divmod(lo, HALF)
-            return rounded[c][:, PACK * first : PACK * (first + hi - lo)]
+            start = lo // HALF * HALF
+            if a == 0:
+                tile = rounded[lo // HALF][:]
+            elif lo < HALF:
+                tile = picked[0, 0][:].bitcast(BF16)
+            else:
+                tile = first_gated[:, PASS : 3 * PASS].bitcast(BF16)
+            return tile[:, PACK * (lo - start) : PACK * (hi - start)]
 
         def h_rounded(chunk):
-            lo, hi = CHUNKS[chunk]
-            return rounded[min(chunk, 1)][:, 0 : 2 * PACK * (hi - lo)]
+            return rounded[min(chunk, 1)][:]
 
         def h_codes(chunk):
-            lo, hi = CHUNKS[chunk]
-            c, first = divmod(lo, HALF)
-            cols = slice(2 * first, 2 * (first + hi - lo))
-            return wg_raw[c][:, cols], h_sc_tiles[c][:, cols]
+            cols = slice(chunk % 2 * 2 * CHUNK, (chunk % 2 + 1) * 2 * CHUNK)
+            return wg_raw[chunk // 2][:, cols], h_sc_tiles[chunk // 2][:, cols]
 
         x_rows = xT.rearrange("(a p i) t -> a i p t", a=2, i=PACK)
 
@@ -131,8 +133,7 @@ def tile_list_tanh_mix_scatb_kernel(
 
         make_identity(nc, identity[:])
         nc.gpsimd.memset(wg_sc_raw[:].bitcast(I32), 0)
-        nc.gpsimd.memset(zeros[:], 0.0)
-        no_bias = zeros[:, 4:5]
+        nc.gpsimd.memset(no_bias[:], 0.0)
         for page in pages:
             nc.gpsimd.memset(page[:], 0.0)
         for tile in (wd8_sc, wd4_sc):
@@ -168,15 +169,14 @@ def tile_list_tanh_mix_scatb_kernel(
         nc.sync.dma_start(place_list[:], offs2)
 
         def spread_weights():
-            repeated = picked[1, 0][:]
             copies = [nc.scalar.copy, nc.vector.tensor_copy, nc.scalar.copy, nc.scalar.copy]
             for v in range(2):
                 nc.tensor.transpose(banks[v][:, 0:P], packed[:], identity[:])
             for v in range(4):
                 by_run = banks[int(v == 1)][:, 0:P].rearrange("p (g b) -> p b g", b=GROUP)
                 copies[v](
-                    out=repeated[:, v * PASS : (v + 1) * PASS].rearrange("p (b g r) -> p b g r", g=8, r=GROUP),
-                    in_=by_run[:, 4 * v : 4 * v + 4, :].unsqueeze(3).to_broadcast([P, 4, 8, GROUP]),
+                    out=repeated[:, v * PASS : (v + 1) * PASS].rearrange("p (b g r) -> p b g r", g=GROUPS, r=GROUP),
+                    in_=by_run[:, 4 * v : 4 * v + 4, :].unsqueeze(3).to_broadcast([P, 4, GROUPS, GROUP]),
                 )
                 for k in range(4):
                     run = repeated[:, (4 * v + k) * P : (4 * v + k + 1) * P]
@@ -184,28 +184,26 @@ def tile_list_tanh_mix_scatb_kernel(
             for w, rows in enumerate((wgt_sb, wgo_sb)):
                 for v in range(4):
                     (copies[v] if w == 0 else nc.scalar.copy)(
-                        out=rows[:, v * 256 : (v + 1) * 256].rearrange("p (k c) -> p k c", c=RUN),
+                        out=rows[:, v * 4 * RUN : (v + 1) * 4 * RUN].rearrange("p (k c) -> p k c", c=RUN),
                         in_=banks[2 + v][:].rearrange("p (k w c) -> p w k c", k=4, w=2)[:, w],
                     )
 
-        def piece(a, lo):
-            start, stop = [part for part in pieces[a] if part[0] <= lo][-1]
-            return picked[a, start][:, 0 : PACK * (stop - start)].rearrange("p (i j) -> p i j", i=PACK), start
+        def picks(a, lo, hi):
+            start = lo // HALF * HALF
+            return picked[a, start][:].rearrange("p (i j) -> p i j", i=PACK)[:, :, lo - start : hi - start]
 
         def gather(a, i, lo, hi):
-            rows, start = piece(a, lo)
             nc.vector.tensor_tensor(
-                rows[:, i, lo - start : hi - start],
+                picks(a, lo, hi)[:, i, :],
                 planes[a][i][:].indirect(pick_list[:, lo // GROUP : hi // GROUP]),
                 wgt_sb[:, lo:hi],
                 MULT,
             )
 
-        def round_x(a, lo, hi, copy=nc.scalar.copy):
-            rows, start = piece(a, lo)
-            copy(
+        def round_x(a, lo, hi):
+            nc.scalar.copy(
                 out=x_rounded(a, lo, hi).rearrange("p (g e i) -> p g i e", e=4, i=PACK),
-                in_=rows[:, :, lo - start : hi - start].rearrange("p i (g e) -> p g i e", e=4),
+                in_=picks(a, lo, hi).rearrange("p i (g e) -> p g i e", e=4),
             )
 
         def quantise_x(a, lo, hi):
@@ -215,15 +213,13 @@ def tile_list_tanh_mix_scatb_kernel(
 
         def round_wu(a, s, copy, first=0, last=PACK):
             copy(
-                out=wu_rounded[a, s][:, first * PASS : last * PASS].rearrange("p (t q i) -> p q i t", q=P, i=PACK),
+                out=wu_rounded(s)[:, first * PASS : last * PASS].rearrange("p (t q i) -> p q i t", q=P, i=PACK),
                 in_=wu_raw[a, s][:].rearrange("p (i q t) -> p q i t", i=PACK, t=PACK)[:, :, :, first:last],
             )
 
         def quantise_wu(a, s):
             cols = slice(s * PASS, (s + 1) * PASS)
-            nc.vector.quantize_mx(
-                out=wu_codes[a][:, cols].bitcast(FP8X4), scales=wu_sc[a, s], in_=wu_rounded[a, s][:]
-            )
+            nc.vector.quantize_mx(out=wu_codes[a][:, cols].bitcast(FP8X4), scales=wu_sc[a, s], in_=wu_rounded(s)[:])
 
         def deal_wg_words(a, lo, hi):
             nc.vector.tensor_copy(
@@ -237,15 +233,15 @@ def tile_list_tanh_mix_scatb_kernel(
                 in_=wg_sc_raw[:].rearrange("p (s q t) -> p s t q", t=PACK, q=P),
             )
 
-        def first_products(u, stationary):
-            bank = banks[turn[0] if turn[0] < 8 else (turn[0] - 8) % SUM_BANKS][:].rearrange("p (t j) -> p t j", t=PACK)
-            turn.insert(0, turn[0] + 1)
+        def first_products(turn, u, stationary):
+            bank = banks[turn if turn < BANKS else (turn - BANKS) % SUM_BANKS]
+            by_t = bank[:].rearrange("p (t j) -> p t j", t=PACK)
             cols = slice(u * UNIT, (u + 1) * UNIT)
             for a in range(2):
                 for t in range(PACK):
                     codes, scales = stationary(a, t)
                     nc.tensor.matmul_mx(
-                        out=bank[:, t, :],
+                        out=by_t[:, t, :],
                         lhsT=codes.bitcast(FP8X4),
                         lhsT_scale=scales,
                         rhs=x_codes[a][:, cols].bitcast(FP8X4),
@@ -253,30 +249,29 @@ def tile_list_tanh_mix_scatb_kernel(
                         start=(a == 0 and t == 0),
                         stop=(a == 1 and t == PACK - 1),
                     )
-            return bank.rearrange("p t j -> p j t")
+            return by_t.rearrange("p t j -> p j t")
 
-        def hidden(chunk, s, u):
-            lo, hi = CHUNKS[chunk]
+        def hidden(chunk, quarter):
+            s, u = quarter // 2, 2 * chunk + quarter % 2
+            step = 4 * chunk + quarter
 
             def wg_stationary(a, t):
                 first = s * PASS + t * P
-                return wg_codes[a][:, first : first + P], wg_sc[4 * a :, first : first + P]
+                return wg_codes[a][:, first : first + P], wg_sc[SCALE_SHIFT * a :, first : first + P]
 
             def wu_stationary(a, t):
                 first = s * PASS + t * P
                 return wu_codes[a][:, first : first + P], wu_sc[a, s][:, t * P : (t + 1) * P]
 
-            slot = turn[0] // 2 % SLOTS
-            ring = slice(slot * PASS, (slot + 1) * PASS)
-            gated = (gated_ring if chunk > 0 else picked[1, 0])[:, ring]
-            gate = first_products(u, wg_stationary)
+            slot = slice(step % SLOTS * PASS, (step % SLOTS + 1) * PASS)
+            gated = (gated_slots if chunk > 0 else first_gated)[:, slot]
+            gate = first_products(2 * step, u, wg_stationary)
             nc.scalar.activation(
-                out=gated.rearrange("p (j t) -> p j t", t=PACK), in_=gate, func=ACT.Tanh, bias=no_bias
+                out=gated.rearrange("p (j t) -> p j t", t=PACK), in_=gate, func=ACT.Tanh, bias=no_bias[:]
             )
-            up = first_products(u, wu_stationary)
-            first = PACK * (s * (hi - lo) + u * UNIT - lo)
-            product = h_rounded(chunk)[:, first : first + PACK * UNIT]
-            if chunk == 0 or (chunk, s, u) == (1, 1, 3):
+            up = first_products(2 * step + 1, u, wu_stationary)
+            product = h_rounded(chunk)[:, quarter * PACK * UNIT : (quarter + 1) * PACK * UNIT]
+            if chunk == 0 or (chunk, quarter) == (1, 3):
                 nc.vector.tensor_tensor(
                     product.rearrange("p (j t) -> p j t", t=PACK),
                     up,
@@ -284,27 +279,22 @@ def tile_list_tanh_mix_scatb_kernel(
                     MULT,
                 )
             else:
-                moved = moved_ring[:, ring]
+                moved = moved_slots[:, slot]
                 nc.scalar.copy(out=moved.rearrange("p (j t) -> p j t", t=PACK), in_=up)
                 nc.gpsimd.tensor_tensor(product, moved, gated, MULT)
 
-        def hidden_half(chunk, s):
-            lo, hi = CHUNKS[chunk]
-            for u in range(lo // UNIT, hi // UNIT):
-                hidden(chunk, s, u)
-
-        def quantise_h(chunk):
+        def hidden_chunk(chunk):
+            for quarter in range(4):
+                hidden(chunk, quarter)
             codes, scales = h_codes(chunk)
             nc.vector.quantize_mx(out=codes.bitcast(FP8X4), scales=scales, in_=h_rounded(chunk))
 
         def output_sums(chunk, n, bank, side):
-            lo, hi = CHUNKS[chunk]
-            width = hi - lo
             codes, scales = h_codes(chunk)
             rows = slice(n * P, (n + 1) * P)
-            acc = bank[:, side * 256 : side * 256 + width]
-            for first in range(0, width, UNIT):
-                below, above = slice(first, first + UNIT), slice(width + first, width + first + UNIT)
+            acc = bank[:, side * CHUNK : (side + 1) * CHUNK]
+            for first in range(0, CHUNK, UNIT):
+                below, above = slice(first, first + UNIT), slice(CHUNK + first, CHUNK + first + UNIT)
                 nc.tensor.matmul_mx(
                     out=acc[:, below],
                     lhsT=wd8_codes[:, rows].bitcast(FP8X4),
@@ -326,33 +316,38 @@ def tile_list_tanh_mix_scatb_kernel(
             return acc
 
         def places(chunk, n):
-            lo, hi = CHUNKS[chunk]
-            return pages[n][:].indirect(place_list[:, lo // GROUP : hi // GROUP])
+            return pages[n][:].indirect(place_list[:, chunk * CHUNK // GROUP : (chunk + 1) * CHUNK // GROUP])
 
-        def weigh(chunk, n, acc, staged):
-            lo, hi = CHUNKS[chunk]
-            nc.vector.scalar_tensor_tensor(staged, acc, bias[:, n : n + 1], wgo_sb[:, lo:hi], ADD, MULT)
-            return staged
+        def wgo_of(chunk):
+            return wgo_sb[:, chunk * CHUNK : (chunk + 1) * CHUNK]
 
-        def by_vector(chunk, n, acc, staged):
-            nc.vector.tensor_copy(places(chunk, n), weigh(chunk, n, acc, staged))
+        def weigh_on_vector(chunk, n, acc, staged):
+            nc.vector.scalar_tensor_tensor(staged, acc, bias[:, n : n + 1], wgo_of(chunk), ADD, MULT)
 
-        def by_gpsimd(chunk, n, acc, staged):
-            lo, hi = CHUNKS[chunk]
+        def add_bias(n, acc, staged):
             nc.scalar.activation(out=staged, in_=acc, func=ACT.Identity, bias=bias[:, n : n + 1])
-            nc.gpsimd.tensor_tensor(staged, staged, wgo_sb[:, lo:hi], MULT)
+
+        def scatter(chunk, n, staged):
             nc.vector.tensor_copy(places(chunk, n), staged)
 
-        def fused(chunk, n, acc, staged):
-            lo, hi = CHUNKS[chunk]
-            nc.scalar.activation(out=staged, in_=acc, func=ACT.Identity, bias=bias[:, n : n + 1])
-            nc.vector.tensor_tensor(places(chunk, n), staged, wgo_sb[:, lo:hi], MULT)
+        def early_place(chunk, n):
+            first = (2 * chunk + n) * CHUNK
+            return early_staged[:, first : first + CHUNK]
 
-        def held_place(chunk, n):
-            lo, hi = CHUNKS[chunk]
-            words = h_rounded(chunk + 1).bitcast(F32)
-            first = words.shape[1] - (PAGES - n) * (hi - lo)
-            return words[:, first : first + hi - lo]
+        def scatter_by_gpsimd(chunk, n, acc):
+            staged = early_place(chunk, n)
+            add_bias(n, acc, staged)
+            nc.gpsimd.tensor_tensor(staged, staged, wgo_of(chunk), MULT)
+            scatter(chunk, n, staged)
+
+        def scatter_held(chunk, n, acc):
+            staged = h_rounded(chunk + 1).bitcast(F32)[:, n * CHUNK : (n + 1) * CHUNK]
+            weigh_on_vector(chunk, n, acc, staged)
+            scatter(chunk, n, staged)
+
+        def scatter_fused(chunk, n, acc, staged):
+            add_bias(n, acc, staged)
+            nc.vector.tensor_tensor(places(chunk, n), staged, wgo_of(chunk), MULT)
 
         def store(n):
             nc.sync.dma_start(out=out[n * P : (n + 1) * P, :], in_=pages[n][:])
@@ -375,56 +370,54 @@ def tile_list_tanh_mix_scatb_kernel(
         round_wu(1, 0, nc.scalar.copy)
         quantise_wu(1, 0)
         deal_wg_words(0, 0, R)
-        gather(1, 3, 0, 256)
-        round_x(1, 0, 256)
-        gather(1, 3, 256, HALF)
+        gather(1, 3, 0, CHUNK)
+        round_x(1, 0, CHUNK)
+        gather(1, 3, CHUNK, HALF)
         gather(1, 3, HALF, J)
         round_wu(1, 1, nc.scalar.copy, 0, 2)
         round_wu(1, 1, nc.vector.tensor_copy, 2, 4)
-        quantise_x(1, 0, 256)
+        quantise_x(1, 0, CHUNK)
         deal_wg_words(1, 0, PASS)
-        round_x(1, 256, HALF)
-        quantise_x(1, 256, HALF)
+        round_x(1, CHUNK, HALF)
+        quantise_x(1, CHUNK, HALF)
         deal_wg_words(1, PASS, R)
         quantise_wu(1, 1)
-        hidden_half(0, 0)
-        hidden_half(0, 1)
-        quantise_h(0)
-        round_x(1, HALF, 768)
-        round_x(1, 768, J)
+        hidden_chunk(0)
+        round_x(1, HALF, HALF + CHUNK)
+        round_x(1, HALF + CHUNK, J)
         quantise_x(1, HALF, J)
-
-        def next_hidden(chunk):
-            hidden_half(chunk, 0)
-            hidden_half(chunk, 1)
-            quantise_h(chunk)
 
         sums = [output_sums(0, 0, bank_a, 0), output_sums(0, 1, bank_c, 0)]
         sums = sums + [output_sums(0, n, bank_b, n % 2) for n in (2, 3)]
-        weighted = [weigh(0, n, sums[n], take(256)) for n in range(2)]
         for n in range(2):
-            nc.vector.tensor_copy(places(0, n), weighted[n])
-        next_hidden(1)
+            weigh_on_vector(0, n, sums[n], early_place(0, n))
+        for n in range(2):
+            scatter(0, n, early_place(0, n))
+        hidden_chunk(1)
         for n in (2, 3):
-            by_vector(0, n, sums[n], held_place(0, n))
+            scatter_held(0, n, sums[n])
+
         sums = [output_sums(1, n, (bank_c, bank_b)[n // 2], n % 2) for n in range(PAGES)]
         for n in range(2):
-            by_gpsimd(1, n, sums[n], take(256))
-        next_hidden(2)
+            scatter_by_gpsimd(1, n, sums[n])
+        hidden_chunk(2)
         for n in (2, 3):
-            by_vector(1, n, sums[n], held_place(1, n))
+            scatter_held(1, n, sums[n])
+
         sums = [output_sums(2, n, bank_c, n) for n in range(2)] + [output_sums(2, 2, bank_a, 0)]
         for n in range(2):
-            by_gpsimd(2, n, sums[n], take(256))
-        next_hidden(3)
-        fused(2, 2, sums[2], moved_ring[:, 3 * PASS : 3 * PASS + 256])
-        staged = [spare[1][:, n * 256 : (n + 1) * 256] for n in range(PAGES)]
+            scatter_by_gpsimd(2, n, sums[n])
+        hidden_chunk(3)
+        last_slot = (SLOTS - 1) * PASS
+        scatter_fused(2, 2, sums[2], moved_slots[:, last_slot : last_slot + CHUNK])
+
+        staged = [last_staged[:, n * CHUNK : (n + 1) * CHUNK] for n in range(PAGES)]
         for n, bank in enumerate((bank_b, banks[0])):
-            fused(3, n, output_sums(3, n, bank, 0), staged[n])
+            scatter_fused(3, n, output_sums(3, n, bank, 0), staged[n])
             store(n)
         sums = [output_sums(3, 2, bank_c, 0), output_sums(2, 3, bank_c, 1)]
-        fused(3, 2, sums[0], staged[2])
+        scatter_fused(3, 2, sums[0], staged[2])
         store(2)
-        fused(2, 3, sums[1], staged[1])
-        fused(3, 3, output_sums(3, 3, banks[1], 0), staged[3])
+        scatter_fused(2, 3, sums[1], staged[1])
+        scatter_fused(3, 3, output_sums(3, 3, banks[1], 0), staged[3])
         store(3)

@@ -28,8 +28,10 @@ PAGES = N // P
 CHUNK = 2 * UNIT
 BANKS = 8
 SUM_BANKS = 5
+LAST_GATE = 6
 SLOTS = 4
-RUN = J // GROUP
+RUNS = J // P
+PLANE_BYTES = 4 * T
 SCALE_SHIFT = 4
 
 
@@ -39,27 +41,35 @@ def tile_list_tanh_mix_scatb_kernel(
     nc = tc.nc
     with ExitStack() as ctx:
         keep = ctx.enter_context(tc.tile_pool(name="keep", bufs=1))
+        arena = ctx.enter_context(tc.tile_pool(name="arena", bufs=1))
         psum = ctx.enter_context(tc.psum_pool(name="psum", bufs=1))
         banks = [psum.tile([P, PASS], F32, name=f"bank{v}") for v in range(BANKS)]
         bank_a, bank_b, bank_c = banks[SUM_BANKS:]
 
         pick_list = keep.tile([P, J // GROUP], U16, name="pick_list")
         place_list = keep.tile([P, J // GROUP], U16, name="place_list")
-        planes = [[keep.tile([P, T], F32, name=f"x{a}{i}") for i in range(PACK)] for a in range(2)]
-        pages = [keep.tile([P, T], F32, name=f"page{n}") for n in range(PAGES)]
-        picked = {
-            (a, start): keep.tile([P, PACK * HALF], F32, name=f"picked{a}_{start}", align_bytes=64)
+        planes = [
+            [arena.tile([P, T], F32, name=f"x{a}{i}", offset=(PACK * a + i) * PLANE_BYTES) for i in range(PACK)]
             for a in range(2)
-            for start in (0, HALF)
-        }
-        wu_raw = {(a, s): keep.tile([P, PACK * PASS], F32, name=f"wu_raw{a}{s}") for a in range(2) for s in range(2)}
+        ]
+
+        def on_plane(a, i, name, shape, dtype, skip=0):
+            return arena.tile(shape, dtype, name=name, offset=(PACK * a + i) * PLANE_BYTES + skip, align_bytes=64)
+
+        pages = [keep.tile([P, T], F32, name=f"page{n}") for n in range(PAGES)]
+        picked = [keep.tile([P, PACK * J], F32, name=f"picked{a}", align_bytes=64) for a in range(2)]
+        wu_raw = {(a, s): keep.tile([P, PACK * PASS], F32, name=f"wu_raw{a}{s}") for a, s in ((0, 0), (0, 1), (1, 0))}
+        wu_last = [keep.tile([P, PACK * PASS // 2], F32, name=f"wu_last{v}") for v in range(2)]
         weights = keep.tile([P, 2 * J], F32, name="weights")
         wgt_sb, wgo_sb = weights[:, 0:J], weights[:, J : 2 * J]
         packed = keep.tile([P, P], F32, name="packed")
         identity = keep.tile([P, P], F32, name="identity")
         bias = keep.tile([P, PAGES], F32, name="bias")
         no_bias = keep.tile([P, 1], F32, name="no_bias")
-        wg_raw = [keep.tile([P, R], I32, name=f"wg_raw{a}", align_bytes=64) for a in range(2)]
+        wg_raw = [
+            arena.tile([P, R], I32, name=f"wg_raw{a}", offset=2 * PACK * PLANE_BYTES + a * 4 * R, align_bytes=64)
+            for a in range(2)
+        ]
         wg_codes = [keep.tile([P, R], I32, name=f"wg_codes{a}", align_bytes=64) for a in range(2)]
         wg_sc_raw = keep.tile([P, R], U8, name="wg_sc_raw", align_bytes=64)
         wg_sc = keep.tile([P, R], U8, name="wg_sc", align_bytes=64)
@@ -67,45 +77,54 @@ def tile_list_tanh_mix_scatb_kernel(
         wd4_codes = keep.tile([P, 2 * N], U8, name="wd4_codes", align_bytes=64)
         wd8_sc = keep.tile([P, N], U8, name="wd8_sc", align_bytes=64)
         wd4_sc = keep.tile([P, N], U8, name="wd4_sc", align_bytes=64)
-        x_codes = [keep.tile([P, J], I32, name=f"x_codes{a}", align_bytes=64) for a in range(2)]
+        x0_codes = on_plane(1, 1, "x_codes0", [P, J], I32, PLANE_BYTES // 2)
+        x1_codes = {c: keep.tile([P, CHUNK], I32, name=f"x_codes1_{c}", align_bytes=64) for c in (0, 2, 3)}
+        x1_codes[1] = arena.tile(
+            [P, CHUNK], I32, name="x_codes1_1", offset=2 * PACK * PLANE_BYTES + 6 * R, align_bytes=64
+        )
+        x0_rounded = on_plane(0, 0, "x0_rounded", [P, PACK * J], BF16)
         x_sc = [keep.tile([P, J], U8, name=f"x_sc{a}", align_bytes=64) for a in range(2)]
-        wu_codes = [keep.tile([P, R], I32, name=f"wu_codes{a}", align_bytes=64) for a in range(2)]
-        wu_sc_tiles = [keep.tile([P, PASS], U8, name=f"wu_sc{v}", align_bytes=64) for v in range(3)]
+        wu_codes = {(0, 0): keep.tile([P, PASS], I32, name="wu_codes00", align_bytes=64)}
+        wu_codes[1, 1] = arena.tile(
+            [P, PASS], I32, name="wu_codes11", offset=2 * PACK * PLANE_BYTES + 4 * R, align_bytes=64
+        )
+        h_words = on_plane(0, 1, "h_words", [P, 2 * J], I32)
+        wu_codes[1, 0] = on_plane(1, 1, "wu_codes10", [P, PASS], I32)
+        wu_codes[0, 1] = on_plane(1, 2, "wu_codes01", [P, PASS], I32)
+        wu_sc = {
+            (a, s): keep.tile([P, PASS], U8, name=f"wu_sc{a}{s}", align_bytes=64) for a in range(2) for s in range(2)
+        }
         h_sc_tiles = [keep.tile([P, J], U8, name=f"h_sc{c}", align_bytes=64) for c in range(2)]
         rounded = [keep.tile([P, PACK * HALF], BF16, name=f"rounded{v}", align_bytes=64) for v in range(4)]
 
-        wu_sc = {
-            (0, 0): wu_sc_tiles[0][:],
-            (1, 0): wu_sc_tiles[0][SCALE_SHIFT:, :],
-            (0, 1): wu_sc_tiles[1][:],
-            (1, 1): wu_sc_tiles[2][:],
-        }
-
-        repeated = picked[1, 0]
-        first_gated = picked[1, 0]
-        last_staged = picked[1, 0]
-        early_staged = picked[0, HALF]
+        repeated = picked[1]
+        first_gated = wu_raw[1, 0]
+        last_staged = picked[1]
+        early_staged = picked[0][:, 2 * J : 4 * J]
         gated_slots, moved_slots = wu_raw[0, 0], wu_raw[0, 1]
 
-        def wu_rounded(s):
-            return rounded[2 + s]
+        def wu_rounded(a, s):
+            if (a, s) == (1, 0):
+                return picked[1][:, 2 * J : 3 * J].bitcast(BF16)
+            return rounded[3 if a == 0 else 2][:]
 
         def x_rounded(a, lo, hi):
-            start = lo // HALF * HALF
             if a == 0:
-                tile = rounded[lo // HALF][:]
-            elif lo < HALF:
-                tile = picked[0, 0][:].bitcast(BF16)
-            else:
-                tile = first_gated[:, PASS : 3 * PASS].bitcast(BF16)
-            return tile[:, PACK * (lo - start) : PACK * (hi - start)]
+                return x0_rounded[:, PACK * lo : PACK * hi]
+            places = {
+                (1, 0): picked[0][:, 0:PASS],
+                (1, CHUNK): picked[0][:, PASS : 2 * PASS],
+                (1, 2 * CHUNK): first_gated[:, 3 * PASS : 4 * PASS],
+                (1, 3 * CHUNK): moved_slots[:, 2 * PASS : 3 * PASS],
+            }
+            return places[a, lo].bitcast(BF16)
 
         def h_rounded(chunk):
             return rounded[min(chunk, 1)][:]
 
         def h_codes(chunk):
             cols = slice(chunk % 2 * 2 * CHUNK, (chunk % 2 + 1) * 2 * CHUNK)
-            return wg_raw[chunk // 2][:, cols], h_sc_tiles[chunk // 2][:, cols]
+            return h_words[:, chunk * 2 * CHUNK : (chunk + 1) * 2 * CHUNK], h_sc_tiles[chunk // 2][:, cols]
 
         x_rows = xT.rearrange("(a p i) t -> a i p t", a=2, i=PACK)
 
@@ -117,6 +136,13 @@ def tile_list_tanh_mix_scatb_kernel(
             nc.sync.dma_start(
                 out=wu_raw[a, s][:].rearrange("p (i r) -> p i r", i=PACK),
                 in_=wu[a * PASS : (a + 1) * PASS, cols].rearrange("(p i) r -> p i r", i=PACK),
+            )
+
+        def load_wu_last(v):
+            cols = slice(PASS + v * PASS // 2, PASS + (v + 1) * PASS // 2)
+            nc.sync.dma_start(
+                out=wu_last[v][:].rearrange("p (i r) -> p i r", i=PACK),
+                in_=wu[PASS : 2 * PASS, cols].rearrange("(p i) r -> p i r", i=PACK),
             )
 
         def load_wg(a, lo, hi):
@@ -143,7 +169,8 @@ def tile_list_tanh_mix_scatb_kernel(
 
         for w, rows in enumerate((wgt, wgo)):
             nc.sync.dma_start(
-                out=packed[:, w * RUN : (w + 1) * RUN], in_=rows[0:P:GROUP, :].rearrange("g (b c) -> g b c", c=RUN)
+                out=packed[w * P // 2 : (w + 1) * P // 2, :],
+                in_=rows[0:P:GROUP, :].rearrange("g (b c) -> g b c", c=P),
             )
         nc.sync.dma_start(pick_list[:], offs)
         load_x(0, 0)
@@ -153,44 +180,43 @@ def tile_list_tanh_mix_scatb_kernel(
         load_wu(0, 0)
         load_x(0, 3)
         load_x(1, 0)
-        load_wu(0, 1)
-        load_x(1, 1)
-        load_x(1, 2)
         load_wu(1, 0)
-        load_wg(0, 0, R)
+        load_x(1, 1)
+        load_wu(0, 1)
+        load_x(1, 2)
+        load_wu_last(0)
         load_x(1, 3)
-        load_wg(1, 0, PASS)
-        load_wu(1, 1)
-        load_wg(1, PASS, R)
+        load_wg(0, 0, R)
+        load_wu_last(1)
+        load_wg(1, 0, R)
         nc.sync.dma_start(out=wd8_codes[:], in_=wd8_words[0].rearrange("p n i -> p (n i)").bitcast(I32))
         nc.sync.dma_start(out=wd4_codes[:].bitcast(I32), in_=wd4_words[0].bitcast(I32))
         with nc.allow_non_contiguous_dma(reason="one bias value for each partition and page"):
             nc.sync.dma_start(out=bias[:], in_=b.rearrange("(n p) -> p n", p=P))
         nc.sync.dma_start(place_list[:], offs2)
 
+        def spread(copy, source, target, w, first, last):
+            by_run = source[:, 0:P].rearrange("p (w g b) -> p w b g", w=2, b=RUNS)[:, w, first:last, :]
+            copy(
+                out=repeated[:, first * P : last * P].rearrange("p (b g r) -> p b g r", g=GROUPS, r=GROUP),
+                in_=by_run.unsqueeze(3).to_broadcast([P, last - first, GROUPS, GROUP]),
+            )
+            for k in range(last - first):
+                run = repeated[:, (first + k) * P : (first + k + 1) * P]
+                nc.tensor.transpose(target[:, k * P : (k + 1) * P], run, identity[:])
+            copy(out=weights[:, w * J + first * P : w * J + last * P], in_=target[:, 0 : (last - first) * P])
+
         def spread_weights():
-            copies = [nc.scalar.copy, nc.vector.tensor_copy, nc.scalar.copy, nc.scalar.copy]
             for v in range(2):
                 nc.tensor.transpose(banks[v][:, 0:P], packed[:], identity[:])
-            for v in range(4):
-                by_run = banks[int(v == 1)][:, 0:P].rearrange("p (g b) -> p b g", b=GROUP)
-                copies[v](
-                    out=repeated[:, v * PASS : (v + 1) * PASS].rearrange("p (b g r) -> p b g r", g=GROUPS, r=GROUP),
-                    in_=by_run[:, 4 * v : 4 * v + 4, :].unsqueeze(3).to_broadcast([P, 4, GROUPS, GROUP]),
-                )
-                for k in range(4):
-                    run = repeated[:, (4 * v + k) * P : (4 * v + k + 1) * P]
-                    nc.tensor.transpose(banks[2 + v][:, k * P : (k + 1) * P], run, identity[:])
-            for w, rows in enumerate((wgt_sb, wgo_sb)):
-                for v in range(4):
-                    (copies[v] if w == 0 else nc.scalar.copy)(
-                        out=rows[:, v * 4 * RUN : (v + 1) * 4 * RUN].rearrange("p (k c) -> p k c", c=RUN),
-                        in_=banks[2 + v][:].rearrange("p (k w c) -> p w k c", k=4, w=2)[:, w],
-                    )
+            spread(nc.scalar.copy, banks[0], banks[2], 0, 0, 2)
+            spread(nc.vector.tensor_copy, banks[1], banks[3], 0, 2, 4)
+            spread(nc.scalar.copy, banks[0], banks[4], 0, 4, RUNS)
+            spread(nc.scalar.copy, banks[0], banks[5], 1, 0, 4)
+            spread(nc.scalar.copy, banks[0], banks[6], 1, 4, RUNS)
 
         def picks(a, lo, hi):
-            start = lo // HALF * HALF
-            return picked[a, start][:].rearrange("p (i j) -> p i j", i=PACK)[:, :, lo - start : hi - start]
+            return picked[a][:].rearrange("p (i j) -> p i j", i=PACK)[:, :, lo:hi]
 
         def gather(a, i, lo, hi):
             nc.vector.tensor_tensor(
@@ -200,26 +226,37 @@ def tile_list_tanh_mix_scatb_kernel(
                 MULT,
             )
 
-        def round_x(a, lo, hi):
-            nc.scalar.copy(
+        def round_x(a, lo, hi, copy=nc.scalar.copy):
+            copy(
                 out=x_rounded(a, lo, hi).rearrange("p (g e i) -> p g i e", e=4, i=PACK),
                 in_=picks(a, lo, hi).rearrange("p i (g e) -> p g i e", e=4),
             )
 
+        def x_words(a, lo, hi):
+            if a == 0:
+                return x0_codes[:, lo:hi]
+            start = lo // CHUNK * CHUNK
+            return x1_codes[lo // CHUNK][:, lo - start : hi - start]
+
         def quantise_x(a, lo, hi):
             nc.vector.quantize_mx(
-                out=x_codes[a][:, lo:hi].bitcast(FP8X4), scales=x_sc[a][:, lo:hi], in_=x_rounded(a, lo, hi)
+                out=x_words(a, lo, hi).bitcast(FP8X4), scales=x_sc[a][:, lo:hi], in_=x_rounded(a, lo, hi)
             )
 
-        def round_wu(a, s, copy, first=0, last=PACK):
-            copy(
-                out=wu_rounded(s)[:, first * PASS : last * PASS].rearrange("p (t q i) -> p q i t", q=P, i=PACK),
-                in_=wu_raw[a, s][:].rearrange("p (i q t) -> p q i t", i=PACK, t=PACK)[:, :, :, first:last],
+        def round_wu(a, s):
+            nc.scalar.copy(
+                out=wu_rounded(a, s).rearrange("p (t q i) -> p q i t", q=P, i=PACK),
+                in_=wu_raw[a, s][:].rearrange("p (i q t) -> p q i t", i=PACK, t=PACK),
+            )
+
+        def round_wu_last(v):
+            nc.scalar.copy(
+                out=wu_rounded(1, 1).rearrange("p (t q i) -> p q i t", q=P, i=PACK)[:, v * P // 2 : (v + 1) * P // 2],
+                in_=wu_last[v][:].rearrange("p (i q t) -> p q i t", i=PACK, t=PACK),
             )
 
         def quantise_wu(a, s):
-            cols = slice(s * PASS, (s + 1) * PASS)
-            nc.vector.quantize_mx(out=wu_codes[a][:, cols].bitcast(FP8X4), scales=wu_sc[a, s], in_=wu_rounded(s)[:])
+            nc.vector.quantize_mx(out=wu_codes[a, s][:].bitcast(FP8X4), scales=wu_sc[a, s][:], in_=wu_rounded(a, s))
 
         def deal_wg_words(a, lo, hi):
             nc.vector.tensor_copy(
@@ -234,7 +271,11 @@ def tile_list_tanh_mix_scatb_kernel(
             )
 
         def first_products(turn, u, stationary):
-            bank = banks[turn if turn < BANKS else (turn - BANKS) % SUM_BANKS]
+            chunk, place = divmod(turn, BANKS)
+            if chunk == 0 or place == LAST_GATE:
+                bank = banks[place]
+            else:
+                bank = banks[((BANKS - 1) * (chunk - 1) + place - (place > LAST_GATE)) % SUM_BANKS]
             by_t = bank[:].rearrange("p (t j) -> p t j", t=PACK)
             cols = slice(u * UNIT, (u + 1) * UNIT)
             for a in range(2):
@@ -244,7 +285,7 @@ def tile_list_tanh_mix_scatb_kernel(
                         out=by_t[:, t, :],
                         lhsT=codes.bitcast(FP8X4),
                         lhsT_scale=scales,
-                        rhs=x_codes[a][:, cols].bitcast(FP8X4),
+                        rhs=x_words(a, u * UNIT, (u + 1) * UNIT).bitcast(FP8X4),
                         rhs_scale=x_sc[a][:, cols],
                         start=(a == 0 and t == 0),
                         stop=(a == 1 and t == PACK - 1),
@@ -260,8 +301,7 @@ def tile_list_tanh_mix_scatb_kernel(
                 return wg_codes[a][:, first : first + P], wg_sc[SCALE_SHIFT * a :, first : first + P]
 
             def wu_stationary(a, t):
-                first = s * PASS + t * P
-                return wu_codes[a][:, first : first + P], wu_sc[a, s][:, t * P : (t + 1) * P]
+                return wu_codes[a, s][:, t * P : (t + 1) * P], wu_sc[a, s][:, t * P : (t + 1) * P]
 
             slot = slice(step % SLOTS * PASS, (step % SLOTS + 1) * PASS)
             gated = (gated_slots if chunk > 0 else first_gated)[:, slot]
@@ -271,7 +311,7 @@ def tile_list_tanh_mix_scatb_kernel(
             )
             up = first_products(2 * step + 1, u, wu_stationary)
             product = h_rounded(chunk)[:, quarter * PACK * UNIT : (quarter + 1) * PACK * UNIT]
-            if chunk == 0 or (chunk, quarter) == (1, 3):
+            if chunk == 0:
                 nc.vector.tensor_tensor(
                     product.rearrange("p (j t) -> p j t", t=PACK),
                     up,
@@ -286,6 +326,9 @@ def tile_list_tanh_mix_scatb_kernel(
         def hidden_chunk(chunk):
             for quarter in range(4):
                 hidden(chunk, quarter)
+                if (chunk, quarter) == (1, 2):
+                    round_x(1, 3 * CHUNK, J)
+                    quantise_x(1, 3 * CHUNK, J)
             codes, scales = h_codes(chunk)
             nc.vector.quantize_mx(out=codes.bitcast(FP8X4), scales=scales, in_=h_rounded(chunk))
 
@@ -354,55 +397,55 @@ def tile_list_tanh_mix_scatb_kernel(
 
         spread_weights()
         for i in range(PACK):
-            gather(0, i, 0, HALF)
-            gather(0, i, HALF, J)
+            if i == 0:
+                gather(0, i, 0, HALF)
+                gather(0, i, HALF, J)
+            else:
+                gather(0, i, 0, J)
         deal_wg_scales()
-        round_x(0, 0, HALF)
-        round_x(0, HALF, J)
-        quantise_x(0, 0, HALF)
-        quantise_x(0, HALF, J)
-        for s in range(2):
-            round_wu(0, s, nc.scalar.copy)
-            quantise_wu(0, s)
-        for i in range(PACK - 1):
-            gather(1, i, 0, HALF)
-            gather(1, i, HALF, J)
-        round_wu(1, 0, nc.scalar.copy)
+        round_wu(0, 0)
+        quantise_wu(0, 0)
+        gather(1, 0, 0, J)
+        round_x(0, 0, J)
+        gather(1, 1, 0, J)
+        quantise_x(0, 0, J)
+        round_wu(1, 0)
         quantise_wu(1, 0)
+        gather(1, 2, 0, J)
+        round_wu(0, 1)
+        quantise_wu(0, 1)
+        round_wu_last(0)
+        gather(1, 3, 0, HALF)
         deal_wg_words(0, 0, R)
-        gather(1, 3, 0, CHUNK)
-        round_x(1, 0, CHUNK)
-        gather(1, 3, CHUNK, HALF)
         gather(1, 3, HALF, J)
-        round_wu(1, 1, nc.scalar.copy, 0, 2)
-        round_wu(1, 1, nc.vector.tensor_copy, 2, 4)
+        round_x(1, 0, CHUNK)
         quantise_x(1, 0, CHUNK)
-        deal_wg_words(1, 0, PASS)
         round_x(1, CHUNK, HALF)
+        round_wu_last(1)
+        deal_wg_words(1, 0, R)
         quantise_x(1, CHUNK, HALF)
-        deal_wg_words(1, PASS, R)
         quantise_wu(1, 1)
         hidden_chunk(0)
-        round_x(1, HALF, HALF + CHUNK)
-        round_x(1, HALF + CHUNK, J)
-        quantise_x(1, HALF, J)
+        round_x(1, HALF, HALF + CHUNK, nc.vector.tensor_copy)
 
         sums = [output_sums(0, 0, bank_a, 0), output_sums(0, 1, bank_c, 0)]
-        sums = sums + [output_sums(0, n, bank_b, n % 2) for n in (2, 3)]
         for n in range(2):
             weigh_on_vector(0, n, sums[n], early_place(0, n))
+        quantise_x(1, HALF, HALF + CHUNK)
         for n in range(2):
             scatter(0, n, early_place(0, n))
         hidden_chunk(1)
+        held = [output_sums(0, n, bank_b, n % 2) for n in (2, 3)]
         for n in (2, 3):
-            scatter_held(0, n, sums[n])
+            scatter_held(0, n, held[n - 2])
 
-        sums = [output_sums(1, n, (bank_c, bank_b)[n // 2], n % 2) for n in range(PAGES)]
+        sums = [output_sums(1, n, bank_c, n) for n in range(2)]
         for n in range(2):
             scatter_by_gpsimd(1, n, sums[n])
         hidden_chunk(2)
+        held = [output_sums(1, n, bank_b, n % 2) for n in (2, 3)]
         for n in (2, 3):
-            scatter_held(1, n, sums[n])
+            scatter_held(1, n, held[n - 2])
 
         sums = [output_sums(2, n, bank_c, n) for n in range(2)] + [output_sums(2, 2, bank_a, 0)]
         for n in range(2):
@@ -415,9 +458,11 @@ def tile_list_tanh_mix_scatb_kernel(
         for n, bank in enumerate((bank_b, banks[0])):
             scatter_fused(3, n, output_sums(3, n, bank, 0), staged[n])
             store(n)
-        sums = [output_sums(3, 2, bank_c, 0), output_sums(2, 3, bank_c, 1)]
-        scatter_fused(3, 2, sums[0], staged[2])
+        scatter_fused(3, 2, output_sums(3, 2, bank_c, 0), staged[2])
         store(2)
-        scatter_fused(2, 3, sums[1], staged[1])
-        scatter_fused(3, 3, output_sums(3, 3, banks[1], 0), staged[3])
+        both = last_staged[:, PAGES * CHUNK : (PAGES + 2) * CHUNK]
+        for side in range(2):
+            output_sums(2 + side, 3, banks[1], side)
+        add_bias(3, banks[1][:], both)
+        nc.vector.tensor_tensor(pages[3][:].indirect(place_list[:, HALF // GROUP :]), both, wgo_sb[:, HALF:], MULT)
         store(3)

@@ -78,7 +78,7 @@ def tile_list_tanh_mix_scatb_kernel(
         wd8_sc = keep.tile([P, N], U8, name="wd8_sc", align_bytes=64)
         wd4_sc = keep.tile([P, N], U8, name="wd4_sc", align_bytes=64)
         x0_codes = on_plane(1, 1, "x_codes0", [P, J], I32, PLANE_BYTES // 2)
-        x1_codes = {c: keep.tile([P, CHUNK], I32, name=f"x_codes1_{c}", align_bytes=64) for c in (0, 2, 3)}
+        x1_codes = {c: keep.tile([P, CHUNK], I32, name=f"x_codes1_{c}", align_bytes=64) for c in (0,)}
         x1_codes[1] = arena.tile(
             [P, CHUNK], I32, name="x_codes1_1", offset=2 * PACK * PLANE_BYTES + 6 * R, align_bytes=64
         )
@@ -95,7 +95,10 @@ def tile_list_tanh_mix_scatb_kernel(
             (a, s): keep.tile([P, PASS], U8, name=f"wu_sc{a}{s}", align_bytes=64) for a in range(2) for s in range(2)
         }
         h_sc_tiles = [keep.tile([P, J], U8, name=f"h_sc{c}", align_bytes=64) for c in range(2)]
-        rounded = [keep.tile([P, PACK * HALF], BF16, name=f"rounded{v}", align_bytes=64) for v in range(4)]
+        rounded = [keep.tile([P, PACK * HALF], BF16, name=f"rounded{v}", align_bytes=64) for v in range(4) if v > 1]
+        rounded = {2: rounded[0], 3: rounded[1]}
+        first_h = on_plane(0, 3, "first_h", [P, PACK * HALF], BF16)
+        x1_late = on_plane(0, 3, "x1_late", [P, HALF], I32)
 
         repeated = picked[1]
         first_gated = wu_raw[1, 0]
@@ -114,13 +117,12 @@ def tile_list_tanh_mix_scatb_kernel(
             places = {
                 (1, 0): picked[0][:, 0:PASS],
                 (1, CHUNK): picked[0][:, PASS : 2 * PASS],
-                (1, 2 * CHUNK): first_gated[:, 3 * PASS : 4 * PASS],
-                (1, 3 * CHUNK): moved_slots[:, 2 * PASS : 3 * PASS],
+                (1, HALF): rounded[2][:].bitcast(F32),
             }
             return places[a, lo].bitcast(BF16)
 
         def h_rounded(chunk):
-            return rounded[min(chunk, 1)][:]
+            return first_h[:] if chunk == 0 else rounded[2][:]
 
         def h_codes(chunk):
             cols = slice(chunk % 2 * 2 * CHUNK, (chunk % 2 + 1) * 2 * CHUNK)
@@ -232,9 +234,21 @@ def tile_list_tanh_mix_scatb_kernel(
                 in_=picks(a, lo, hi).rearrange("p i (g e) -> p g i e", e=4),
             )
 
+        def round_on_gpsimd(a, lo, hi):
+            nc.gpsimd.tensor_scalar(
+                x_rounded(a, lo, hi).rearrange("p (j i) -> p j i", i=PACK),
+                picks(a, lo, hi).rearrange("p i j -> p j i"),
+                1.0,
+                0.0,
+                MULT,
+                ADD,
+            )
+
         def x_words(a, lo, hi):
             if a == 0:
                 return x0_codes[:, lo:hi]
+            if lo >= HALF:
+                return x1_late[:, lo - HALF : hi - HALF]
             start = lo // CHUNK * CHUNK
             return x1_codes[lo // CHUNK][:, lo - start : hi - start]
 
@@ -311,7 +325,7 @@ def tile_list_tanh_mix_scatb_kernel(
             )
             up = first_products(2 * step + 1, u, wu_stationary)
             product = h_rounded(chunk)[:, quarter * PACK * UNIT : (quarter + 1) * PACK * UNIT]
-            if chunk == 0:
+            if chunk == 0 or (chunk, quarter) == (1, 3):
                 nc.vector.tensor_tensor(
                     product.rearrange("p (j t) -> p j t", t=PACK),
                     up,
@@ -326,9 +340,6 @@ def tile_list_tanh_mix_scatb_kernel(
         def hidden_chunk(chunk):
             for quarter in range(4):
                 hidden(chunk, quarter)
-                if (chunk, quarter) == (1, 2):
-                    round_x(1, 3 * CHUNK, J)
-                    quantise_x(1, 3 * CHUNK, J)
             codes, scales = h_codes(chunk)
             nc.vector.quantize_mx(out=codes.bitcast(FP8X4), scales=scales, in_=h_rounded(chunk))
 
@@ -425,13 +436,13 @@ def tile_list_tanh_mix_scatb_kernel(
         deal_wg_words(1, 0, R)
         quantise_x(1, CHUNK, HALF)
         quantise_wu(1, 1)
+        round_on_gpsimd(1, HALF, J)
         hidden_chunk(0)
-        round_x(1, HALF, HALF + CHUNK, nc.vector.tensor_copy)
+        quantise_x(1, HALF, J)
 
         sums = [output_sums(0, 0, bank_a, 0), output_sums(0, 1, bank_c, 0)]
         for n in range(2):
             weigh_on_vector(0, n, sums[n], early_place(0, n))
-        quantise_x(1, HALF, HALF + CHUNK)
         for n in range(2):
             scatter(0, n, early_place(0, n))
         hidden_chunk(1)

@@ -66,11 +66,14 @@ def tile_list_tanh_mix_scatb_kernel(
         identity = keep.tile([P, P], F32, name="identity")
         bias = keep.tile([P, PAGES], F32, name="bias")
         no_bias = keep.tile([P, 1], F32, name="no_bias")
-        wg_raw = [
-            arena.tile([P, R], I32, name=f"wg_raw{a}", offset=2 * PACK * PLANE_BYTES + a * 4 * R, align_bytes=64)
-            for a in range(2)
-        ]
-        wg_codes = [keep.tile([P, R], I32, name=f"wg_codes{a}", align_bytes=64) for a in range(2)]
+        wg_first = keep.tile([P, 2 * PASS], I32, name="wg_first", align_bytes=64)
+        wg_raw = {
+            (0, 0): wg_first[:, 0:PASS],
+            (1, 0): wg_first[:, PASS : 2 * PASS],
+            (0, 1): keep.tile([P, PASS], I32, name="wg_raw01", align_bytes=64)[:],
+            (1, 1): arena.tile([P, PASS], I32, name="wg_raw11", offset=2 * PACK * PLANE_BYTES, align_bytes=64)[:],
+        }
+        wg_codes = [keep.tile([P, 2 * PASS], I32, name=f"wg_codes{s}", align_bytes=64) for s in range(2)]
         wg_sc_raw = keep.tile([P, R], U8, name="wg_sc_raw", align_bytes=64)
         wg_sc = keep.tile([P, R], U8, name="wg_sc", align_bytes=64)
         wd8_codes = keep.tile([P, N], I32, name="wd8_codes", align_bytes=64)
@@ -79,14 +82,15 @@ def tile_list_tanh_mix_scatb_kernel(
         wd4_sc = keep.tile([P, N], U8, name="wd4_sc", align_bytes=64)
         x0_codes = on_plane(1, 1, "x_codes0", [P, J], I32, PLANE_BYTES // 2)
         x1_codes = {c: keep.tile([P, CHUNK], I32, name=f"x_codes1_{c}", align_bytes=64) for c in (0,)}
-        x1_codes[1] = arena.tile(
-            [P, CHUNK], I32, name="x_codes1_1", offset=2 * PACK * PLANE_BYTES + 6 * R, align_bytes=64
-        )
+        x1_codes[1] = keep.tile([P, CHUNK], I32, name="x_codes1_1", align_bytes=64)
         x0_rounded = on_plane(0, 0, "x0_rounded", [P, PACK * J], BF16)
         x_sc = [keep.tile([P, J], U8, name=f"x_sc{a}", align_bytes=64) for a in range(2)]
         wu_codes = {(0, 0): keep.tile([P, PASS], I32, name="wu_codes00", align_bytes=64)}
         wu_codes[1, 1] = arena.tile(
-            [P, PASS], I32, name="wu_codes11", offset=2 * PACK * PLANE_BYTES + 4 * R, align_bytes=64
+            [P, PASS], I32, name="wu_codes11", offset=2 * PACK * PLANE_BYTES + 2 * PASS, align_bytes=64
+        )
+        second_rounded = arena.tile(
+            [P, PASS], F32, name="second_rounded", offset=2 * PACK * PLANE_BYTES + 4 * PASS, align_bytes=64
         )
         h_words = on_plane(0, 1, "h_words", [P, 2 * J], I32)
         wu_codes[1, 0] = on_plane(1, 1, "wu_codes10", [P, PASS], I32)
@@ -116,7 +120,7 @@ def tile_list_tanh_mix_scatb_kernel(
                 return x0_rounded[:, PACK * lo : PACK * hi]
             places = {
                 (1, 0): picked[0][:, 0:PASS],
-                (1, CHUNK): picked[0][:, PASS : 2 * PASS],
+                (1, CHUNK): second_rounded[:],
                 (1, HALF): rounded[2][:].bitcast(F32),
             }
             return places[a, lo].bitcast(BF16)
@@ -147,9 +151,13 @@ def tile_list_tanh_mix_scatb_kernel(
                 in_=wu[PASS : 2 * PASS, cols].rearrange("(p i) r -> p i r", i=PACK),
             )
 
-        def load_wg(a, lo, hi):
-            words = wg_words[a, :, lo:hi, :].rearrange("p r i -> p (r i)")
-            nc.sync.dma_start(out=wg_raw[a][:, lo:hi], in_=words.bitcast(I32))
+        def load_wg_first():
+            words = wg_words[:, :, 0:PASS, :].rearrange("a p r i -> p a (r i)")
+            nc.sync.dma_start(out=wg_first[:].rearrange("p (a r) -> p a r", a=2), in_=words.bitcast(I32))
+
+        def load_wg(a, s):
+            words = wg_words[a, :, s * PASS : (s + 1) * PASS, :].rearrange("p r i -> p (r i)")
+            nc.sync.dma_start(out=wg_raw[a, s], in_=words.bitcast(I32))
 
         def load_scale_rows(queue, tile, rows):
             passes = rows.shape[0]
@@ -188,9 +196,10 @@ def tile_list_tanh_mix_scatb_kernel(
         load_x(1, 2)
         load_wu_last(0)
         load_x(1, 3)
-        load_wg(0, 0, R)
+        load_wg_first()
         load_wu_last(1)
-        load_wg(1, 0, R)
+        load_wg(0, 1)
+        load_wg(1, 1)
         nc.sync.dma_start(out=wd8_codes[:], in_=wd8_words[0].rearrange("p n i -> p (n i)").bitcast(I32))
         nc.sync.dma_start(out=wd4_codes[:].bitcast(I32), in_=wd4_words[0].bitcast(I32))
         with nc.allow_non_contiguous_dma(reason="one bias value for each partition and page"):
@@ -272,10 +281,10 @@ def tile_list_tanh_mix_scatb_kernel(
         def quantise_wu(a, s):
             nc.vector.quantize_mx(out=wu_codes[a, s][:].bitcast(FP8X4), scales=wu_sc[a, s][:], in_=wu_rounded(a, s))
 
-        def deal_wg_words(a, lo, hi):
+        def deal_wg_words(dealt, raw):
             nc.vector.tensor_copy(
-                out=wg_codes[a][:, lo:hi].rearrange("p (s t q) -> p s q t", t=PACK, q=P),
-                in_=wg_raw[a][:, lo:hi].rearrange("p (s q t) -> p s q t", t=PACK, q=P),
+                out=dealt.rearrange("p (a t q) -> p a q t", t=PACK, q=P),
+                in_=raw.rearrange("p (a q t) -> p a q t", t=PACK, q=P),
             )
 
         def deal_wg_scales():
@@ -312,7 +321,7 @@ def tile_list_tanh_mix_scatb_kernel(
 
             def wg_stationary(a, t):
                 first = s * PASS + t * P
-                return wg_codes[a][:, first : first + P], wg_sc[SCALE_SHIFT * a :, first : first + P]
+                return wg_codes[s][:, a * PASS + t * P : a * PASS + (t + 1) * P], wg_sc[SCALE_SHIFT * a :, first : first + P]
 
             def wu_stationary(a, t):
                 return wu_codes[a, s][:, t * P : (t + 1) * P], wu_sc[a, s][:, t * P : (t + 1) * P]
@@ -427,14 +436,15 @@ def tile_list_tanh_mix_scatb_kernel(
         quantise_wu(0, 1)
         round_wu_last(0)
         gather(1, 3, 0, HALF)
-        deal_wg_words(0, 0, R)
+        deal_wg_words(wg_codes[0][:], wg_first[:])
         gather(1, 3, HALF, J)
         round_x(1, 0, CHUNK)
         quantise_x(1, 0, CHUNK)
         round_x(1, CHUNK, HALF)
         round_wu_last(1)
-        deal_wg_words(1, 0, R)
         quantise_x(1, CHUNK, HALF)
+        deal_wg_words(wg_codes[1][:, 0:PASS], wg_raw[0, 1])
+        deal_wg_words(wg_codes[1][:, PASS : 2 * PASS], wg_raw[1, 1])
         quantise_wu(1, 1)
         round_on_gpsimd(1, HALF, J)
         hidden_chunk(0)

@@ -101,8 +101,8 @@ def tile_list_tanh_mix_scatb_kernel(
         h_sc_tiles = [keep.tile([P, J], U8, name=f"h_sc{c}", align_bytes=64) for c in range(2)]
         rounded = [keep.tile([P, PACK * HALF], BF16, name=f"rounded{v}", align_bytes=64) for v in range(4) if v > 1]
         rounded = {2: rounded[0], 3: rounded[1]}
-        first_h = on_plane(0, 3, "first_h", [P, PACK * HALF], BF16)
-        x1_late = on_plane(0, 3, "x1_late", [P, HALF], I32)
+        first_h = on_plane(1, 3, "first_h", [P, PACK * HALF], BF16, PLANE_BYTES - 6 * PASS)
+        x1_late = on_plane(1, 3, "x1_late", [P, HALF], I32, PLANE_BYTES - 6 * PASS)
 
         repeated = picked[1]
         first_gated = wu_raw[1, 0]
@@ -272,8 +272,8 @@ def tile_list_tanh_mix_scatb_kernel(
                 in_=wu_raw[a, s][:].rearrange("p (i q t) -> p q i t", i=PACK, t=PACK),
             )
 
-        def round_wu_last(v):
-            nc.scalar.copy(
+        def round_wu_last(v, copy):
+            copy(
                 out=wu_rounded(1, 1).rearrange("p (t q i) -> p q i t", q=P, i=PACK)[:, v * P // 2 : (v + 1) * P // 2],
                 in_=wu_last[v][:].rearrange("p (i q t) -> p q i t", i=PACK, t=PACK),
             )
@@ -434,14 +434,14 @@ def tile_list_tanh_mix_scatb_kernel(
         gather(1, 2, 0, J)
         round_wu(0, 1)
         quantise_wu(0, 1)
-        round_wu_last(0)
+        round_wu_last(0, nc.scalar.copy)
         gather(1, 3, 0, HALF)
         deal_wg_words(wg_codes[0][:], wg_first[:])
         gather(1, 3, HALF, J)
         round_x(1, 0, CHUNK)
         quantise_x(1, 0, CHUNK)
         round_x(1, CHUNK, HALF)
-        round_wu_last(1)
+        round_wu_last(1, nc.vector.tensor_copy)
         quantise_x(1, CHUNK, HALF)
         deal_wg_words(wg_codes[1][:, 0:PASS], wg_raw[0, 1])
         deal_wg_words(wg_codes[1][:, PASS : 2 * PASS], wg_raw[1, 1])

@@ -80,7 +80,7 @@ def tile_list_tanh_mix_scatb_kernel(
         wd4_codes = keep.tile([P, 2 * N], U8, name="wd4_codes", align_bytes=64)
         wd8_sc = keep.tile([P, N], U8, name="wd8_sc", align_bytes=64)
         wd4_sc = keep.tile([P, N], U8, name="wd4_sc", align_bytes=64)
-        x0_codes = on_plane(1, 1, "x_codes0", [P, J], I32, PLANE_BYTES // 2)
+        x0_codes = on_plane(0, 2, "x_codes0", [P, J], I32, PLANE_BYTES // 2)
         x1_codes = {c: keep.tile([P, CHUNK], I32, name=f"x_codes1_{c}", align_bytes=64) for c in (0,)}
         x1_codes[1] = keep.tile([P, CHUNK], I32, name="x_codes1_1", align_bytes=64)
         x0_rounded = on_plane(0, 0, "x0_rounded", [P, PACK * J], BF16)
@@ -93,10 +93,14 @@ def tile_list_tanh_mix_scatb_kernel(
             [P, PASS], F32, name="second_rounded", offset=2 * PACK * PLANE_BYTES + 4 * PASS, align_bytes=64
         )
         h_words = on_plane(0, 1, "h_words", [P, 2 * J], I32)
-        wu_codes[1, 0] = on_plane(1, 1, "wu_codes10", [P, PASS], I32)
+        wu_codes[1, 0] = on_plane(0, 2, "wu_codes10", [P, PASS], I32)
         wu_codes[0, 1] = on_plane(1, 2, "wu_codes01", [P, PASS], I32)
+        wu_sc_tiles = [keep.tile([P, PASS], U8, name=f"wu_sc{v}", align_bytes=64) for v in range(3)]
         wu_sc = {
-            (a, s): keep.tile([P, PASS], U8, name=f"wu_sc{a}{s}", align_bytes=64) for a in range(2) for s in range(2)
+            (0, 0): wu_sc_tiles[0][:],
+            (0, 1): wu_sc_tiles[0][SCALE_SHIFT:, :],
+            (1, 0): wu_sc_tiles[1][:],
+            (1, 1): wu_sc_tiles[2][:],
         }
         h_sc_tiles = [keep.tile([P, J], U8, name=f"h_sc{c}", align_bytes=64) for c in range(2)]
         rounded = [keep.tile([P, PACK * HALF], BF16, name=f"rounded{v}", align_bytes=64) for v in range(4) if v > 1]
@@ -279,7 +283,7 @@ def tile_list_tanh_mix_scatb_kernel(
             )
 
         def quantise_wu(a, s):
-            nc.vector.quantize_mx(out=wu_codes[a, s][:].bitcast(FP8X4), scales=wu_sc[a, s][:], in_=wu_rounded(a, s))
+            nc.vector.quantize_mx(out=wu_codes[a, s][:].bitcast(FP8X4), scales=wu_sc[a, s], in_=wu_rounded(a, s))
 
         def deal_wg_words(dealt, raw):
             nc.vector.tensor_copy(
@@ -417,7 +421,7 @@ def tile_list_tanh_mix_scatb_kernel(
 
         spread_weights()
         for i in range(PACK):
-            if i == 0:
+            if i in (0, PACK - 1):
                 gather(0, i, 0, HALF)
                 gather(0, i, HALF, J)
             else:
@@ -426,9 +430,10 @@ def tile_list_tanh_mix_scatb_kernel(
         round_wu(0, 0)
         quantise_wu(0, 0)
         gather(1, 0, 0, J)
-        round_x(0, 0, J)
-        gather(1, 1, 0, J)
+        round_x(0, 0, HALF)
+        round_x(0, HALF, J)
         quantise_x(0, 0, J)
+        gather(1, 1, 0, J)
         round_wu(1, 0)
         quantise_wu(1, 0)
         gather(1, 2, 0, J)

@@ -92,6 +92,7 @@ def tile_list_tanh_mix_scatb_kernel(
         second_rounded = arena.tile(
             [P, PASS], F32, name="second_rounded", offset=2 * PACK * PLANE_BYTES + 4 * PASS, align_bytes=64
         )
+        wu10_rounded = on_plane(0, 3, "wu10_rounded", [P, PACK * PASS], BF16)
         h_words = on_plane(0, 1, "h_words", [P, 2 * J], I32)
         wu_codes[1, 0] = on_plane(0, 2, "wu_codes10", [P, PASS], I32)
         wu_codes[0, 1] = on_plane(1, 2, "wu_codes01", [P, PASS], I32)
@@ -116,7 +117,7 @@ def tile_list_tanh_mix_scatb_kernel(
 
         def wu_rounded(a, s):
             if (a, s) == (1, 0):
-                return picked[1][:, 2 * J : 3 * J].bitcast(BF16)
+                return wu10_rounded[:]
             return rounded[3 if a == 0 else 2][:]
 
         def x_rounded(a, lo, hi):
@@ -186,8 +187,8 @@ def tile_list_tanh_mix_scatb_kernel(
                 out=packed[w * P // 2 : (w + 1) * P // 2, :],
                 in_=rows[0:P:GROUP, :].rearrange("g (b c) -> g b c", c=P),
             )
-        nc.sync.dma_start(pick_list[:], offs)
         load_x(0, 0)
+        nc.sync.dma_start(pick_list[:], offs)
         load_x(0, 1)
         load_x(0, 2)
         load_scale_rows(nc.sync, wg_sc_raw, wg_scales)

@@ -32,6 +32,8 @@ LAST_GATE = 6
 SLOTS = 4
 RUNS = J // P
 PLANE_BYTES = 4 * T
+SPARE = 2 * PACK * PLANE_BYTES
+WORDS_BYTES = 4 * PASS
 SCALE_SHIFT = 4
 
 
@@ -67,12 +69,10 @@ def tile_list_tanh_mix_scatb_kernel(
         bias = keep.tile([P, PAGES], F32, name="bias")
         no_bias = keep.tile([P, 1], F32, name="no_bias")
         wg_first = keep.tile([P, 2 * PASS], I32, name="wg_first", align_bytes=64)
-        wg_raw = {
-            (0, 0): wg_first[:, 0:PASS],
-            (1, 0): wg_first[:, PASS : 2 * PASS],
-            (0, 1): keep.tile([P, PASS], I32, name="wg_raw01", align_bytes=64)[:],
-            (1, 1): arena.tile([P, PASS], I32, name="wg_raw11", offset=2 * PACK * PLANE_BYTES, align_bytes=64)[:],
-        }
+        wg_second = [
+            keep.tile([P, PASS], I32, name="wg_raw01", align_bytes=64),
+            arena.tile([P, PASS], I32, name="wg_raw11", offset=SPARE, align_bytes=64),
+        ]
         wg_codes = [keep.tile([P, 2 * PASS], I32, name=f"wg_codes{s}", align_bytes=64) for s in range(2)]
         wg_sc_raw = keep.tile([P, R], U8, name="wg_sc_raw", align_bytes=64)
         wg_sc = keep.tile([P, R], U8, name="wg_sc", align_bytes=64)
@@ -81,17 +81,12 @@ def tile_list_tanh_mix_scatb_kernel(
         wd8_sc = keep.tile([P, N], U8, name="wd8_sc", align_bytes=64)
         wd4_sc = keep.tile([P, N], U8, name="wd4_sc", align_bytes=64)
         x0_codes = on_plane(0, 2, "x_codes0", [P, J], I32, PLANE_BYTES // 2)
-        x1_codes = {c: keep.tile([P, CHUNK], I32, name=f"x_codes1_{c}", align_bytes=64) for c in (0,)}
-        x1_codes[1] = keep.tile([P, CHUNK], I32, name="x_codes1_1", align_bytes=64)
+        x1_codes = [keep.tile([P, CHUNK], I32, name=f"x_codes1_{c}", align_bytes=64) for c in range(2)]
         x0_rounded = on_plane(0, 0, "x0_rounded", [P, PACK * J], BF16)
         x_sc = [keep.tile([P, J], U8, name=f"x_sc{a}", align_bytes=64) for a in range(2)]
         wu_codes = {(0, 0): keep.tile([P, PASS], I32, name="wu_codes00", align_bytes=64)}
-        wu_codes[1, 1] = arena.tile(
-            [P, PASS], I32, name="wu_codes11", offset=2 * PACK * PLANE_BYTES + 2 * PASS, align_bytes=64
-        )
-        second_rounded = arena.tile(
-            [P, PASS], F32, name="second_rounded", offset=2 * PACK * PLANE_BYTES + 4 * PASS, align_bytes=64
-        )
+        wu_codes[1, 1] = arena.tile([P, PASS], I32, name="wu_codes11", offset=SPARE + WORDS_BYTES // 2, align_bytes=64)
+        second_rounded = arena.tile([P, PASS], F32, name="second_rounded", offset=SPARE + WORDS_BYTES, align_bytes=64)
         wu10_rounded = on_plane(0, 3, "wu10_rounded", [P, PACK * PASS], BF16)
         h_words = on_plane(0, 1, "h_words", [P, 2 * J], I32)
         wu_codes[1, 0] = on_plane(0, 2, "wu_codes10", [P, PASS], I32)
@@ -104,10 +99,11 @@ def tile_list_tanh_mix_scatb_kernel(
             (1, 1): wu_sc_tiles[2][:],
         }
         h_sc_tiles = [keep.tile([P, J], U8, name=f"h_sc{c}", align_bytes=64) for c in range(2)]
-        rounded = [keep.tile([P, PACK * HALF], BF16, name=f"rounded{v}", align_bytes=64) for v in range(4) if v > 1]
-        rounded = {2: rounded[0], 3: rounded[1]}
-        first_h = on_plane(1, 3, "first_h", [P, PACK * HALF], BF16, PLANE_BYTES - 6 * PASS)
-        x1_late = on_plane(1, 3, "x1_late", [P, HALF], I32, PLANE_BYTES - 6 * PASS)
+        shared_rounded = keep.tile([P, PACK * HALF], BF16, name="rounded2", align_bytes=64)
+        wu0_rounded = keep.tile([P, PACK * PASS], BF16, name="rounded3", align_bytes=64)
+        first_h_skip = PLANE_BYTES - 3 * WORDS_BYTES // 2
+        first_h = on_plane(1, 3, "first_h", [P, PACK * HALF], BF16, first_h_skip)
+        x1_late = on_plane(1, 3, "x1_late", [P, HALF], I32, first_h_skip)
 
         repeated = picked[1]
         first_gated = wu_raw[1, 0]
@@ -116,22 +112,19 @@ def tile_list_tanh_mix_scatb_kernel(
         gated_slots, moved_slots = wu_raw[0, 0], wu_raw[0, 1]
 
         def wu_rounded(a, s):
-            if (a, s) == (1, 0):
-                return wu10_rounded[:]
-            return rounded[3 if a == 0 else 2][:]
+            if a == 0:
+                return wu0_rounded[:]
+            return (wu10_rounded, shared_rounded)[s][:]
 
         def x_rounded(a, lo, hi):
             if a == 0:
                 return x0_rounded[:, PACK * lo : PACK * hi]
-            places = {
-                (1, 0): picked[0][:, 0:PASS],
-                (1, CHUNK): second_rounded[:],
-                (1, HALF): rounded[2][:].bitcast(F32),
-            }
-            return places[a, lo].bitcast(BF16)
+            if lo >= HALF:
+                return shared_rounded[:, PACK * (lo - HALF) : PACK * (hi - HALF)]
+            return (picked[0][:, 0:PASS] if lo == 0 else second_rounded[:]).bitcast(BF16)
 
         def h_rounded(chunk):
-            return first_h[:] if chunk == 0 else rounded[2][:]
+            return first_h[:] if chunk == 0 else shared_rounded[:]
 
         def h_codes(chunk):
             cols = slice(chunk % 2 * 2 * CHUNK, (chunk % 2 + 1) * 2 * CHUNK)
@@ -160,9 +153,9 @@ def tile_list_tanh_mix_scatb_kernel(
             words = wg_words[:, :, 0:PASS, :].rearrange("a p r i -> p a (r i)")
             nc.sync.dma_start(out=wg_first[:].rearrange("p (a r) -> p a r", a=2), in_=words.bitcast(I32))
 
-        def load_wg(a, s):
-            words = wg_words[a, :, s * PASS : (s + 1) * PASS, :].rearrange("p r i -> p (r i)")
-            nc.sync.dma_start(out=wg_raw[a, s], in_=words.bitcast(I32))
+        def load_wg_second(a):
+            words = wg_words[a, :, PASS:R, :].rearrange("p r i -> p (r i)")
+            nc.sync.dma_start(out=wg_second[a][:], in_=words.bitcast(I32))
 
         def load_scale_rows(queue, tile, rows):
             passes = rows.shape[0]
@@ -203,8 +196,8 @@ def tile_list_tanh_mix_scatb_kernel(
         load_x(1, 3)
         load_wg_first()
         load_wu_last(1)
-        load_wg(0, 1)
-        load_wg(1, 1)
+        load_wg_second(0)
+        load_wg_second(1)
         nc.sync.dma_start(out=wd8_codes[:], in_=wd8_words[0].rearrange("p n i -> p (n i)").bitcast(I32))
         nc.sync.dma_start(out=wd4_codes[:].bitcast(I32), in_=wd4_words[0].bitcast(I32))
         with nc.allow_non_contiguous_dma(reason="one bias value for each partition and page"):
@@ -242,13 +235,13 @@ def tile_list_tanh_mix_scatb_kernel(
                 MULT,
             )
 
-        def round_x(a, lo, hi, copy=nc.scalar.copy):
-            copy(
+        def round_x(a, lo, hi):
+            nc.scalar.copy(
                 out=x_rounded(a, lo, hi).rearrange("p (g e i) -> p g i e", e=4, i=PACK),
                 in_=picks(a, lo, hi).rearrange("p i (g e) -> p g i e", e=4),
             )
 
-        def round_on_gpsimd(a, lo, hi):
+        def round_x_on_gpsimd(a, lo, hi):
             nc.gpsimd.tensor_scalar(
                 x_rounded(a, lo, hi).rearrange("p (j i) -> p j i", i=PACK),
                 picks(a, lo, hi).rearrange("p i j -> p j i"),
@@ -325,8 +318,8 @@ def tile_list_tanh_mix_scatb_kernel(
             step = 4 * chunk + quarter
 
             def wg_stationary(a, t):
-                first = s * PASS + t * P
-                return wg_codes[s][:, a * PASS + t * P : a * PASS + (t + 1) * P], wg_sc[SCALE_SHIFT * a :, first : first + P]
+                word, scale = a * PASS + t * P, s * PASS + t * P
+                return wg_codes[s][:, word : word + P], wg_sc[SCALE_SHIFT * a :, scale : scale + P]
 
             def wu_stationary(a, t):
                 return wu_codes[a, s][:, t * P : (t + 1) * P], wu_sc[a, s][:, t * P : (t + 1) * P]
@@ -449,11 +442,12 @@ def tile_list_tanh_mix_scatb_kernel(
         round_x(1, CHUNK, HALF)
         round_wu_last(1, nc.vector.tensor_copy)
         quantise_x(1, CHUNK, HALF)
-        deal_wg_words(wg_codes[1][:, 0:PASS], wg_raw[0, 1])
-        deal_wg_words(wg_codes[1][:, PASS : 2 * PASS], wg_raw[1, 1])
+        for a in range(2):
+            deal_wg_words(wg_codes[1][:, a * PASS : (a + 1) * PASS], wg_second[a][:])
         quantise_wu(1, 1)
-        round_on_gpsimd(1, HALF, J)
+        round_x_on_gpsimd(1, HALF, J - UNIT)
         hidden_chunk(0)
+        round_x(1, J - UNIT, J)
         quantise_x(1, HALF, J)
 
         sums = [output_sums(0, 0, bank_a, 0), output_sums(0, 1, bank_c, 0)]
@@ -481,7 +475,7 @@ def tile_list_tanh_mix_scatb_kernel(
         last_slot = (SLOTS - 1) * PASS
         scatter_fused(2, 2, sums[2], moved_slots[:, last_slot : last_slot + CHUNK])
 
-        staged = [last_staged[:, n * CHUNK : (n + 1) * CHUNK] for n in range(PAGES)]
+        staged = [last_staged[:, n * CHUNK : (n + 1) * CHUNK] for n in range(PAGES - 1)]
         for n, bank in enumerate((bank_b, banks[0])):
             scatter_fused(3, n, output_sums(3, n, bank, 0), staged[n])
             store(n)

@@ -99,7 +99,8 @@ def tile_list_tanh_mix_scatb_kernel(
             (1, 1): wu_sc_tiles[2][:],
         }
         h_sc_tiles = [keep.tile([P, J], U8, name=f"h_sc{c}", align_bytes=64) for c in range(2)]
-        shared_rounded = keep.tile([P, PACK * HALF], BF16, name="rounded2", align_bytes=64)
+        shared = keep.tile([P, PACK * (HALF + UNIT)], BF16, name="shared", align_bytes=64)
+        wu11_rounded, late_rounded = shared[:, 0 : PACK * PASS], shared[:, PACK * UNIT :]
         wu0_rounded = keep.tile([P, PACK * PASS], BF16, name="rounded3", align_bytes=64)
         first_h_skip = PLANE_BYTES - 3 * WORDS_BYTES // 2
         first_h = on_plane(1, 3, "first_h", [P, PACK * HALF], BF16, first_h_skip)
@@ -114,17 +115,17 @@ def tile_list_tanh_mix_scatb_kernel(
         def wu_rounded(a, s):
             if a == 0:
                 return wu0_rounded[:]
-            return (wu10_rounded, shared_rounded)[s][:]
+            return (wu10_rounded[:], wu11_rounded)[s]
 
         def x_rounded(a, lo, hi):
             if a == 0:
                 return x0_rounded[:, PACK * lo : PACK * hi]
             if lo >= HALF:
-                return shared_rounded[:, PACK * (lo - HALF) : PACK * (hi - HALF)]
+                return late_rounded[:, PACK * (lo - HALF) : PACK * (hi - HALF)]
             return (picked[0][:, 0:PASS] if lo == 0 else second_rounded[:]).bitcast(BF16)
 
         def h_rounded(chunk):
-            return first_h[:] if chunk == 0 else shared_rounded[:]
+            return first_h[:] if chunk == 0 else late_rounded
 
         def h_codes(chunk):
             cols = slice(chunk % 2 * 2 * CHUNK, (chunk % 2 + 1) * 2 * CHUNK)
@@ -440,6 +441,7 @@ def tile_list_tanh_mix_scatb_kernel(
         round_x(1, 0, CHUNK)
         quantise_x(1, 0, CHUNK)
         round_x(1, CHUNK, HALF)
+        round_x(1, J - UNIT, J)
         round_wu_last(1, nc.vector.tensor_copy)
         quantise_x(1, CHUNK, HALF)
         for a in range(2):
@@ -447,7 +449,6 @@ def tile_list_tanh_mix_scatb_kernel(
         quantise_wu(1, 1)
         round_x_on_gpsimd(1, HALF, J - UNIT)
         hidden_chunk(0)
-        round_x(1, J - UNIT, J)
         quantise_x(1, HALF, J)
 
         sums = [output_sums(0, 0, bank_a, 0), output_sums(0, 1, bank_c, 0)]

@@ -75,7 +75,7 @@ def tile_list_tanh_mix_scatb_kernel(
         ]
         wg_codes = [keep.tile([P, 2 * PASS], I32, name=f"wg_codes{s}", align_bytes=64) for s in range(2)]
         wg_sc_raw = keep.tile([P, R], U8, name="wg_sc_raw", align_bytes=64)
-        wg_sc = keep.tile([P, R], U8, name="wg_sc", align_bytes=64)
+        wg_sc = on_plane(1, 2, "wg_sc", [P, R], U8, WORDS_BYTES)
         wd8_codes = keep.tile([P, N], I32, name="wd8_codes", align_bytes=64)
         wd4_codes = keep.tile([P, 2 * N], U8, name="wd4_codes", align_bytes=64)
         wd8_sc = keep.tile([P, N], U8, name="wd8_sc", align_bytes=64)
@@ -84,7 +84,7 @@ def tile_list_tanh_mix_scatb_kernel(
         x1_codes = [keep.tile([P, CHUNK], I32, name=f"x_codes1_{c}", align_bytes=64) for c in range(2)]
         x0_rounded = on_plane(0, 0, "x0_rounded", [P, PACK * J], BF16)
         x_sc = [keep.tile([P, J], U8, name=f"x_sc{a}", align_bytes=64) for a in range(2)]
-        wu_codes = {(0, 0): keep.tile([P, PASS], I32, name="wu_codes00", align_bytes=64)}
+        wu_codes = {(0, 0): on_plane(1, 1, "wu_codes00", [P, PASS], I32)}
         wu_codes[1, 1] = arena.tile([P, PASS], I32, name="wu_codes11", offset=SPARE + WORDS_BYTES // 2, align_bytes=64)
         second_rounded = arena.tile([P, PASS], F32, name="second_rounded", offset=SPARE + WORDS_BYTES, align_bytes=64)
         wu10_rounded = on_plane(0, 3, "wu10_rounded", [P, PACK * PASS], BF16)
@@ -99,8 +99,9 @@ def tile_list_tanh_mix_scatb_kernel(
             (1, 1): wu_sc_tiles[2][:],
         }
         h_sc_tiles = [keep.tile([P, J], U8, name=f"h_sc{c}", align_bytes=64) for c in range(2)]
-        shared = keep.tile([P, PACK * (HALF + UNIT)], BF16, name="shared", align_bytes=64)
-        wu11_rounded, late_rounded = shared[:, 0 : PACK * PASS], shared[:, PACK * UNIT :]
+        shared = keep.tile([P, PACK * (HALF + CHUNK)], BF16, name="shared", align_bytes=64)
+        wu11_rounded, late_rounded = shared[:, 0 : PACK * PASS], shared[:, PACK * UNIT : PACK * (HALF + UNIT)]
+        third_gated = shared[:, PACK * HALF :].bitcast(F32)
         wu0_rounded = keep.tile([P, PACK * PASS], BF16, name="rounded3", align_bytes=64)
         first_h_skip = PLANE_BYTES - 3 * WORDS_BYTES // 2
         first_h = on_plane(1, 3, "first_h", [P, PACK * HALF], BF16, first_h_skip)
@@ -122,7 +123,7 @@ def tile_list_tanh_mix_scatb_kernel(
                 return x0_rounded[:, PACK * lo : PACK * hi]
             if lo >= HALF:
                 return late_rounded[:, PACK * (lo - HALF) : PACK * (hi - HALF)]
-            return (picked[0][:, 0:PASS] if lo == 0 else second_rounded[:]).bitcast(BF16)
+            return (picked[1][:, PACK * J - HALF :] if lo == 0 else second_rounded[:]).bitcast(BF16)
 
         def h_rounded(chunk):
             return first_h[:] if chunk == 0 else late_rounded
@@ -169,6 +170,7 @@ def tile_list_tanh_mix_scatb_kernel(
         make_identity(nc, identity[:])
         nc.gpsimd.memset(wg_sc_raw[:].bitcast(I32), 0)
         nc.gpsimd.memset(no_bias[:], 0.0)
+        load_scale_rows(nc.gpsimd, wg_sc_raw, wg_scales)
         for page in pages:
             nc.gpsimd.memset(page[:], 0.0)
         for tile in (wd8_sc, wd4_sc):
@@ -185,14 +187,13 @@ def tile_list_tanh_mix_scatb_kernel(
         nc.sync.dma_start(pick_list[:], offs)
         load_x(0, 1)
         load_x(0, 2)
-        load_scale_rows(nc.sync, wg_sc_raw, wg_scales)
-        load_wu(0, 0)
         load_x(0, 3)
+        load_wu(0, 0)
         load_x(1, 0)
-        load_wu(1, 0)
         load_x(1, 1)
-        load_wu(0, 1)
+        load_wu(1, 0)
         load_x(1, 2)
+        load_wu(0, 1)
         load_wu_last(0)
         load_x(1, 3)
         load_wg_first()
@@ -326,7 +327,7 @@ def tile_list_tanh_mix_scatb_kernel(
                 return wu_codes[a, s][:, t * P : (t + 1) * P], wu_sc[a, s][:, t * P : (t + 1) * P]
 
             slot = slice(step % SLOTS * PASS, (step % SLOTS + 1) * PASS)
-            gated = (gated_slots if chunk > 0 else first_gated)[:, slot]
+            gated = third_gated if step == 2 else (gated_slots if chunk > 0 else first_gated)[:, slot]
             gate = first_products(2 * step, u, wg_stationary)
             nc.scalar.activation(
                 out=gated.rearrange("p (j t) -> p j t", t=PACK), in_=gate, func=ACT.Tanh, bias=no_bias[:]
@@ -416,39 +417,39 @@ def tile_list_tanh_mix_scatb_kernel(
 
         spread_weights()
         for i in range(PACK):
-            if i in (0, PACK - 1):
+            if i == 0:
                 gather(0, i, 0, HALF)
                 gather(0, i, HALF, J)
             else:
                 gather(0, i, 0, J)
-        deal_wg_scales()
         round_wu(0, 0)
-        quantise_wu(0, 0)
+        round_x(0, 0, J)
         gather(1, 0, 0, J)
-        round_x(0, 0, HALF)
-        round_x(0, HALF, J)
-        quantise_x(0, 0, J)
         gather(1, 1, 0, J)
+        quantise_wu(0, 0)
+        quantise_x(0, 0, J)
         round_wu(1, 0)
-        quantise_wu(1, 0)
         gather(1, 2, 0, J)
+        quantise_wu(1, 0)
+        deal_wg_scales()
         round_wu(0, 1)
         quantise_wu(0, 1)
         round_wu_last(0, nc.scalar.copy)
-        gather(1, 3, 0, HALF)
+        gather(1, 3, 0, CHUNK)
+        gather(1, 3, CHUNK, HALF)
         deal_wg_words(wg_codes[0][:], wg_first[:])
-        gather(1, 3, HALF, J)
         round_x(1, 0, CHUNK)
         quantise_x(1, 0, CHUNK)
+        gather(1, 3, HALF, J)
         round_x(1, CHUNK, HALF)
-        round_x(1, J - UNIT, J)
-        round_wu_last(1, nc.vector.tensor_copy)
+        round_wu_last(1, nc.scalar.copy)
         quantise_x(1, CHUNK, HALF)
         for a in range(2):
             deal_wg_words(wg_codes[1][:, a * PASS : (a + 1) * PASS], wg_second[a][:])
         quantise_wu(1, 1)
         round_x_on_gpsimd(1, HALF, J - UNIT)
         hidden_chunk(0)
+        round_x(1, J - UNIT, J)
         quantise_x(1, HALF, J)
 
         sums = [output_sums(0, 0, bank_a, 0), output_sums(0, 1, bank_c, 0)]

@@ -60,7 +60,7 @@ def tile_list_tanh_mix_scatb_kernel(
 
         pages = [keep.tile([P, T], F32, name=f"page{n}") for n in range(PAGES)]
         picked = [keep.tile([P, PACK * J], F32, name=f"picked{a}", align_bytes=64) for a in range(2)]
-        wu_raw = {(a, s): keep.tile([P, PACK * PASS], F32, name=f"wu_raw{a}{s}") for a, s in ((0, 0), (0, 1), (1, 0))}
+        wu_raw = {(a, s): keep.tile([P, PACK * PASS], F32, name=f"wu_raw{a}{s}", align_bytes=64) for a, s in ((0, 0), (0, 1), (1, 0))}
         wu_last = [keep.tile([P, PACK * PASS // 2], F32, name=f"wu_last{v}") for v in range(2)]
         weights = keep.tile([P, 2 * J], F32, name="weights")
         wgt_sb, wgo_sb = weights[:, 0:J], weights[:, J : 2 * J]
@@ -69,10 +69,7 @@ def tile_list_tanh_mix_scatb_kernel(
         bias = keep.tile([P, PAGES], F32, name="bias")
         no_bias = keep.tile([P, 1], F32, name="no_bias")
         wg_first = keep.tile([P, 2 * PASS], I32, name="wg_first", align_bytes=64)
-        wg_second = [
-            keep.tile([P, PASS], I32, name="wg_raw01", align_bytes=64),
-            arena.tile([P, PASS], I32, name="wg_raw11", offset=SPARE, align_bytes=64),
-        ]
+        wg_second = arena.tile([P, 2 * PASS], I32, name="wg_second", offset=SPARE, align_bytes=64)
         wg_codes = [keep.tile([P, 2 * PASS], I32, name=f"wg_codes{s}", align_bytes=64) for s in range(2)]
         wg_sc_raw = keep.tile([P, R], U8, name="wg_sc_raw", align_bytes=64)
         wg_sc = on_plane(1, 2, "wg_sc", [P, R], U8, WORDS_BYTES)
@@ -82,15 +79,15 @@ def tile_list_tanh_mix_scatb_kernel(
         wd4_sc = keep.tile([P, N], U8, name="wd4_sc", align_bytes=64)
         x0_codes = on_plane(0, 2, "x_codes0", [P, J], I32, PLANE_BYTES // 2)
         x1_codes = [keep.tile([P, CHUNK], I32, name=f"x_codes1_{c}", align_bytes=64) for c in range(2)]
-        x0_rounded = on_plane(0, 0, "x0_rounded", [P, PACK * J], BF16)
+        x0_rounded = wu_raw[0, 0][:].bitcast(BF16)
         x_sc = [keep.tile([P, J], U8, name=f"x_sc{a}", align_bytes=64) for a in range(2)]
-        wu_codes = {(0, 0): on_plane(1, 1, "wu_codes00", [P, PASS], I32)}
-        wu_codes[1, 1] = arena.tile([P, PASS], I32, name="wu_codes11", offset=SPARE + WORDS_BYTES // 2, align_bytes=64)
-        second_rounded = arena.tile([P, PASS], F32, name="second_rounded", offset=SPARE + WORDS_BYTES, align_bytes=64)
+        wu_codes = {(0, 0): keep.tile([P, PASS], I32, name="wu_codes00", align_bytes=64)}
+        wu_codes[1, 1] = keep.tile([P, PASS], I32, name="wu_codes11", align_bytes=64)
+        second_rounded = arena.tile([P, PASS], F32, name="second_rounded", offset=SPARE + 2 * WORDS_BYTES, align_bytes=64)
         wu10_rounded = on_plane(0, 3, "wu10_rounded", [P, PACK * PASS], BF16)
         h_words = on_plane(0, 1, "h_words", [P, 2 * J], I32)
         wu_codes[1, 0] = on_plane(0, 2, "wu_codes10", [P, PASS], I32)
-        wu_codes[0, 1] = on_plane(1, 2, "wu_codes01", [P, PASS], I32)
+        wu_codes[0, 1] = on_plane(1, 1, "wu_codes01", [P, PASS], I32)
         wu_sc_tiles = [keep.tile([P, PASS], U8, name=f"wu_sc{v}", align_bytes=64) for v in range(3)]
         wu_sc = {
             (0, 0): wu_sc_tiles[0][:],
@@ -99,19 +96,23 @@ def tile_list_tanh_mix_scatb_kernel(
             (1, 1): wu_sc_tiles[2][:],
         }
         h_sc_tiles = [keep.tile([P, J], U8, name=f"h_sc{c}", align_bytes=64) for c in range(2)]
-        shared = keep.tile([P, PACK * (HALF + CHUNK)], BF16, name="shared", align_bytes=64)
-        wu11_rounded, late_rounded = shared[:, 0 : PACK * PASS], shared[:, PACK * UNIT : PACK * (HALF + UNIT)]
-        third_gated = shared[:, PACK * HALF :].bitcast(F32)
+        wu11_rounded = arena.tile([P, PACK * PASS], BF16, name="wu11_rounded", offset=SPARE + 3 * WORDS_BYTES, align_bytes=64)[:]
+        shared = arena.tile([P, PACK * (HALF + UNIT)], BF16, name="shared", offset=SPARE + 3 * WORDS_BYTES // 2, align_bytes=64)
+        late_rounded = shared[:, 0 : PACK * HALF]
+        third_gated = shared[:, PACK * (HALF - UNIT) :].bitcast(F32)
         wu0_rounded = keep.tile([P, PACK * PASS], BF16, name="rounded3", align_bytes=64)
         first_h_skip = PLANE_BYTES - 3 * WORDS_BYTES // 2
         first_h = on_plane(1, 3, "first_h", [P, PACK * HALF], BF16, first_h_skip)
         x1_late = on_plane(1, 3, "x1_late", [P, HALF], I32, first_h_skip)
 
         repeated = picked[1]
-        first_gated = wu_raw[1, 0]
+        first_gated = wu_last[1][:, 0:PASS], wu_last[1][:, PASS:], third_gated, wu_raw[1, 0][:, 0:PASS]
         last_staged = picked[1]
         early_staged = picked[0][:, 2 * J : 4 * J]
         gated_slots, moved_slots = wu_raw[0, 0], wu_raw[0, 1]
+
+        def held_place(chunk):
+            return picked[0][:, chunk * PASS : (chunk + 1) * PASS]
 
         def wu_rounded(a, s):
             if a == 0:
@@ -151,13 +152,10 @@ def tile_list_tanh_mix_scatb_kernel(
                 in_=wu[PASS : 2 * PASS, cols].rearrange("(p i) r -> p i r", i=PACK),
             )
 
-        def load_wg_first():
-            words = wg_words[:, :, 0:PASS, :].rearrange("a p r i -> p a (r i)")
-            nc.sync.dma_start(out=wg_first[:].rearrange("p (a r) -> p a r", a=2), in_=words.bitcast(I32))
-
-        def load_wg_second(a):
-            words = wg_words[a, :, PASS:R, :].rearrange("p r i -> p (r i)")
-            nc.sync.dma_start(out=wg_second[a][:], in_=words.bitcast(I32))
+        def load_wg(s):
+            words = wg_words[:, :, s * PASS : (s + 1) * PASS, :].rearrange("a p r i -> p a (r i)")
+            tile = (wg_first, wg_second)[s]
+            nc.sync.dma_start(out=tile[:].rearrange("p (a r) -> p a r", a=2), in_=words.bitcast(I32))
 
         def load_scale_rows(queue, tile, rows):
             passes = rows.shape[0]
@@ -196,10 +194,9 @@ def tile_list_tanh_mix_scatb_kernel(
         load_wu(0, 1)
         load_wu_last(0)
         load_x(1, 3)
-        load_wg_first()
+        load_wg(0)
+        load_wg(1)
         load_wu_last(1)
-        load_wg_second(0)
-        load_wg_second(1)
         nc.sync.dma_start(out=wd8_codes[:], in_=wd8_words[0].rearrange("p n i -> p (n i)").bitcast(I32))
         nc.sync.dma_start(out=wd4_codes[:].bitcast(I32), in_=wd4_words[0].bitcast(I32))
         with nc.allow_non_contiguous_dma(reason="one bias value for each partition and page"):
@@ -327,7 +324,7 @@ def tile_list_tanh_mix_scatb_kernel(
                 return wu_codes[a, s][:, t * P : (t + 1) * P], wu_sc[a, s][:, t * P : (t + 1) * P]
 
             slot = slice(step % SLOTS * PASS, (step % SLOTS + 1) * PASS)
-            gated = third_gated if step == 2 else (gated_slots if chunk > 0 else first_gated)[:, slot]
+            gated = first_gated[quarter] if chunk == 0 else gated_slots[:, slot]
             gate = first_products(2 * step, u, wg_stationary)
             nc.scalar.activation(
                 out=gated.rearrange("p (j t) -> p j t", t=PACK), in_=gate, func=ACT.Tanh, bias=no_bias[:]
@@ -342,7 +339,7 @@ def tile_list_tanh_mix_scatb_kernel(
                     MULT,
                 )
             else:
-                moved = moved_slots[:, slot]
+                moved = held_place(1) if (chunk, quarter) == (2, 3) else moved_slots[:, slot]
                 nc.scalar.copy(out=moved.rearrange("p (j t) -> p j t", t=PACK), in_=up)
                 nc.gpsimd.tensor_tensor(product, moved, gated, MULT)
 
@@ -356,26 +353,25 @@ def tile_list_tanh_mix_scatb_kernel(
             codes, scales = h_codes(chunk)
             rows = slice(n * P, (n + 1) * P)
             acc = bank[:, side * CHUNK : (side + 1) * CHUNK]
-            for first in range(0, CHUNK, UNIT):
-                below, above = slice(first, first + UNIT), slice(CHUNK + first, CHUNK + first + UNIT)
-                nc.tensor.matmul_mx(
-                    out=acc[:, below],
-                    lhsT=wd8_codes[:, rows].bitcast(FP8X4),
-                    lhsT_scale=wd8_sc[:, rows],
-                    rhs=codes[:, below].bitcast(FP8X4),
-                    rhs_scale=scales[:, below],
-                    start=True,
-                    stop=False,
-                )
-                nc.tensor.matmul_mx(
-                    out=acc[:, below],
-                    lhsT=wd4_codes[:, 2 * n * P : 2 * (n + 1) * P].bitcast(FP4X4),
-                    lhsT_scale=wd4_sc[:, rows],
-                    rhs=codes[:, above].bitcast(FP8X4),
-                    rhs_scale=scales[:, above],
-                    start=False,
-                    stop=True,
-                )
+            below, above = slice(0, CHUNK), slice(CHUNK, 2 * CHUNK)
+            nc.tensor.matmul_mx(
+                out=acc,
+                lhsT=wd8_codes[:, rows].bitcast(FP8X4),
+                lhsT_scale=wd8_sc[:, rows],
+                rhs=codes[:, below].bitcast(FP8X4),
+                rhs_scale=scales[:, below],
+                start=True,
+                stop=False,
+            )
+            nc.tensor.matmul_mx(
+                out=acc,
+                lhsT=wd4_codes[:, 2 * n * P : 2 * (n + 1) * P].bitcast(FP4X4),
+                lhsT_scale=wd4_sc[:, rows],
+                rhs=codes[:, above].bitcast(FP8X4),
+                rhs_scale=scales[:, above],
+                start=False,
+                stop=True,
+            )
             return acc
 
         def places(chunk, n):
@@ -404,7 +400,7 @@ def tile_list_tanh_mix_scatb_kernel(
             scatter(chunk, n, staged)
 
         def scatter_held(chunk, n, acc):
-            staged = h_rounded(chunk + 1).bitcast(F32)[:, n * CHUNK : (n + 1) * CHUNK]
+            staged = held_place(chunk)[:, (n - 2) * CHUNK : (n - 1) * CHUNK]
             weigh_on_vector(chunk, n, acc, staged)
             scatter(chunk, n, staged)
 
@@ -424,9 +420,9 @@ def tile_list_tanh_mix_scatb_kernel(
                 gather(0, i, 0, J)
         round_wu(0, 0)
         round_x(0, 0, J)
+        quantise_wu(0, 0)
         gather(1, 0, 0, J)
         gather(1, 1, 0, J)
-        quantise_wu(0, 0)
         quantise_x(0, 0, J)
         round_wu(1, 0)
         gather(1, 2, 0, J)
@@ -444,8 +440,7 @@ def tile_list_tanh_mix_scatb_kernel(
         round_x(1, CHUNK, HALF)
         round_wu_last(1, nc.scalar.copy)
         quantise_x(1, CHUNK, HALF)
-        for a in range(2):
-            deal_wg_words(wg_codes[1][:, a * PASS : (a + 1) * PASS], wg_second[a][:])
+        deal_wg_words(wg_codes[1][:], wg_second[:])
         quantise_wu(1, 1)
         round_x_on_gpsimd(1, HALF, J - UNIT)
         hidden_chunk(0)

@@ -75,8 +75,8 @@ def tile_list_tanh_mix_scatb_kernel(
         wg_sc = on_plane(1, 2, "wg_sc", [P, R], U8, WORDS_BYTES)
         wd8_codes = keep.tile([P, N], I32, name="wd8_codes", align_bytes=64)
         wd4_codes = keep.tile([P, 2 * N], U8, name="wd4_codes", align_bytes=64)
-        wd8_sc = keep.tile([P, N], U8, name="wd8_sc", align_bytes=64)
-        wd4_sc = keep.tile([P, N], U8, name="wd4_sc", align_bytes=64)
+        wd_sc = keep.tile([P, N], U8, name="wd_sc", align_bytes=64)
+        wd4_sc, wd8_sc = wd_sc[:], wd_sc[3 * SCALE_SHIFT :, :]
         x0_codes = on_plane(0, 2, "x_codes0", [P, J], I32, PLANE_BYTES // 2)
         x1_codes = [keep.tile([P, CHUNK], I32, name=f"x_codes1_{c}", align_bytes=64) for c in range(2)]
         x0_rounded = wu_raw[0, 0][:].bitcast(BF16)
@@ -97,7 +97,7 @@ def tile_list_tanh_mix_scatb_kernel(
         }
         h_sc_tiles = [keep.tile([P, J], U8, name=f"h_sc{c}", align_bytes=64) for c in range(2)]
         wu11_rounded = arena.tile([P, PACK * PASS], BF16, name="wu11_rounded", offset=SPARE + 3 * WORDS_BYTES, align_bytes=64)[:]
-        shared = arena.tile([P, PACK * (HALF + UNIT)], BF16, name="shared", offset=SPARE + 3 * WORDS_BYTES // 2, align_bytes=64)
+        shared = arena.tile([P, PACK * (HALF + UNIT)], BF16, name="shared", offset=SPARE + 3 * WORDS_BYTES // 2 + 64, align_bytes=64)
         late_rounded = shared[:, 0 : PACK * HALF]
         third_gated = shared[:, PACK * (HALF - UNIT) :].bitcast(F32)
         wu0_rounded = keep.tile([P, PACK * PASS], BF16, name="rounded3", align_bytes=64)
@@ -157,29 +157,28 @@ def tile_list_tanh_mix_scatb_kernel(
             tile = (wg_first, wg_second)[s]
             nc.sync.dma_start(out=tile[:].rearrange("p (a r) -> p a r", a=2), in_=words.bitcast(I32))
 
-        def load_scale_rows(queue, tile, rows):
+        def load_scale_rows(tile, shift, rows):
             passes = rows.shape[0]
             for q in range(4):
-                queue.dma_start(
-                    out=tile[32 * q : 32 * q + 4 * passes, :].bitcast(I32),
+                nc.gpsimd.dma_start(
+                    out=tile[32 * q + shift : 32 * q + shift + 4 * passes, :].bitcast(I32),
                     in_=rows[:, 4 * q : 4 * q + 4, :].bitcast(I32),
                 )
 
         make_identity(nc, identity[:])
         nc.gpsimd.memset(wg_sc_raw[:].bitcast(I32), 0)
         nc.gpsimd.memset(no_bias[:], 0.0)
-        load_scale_rows(nc.gpsimd, wg_sc_raw, wg_scales)
+        load_scale_rows(wg_sc_raw, SCALE_SHIFT, wg_scales)
         for page in pages:
             nc.gpsimd.memset(page[:], 0.0)
-        for tile in (wd8_sc, wd4_sc):
-            nc.gpsimd.memset(tile[:].bitcast(I32), 0)
-        load_scale_rows(nc.gpsimd, wd8_sc, wd8_scales)
-        load_scale_rows(nc.gpsimd, wd4_sc, wd4_scales)
+        nc.gpsimd.memset(wd_sc[:].bitcast(I32), 0)
+        load_scale_rows(wd_sc, 3 * SCALE_SHIFT, wd8_scales)
+        load_scale_rows(wd_sc, 0, wd4_scales)
 
         for w, rows in enumerate((wgt, wgo)):
             nc.sync.dma_start(
                 out=packed[w * P // 2 : (w + 1) * P // 2, :],
-                in_=rows[0:P:GROUP, :].rearrange("g (b c) -> g b c", c=P),
+                in_=rows.rearrange("p (h j) -> (p h) j", h=2)[0 : 2 * P : GROUP + 1].rearrange("x (b c) -> x b c", c=P),
             )
         load_x(0, 0)
         nc.sync.dma_start(pick_list[:], offs)
@@ -318,7 +317,7 @@ def tile_list_tanh_mix_scatb_kernel(
 
             def wg_stationary(a, t):
                 word, scale = a * PASS + t * P, s * PASS + t * P
-                return wg_codes[s][:, word : word + P], wg_sc[SCALE_SHIFT * a :, scale : scale + P]
+                return wg_codes[s][:, word : word + P], wg_sc[SCALE_SHIFT * (a + 1) :, scale : scale + P]
 
             def wu_stationary(a, t):
                 return wu_codes[a, s][:, t * P : (t + 1) * P], wu_sc[a, s][:, t * P : (t + 1) * P]

@@ -311,7 +311,7 @@ def tile_list_tanh_mix_scatb_kernel(
                     )
             return by_t.rearrange("p t j -> p j t")
 
-        def hidden(chunk, quarter):
+        def factors(chunk, quarter):
             s, u = quarter // 2, 2 * chunk + quarter % 2
             step = 4 * chunk + quarter
 
@@ -329,22 +329,17 @@ def tile_list_tanh_mix_scatb_kernel(
                 out=gated.rearrange("p (j t) -> p j t", t=PACK), in_=gate, func=ACT.Tanh, bias=no_bias[:]
             )
             up = first_products(2 * step + 1, u, wu_stationary)
-            product = h_rounded(chunk)[:, quarter * PACK * UNIT : (quarter + 1) * PACK * UNIT]
             if chunk == 0 or (chunk, quarter) == (1, 3):
-                nc.vector.tensor_tensor(
-                    product.rearrange("p (j t) -> p j t", t=PACK),
-                    up,
-                    gated.rearrange("p (j t) -> p j t", t=PACK),
-                    MULT,
-                )
-            else:
-                moved = held_place(1) if (chunk, quarter) == (2, 3) else moved_slots[:, slot]
-                nc.scalar.copy(out=moved.rearrange("p (j t) -> p j t", t=PACK), in_=up)
-                nc.gpsimd.tensor_tensor(product, moved, gated, MULT)
+                return nc.vector, up, gated.rearrange("p (j t) -> p j t", t=PACK)
+            moved = held_place(1) if (chunk, quarter) == (2, 3) else moved_slots[:, slot]
+            nc.scalar.copy(out=moved.rearrange("p (j t) -> p j t", t=PACK), in_=up)
+            return nc.gpsimd, moved.rearrange("p (j t) -> p j t", t=PACK), gated.rearrange("p (j t) -> p j t", t=PACK)
 
-        def hidden_chunk(chunk):
+        def hidden_chunk(chunk, ahead=()):
             for quarter in range(4):
-                hidden(chunk, quarter)
+                engine, up, gated = ahead[quarter] if quarter < len(ahead) else factors(chunk, quarter)
+                product = h_rounded(chunk)[:, quarter * PACK * UNIT : (quarter + 1) * PACK * UNIT]
+                engine.tensor_tensor(product.rearrange("p (j t) -> p j t", t=PACK), up, gated, MULT)
             codes, scales = h_codes(chunk)
             nc.vector.quantize_mx(out=codes.bitcast(FP8X4), scales=scales, in_=h_rounded(chunk))
 
@@ -394,14 +389,18 @@ def tile_list_tanh_mix_scatb_kernel(
 
         def scatter_by_gpsimd(chunk, n, acc):
             staged = early_place(chunk, n)
-            add_bias(n, acc, staged)
-            nc.gpsimd.tensor_tensor(staged, staged, wgo_of(chunk), MULT)
+            biased = late_rounded.bitcast(F32)[:, (2 + n) * CHUNK : (3 + n) * CHUNK]
+            add_bias(n, acc, biased)
+            nc.gpsimd.tensor_tensor(staged, biased, wgo_of(chunk), MULT)
             scatter(chunk, n, staged)
 
-        def scatter_held(chunk, n, acc):
-            staged = held_place(chunk)[:, (n - 2) * CHUNK : (n - 1) * CHUNK]
-            weigh_on_vector(chunk, n, acc, staged)
-            scatter(chunk, n, staged)
+        def scatter_held(chunk):
+            staged = {n: held_place(chunk)[:, (n - 2) * CHUNK : (n - 1) * CHUNK] for n in (2, 3)}
+            held = {n: output_sums(chunk, n, bank_b, n % 2) for n in (2, 3)}
+            for n in (2, 3):
+                weigh_on_vector(chunk, n, held[n], staged[n])
+            for n in (2, 3):
+                scatter(chunk, n, staged[n])
 
         def scatter_fused(chunk, n, acc, staged):
             add_bias(n, acc, staged)
@@ -452,22 +451,20 @@ def tile_list_tanh_mix_scatb_kernel(
         for n in range(2):
             scatter(0, n, early_place(0, n))
         hidden_chunk(1)
-        held = [output_sums(0, n, bank_b, n % 2) for n in (2, 3)]
-        for n in (2, 3):
-            scatter_held(0, n, held[n - 2])
+        scatter_held(0)
 
+        ahead = [factors(2, quarter) for quarter in range(2)]
         sums = [output_sums(1, n, bank_c, n) for n in range(2)]
         for n in range(2):
             scatter_by_gpsimd(1, n, sums[n])
-        hidden_chunk(2)
-        held = [output_sums(1, n, bank_b, n % 2) for n in (2, 3)]
-        for n in (2, 3):
-            scatter_held(1, n, held[n - 2])
+        hidden_chunk(2, ahead)
+        scatter_held(1)
 
+        ahead = [factors(3, quarter) for quarter in range(3)]
         sums = [output_sums(2, n, bank_c, n) for n in range(2)] + [output_sums(2, 2, bank_a, 0)]
         for n in range(2):
             scatter_by_gpsimd(2, n, sums[n])
-        hidden_chunk(3)
+        hidden_chunk(3, ahead)
         last_slot = (SLOTS - 1) * PASS
         scatter_fused(2, 2, sums[2], moved_slots[:, last_slot : last_slot + CHUNK])
 

from contextlib import ExitStack

import concourse.mybir as mybir
from concourse.masks import make_identity

K, R, N, T, J = 1024, 1024, 512, 2048, 1024
FLOPS = 2 * J * (2 * K * R + R * N)

F32 = mybir.dt.float32
BF16 = mybir.dt.bfloat16
I32 = mybir.dt.int32
U16 = mybir.dt.uint16
U8 = mybir.dt.uint8
FP8X4 = mybir.dt.float8_e4m3fn_x4
FP4X4 = mybir.dt.float4_e2m1fn_x4
MULT = mybir.AluOpType.mult
ADD = mybir.AluOpType.add
ACT = mybir.ActivationFunctionType

P = 128
PACK = 4
PASS = P * PACK
GROUP = 16
GROUPS = P // GROUP
HALF = J // 2
UNIT = 128
PAGES = N // P
CHUNK = 2 * UNIT
BANKS = 8
SUM_BANKS = 5
LAST_GATE = 6
SLOTS = 4
RUNS = J // P
PLANE_BYTES = 4 * T
SPARE = 2 * PACK * PLANE_BYTES
WORDS_BYTES = 4 * PASS
SCALE_SHIFT = 4


def tile_list_tanh_mix_scatb_kernel(
    tc, xT, wgt, wg_words, wg_scales, wu, wd8_words, wd8_scales, wd4_words, wd4_scales, b, wgo, offs, offs2, out
):
    nc = tc.nc
    with ExitStack() as ctx:
        keep = ctx.enter_context(tc.tile_pool(name="keep", bufs=1))
        arena = ctx.enter_context(tc.tile_pool(name="arena", bufs=1))
        psum = ctx.enter_context(tc.psum_pool(name="psum", bufs=1))
        banks = [psum.tile([P, PASS], F32, name=f"bank{v}") for v in range(BANKS)]
        bank_a, bank_b, bank_c = banks[SUM_BANKS:]

        pick_list = keep.tile([P, J // GROUP], U16, name="pick_list")
        place_list = keep.tile([P, J // GROUP], U16, name="place_list")
        planes = [
            [arena.tile([P, T], F32, name=f"x{a}{i}", offset=(PACK * a + i) * PLANE_BYTES) for i in range(PACK)]
            for a in range(2)
        ]

        def on_plane(a, i, name, shape, dtype, skip=0):
            return arena.tile(shape, dtype, name=name, offset=(PACK * a + i) * PLANE_BYTES + skip, align_bytes=64)

        pages = [keep.tile([P, T], F32, name=f"page{n}") for n in range(PAGES)]
        picked = [keep.tile([P, PACK * J], F32, name=f"picked{a}", align_bytes=64) for a in range(2)]
        wu_raw = {(a, s): keep.tile([P, PACK * PASS], F32, name=f"wu_raw{a}{s}", align_bytes=64) for a, s in ((0, 0), (0, 1), (1, 0))}
        wu_last = [keep.tile([P, PACK * PASS // 2], F32, name=f"wu_last{v}") for v in range(2)]
        weights = keep.tile([P, 2 * J], F32, name="weights")
        wgt_sb, wgo_sb = weights[:, 0:J], weights[:, J : 2 * J]
        packed = keep.tile([P, P], F32, name="packed")
        identity = keep.tile([P, P], F32, name="identity")
        bias = keep.tile([P, PAGES], F32, name="bias")
        no_bias = keep.tile([P, 1], F32, name="no_bias")
        wg_first = keep.tile([P, 2 * PASS], I32, name="wg_first", align_bytes=64)
        wg_second = arena.tile([P, 2 * PASS], I32, name="wg_second", offset=SPARE, align_bytes=64)
        wg_codes = [keep.tile([P, 2 * PASS], I32, name=f"wg_codes{s}", align_bytes=64) for s in range(2)]
        wg_sc_raw = keep.tile([P, R], U8, name="wg_sc_raw", align_bytes=64)
        wg_sc = on_plane(1, 2, "wg_sc", [P, R], U8, WORDS_BYTES)
        wd8_codes = keep.tile([P, N], I32, name="wd8_codes", align_bytes=64)
        wd4_codes = keep.tile([P, 2 * N], U8, name="wd4_codes", align_bytes=64)
        wd_sc = keep.tile([P, N], U8, name="wd_sc", align_bytes=64)
        wd4_sc, wd8_sc = wd_sc[:], wd_sc[3 * SCALE_SHIFT :, :]
        x0_codes = on_plane(0, 2, "x_codes0", [P, J], I32, PLANE_BYTES // 2)
        x1_codes = [keep.tile([P, CHUNK], I32, name=f"x_codes1_{c}", align_bytes=64) for c in range(2)]
        x0_rounded = wu_raw[0, 0][:].bitcast(BF16)
        x_sc = [keep.tile([P, J], U8, name=f"x_sc{a}", align_bytes=64) for a in range(2)]
        wu_codes = {(0, 0): keep.tile([P, PASS], I32, name="wu_codes00", align_bytes=64)}
        wu_codes[1, 1] = keep.tile([P, PASS], I32, name="wu_codes11", align_bytes=64)
        second_rounded = arena.tile([P, PASS], F32, name="second_rounded", offset=SPARE + 2 * WORDS_BYTES, align_bytes=64)
        wu10_rounded = on_plane(0, 3, "wu10_rounded", [P, PACK * PASS], BF16)
        h_words = on_plane(0, 1, "h_words", [P, 2 * J], I32)
        wu_codes[1, 0] = on_plane(0, 2, "wu_codes10", [P, PASS], I32)
        wu_codes[0, 1] = on_plane(1, 1, "wu_codes01", [P, PASS], I32)
        wu_sc_tiles = [keep.tile([P, PASS], U8, name=f"wu_sc{v}", align_bytes=64) for v in range(3)]
        wu_sc = {
            (0, 0): wu_sc_tiles[0][:],
            (0, 1): wu_sc_tiles[0][SCALE_SHIFT:, :],
            (1, 0): wu_sc_tiles[1][:],
            (1, 1): wu_sc_tiles[2][:],
        }
        h_sc_tiles = [keep.tile([P, J], U8, name=f"h_sc{c}", align_bytes=64) for c in range(2)]
        wu11_rounded = arena.tile([P, PACK * PASS], BF16, name="wu11_rounded", offset=SPARE + 3 * WORDS_BYTES, align_bytes=64)[:]
        shared = arena.tile([P, PACK * (HALF + UNIT)], BF16, name="shared", offset=SPARE + 3 * WORDS_BYTES // 2 + 64, align_bytes=64)
        late_rounded = shared[:, 0 : PACK * HALF]
        third_gated = shared[:, PACK * (HALF - UNIT) :].bitcast(F32)
        wu0_rounded = keep.tile([P, PACK * PASS], BF16, name="rounded3", align_bytes=64)
        first_h_skip = PLANE_BYTES - 3 * WORDS_BYTES // 2
        first_h = on_plane(1, 3, "first_h", [P, PACK * HALF], BF16, first_h_skip)
        x1_late = on_plane(1, 3, "x1_late", [P, HALF], I32, first_h_skip)

        repeated = picked[1]
        first_gated = wu_last[1][:, 0:PASS], wu_last[1][:, PASS:], third_gated, wu_raw[1, 0][:, 0:PASS]
        last_staged = picked[1]
        early_staged = picked[0][:, 2 * J : 4 * J]
        gated_slots, moved_slots = wu_raw[0, 0], wu_raw[0, 1]

        def held_place(chunk):
            return picked[0][:, chunk * PASS : (chunk + 1) * PASS]

        def wu_rounded(a, s):
            if a == 0:
                return wu0_rounded[:]
            return (wu10_rounded[:], wu11_rounded)[s]

        def x_rounded(a, lo, hi):
            if a == 0:
                return x0_rounded[:, PACK * lo : PACK * hi]
            if lo >= HALF:
                return late_rounded[:, PACK * (lo - HALF) : PACK * (hi - HALF)]
            return (picked[1][:, PACK * J - HALF :] if lo == 0 else second_rounded[:]).bitcast(BF16)

        def h_rounded(chunk):
            return first_h[:] if chunk == 0 else late_rounded

        def h_codes(chunk):
            cols = slice(chunk % 2 * 2 * CHUNK, (chunk % 2 + 1) * 2 * CHUNK)
            return h_words[:, chunk * 2 * CHUNK : (chunk + 1) * 2 * CHUNK], h_sc_tiles[chunk // 2][:, cols]

        x_rows = xT.rearrange("(a p i) t -> a i p t", a=2, i=PACK)

        def load_x(a, i):
            nc.sync.dma_start(out=planes[a][i][:], in_=x_rows[a, i])

        def load_wu(a, s):
            cols = slice(s * PASS, (s + 1) * PASS)
            nc.sync.dma_start(
                out=wu_raw[a, s][:].rearrange("p (i r) -> p i r", i=PACK),
                in_=wu[a * PASS : (a + 1) * PASS, cols].rearrange("(p i) r -> p i r", i=PACK),
            )

        def load_wu_last(v):
            cols = slice(PASS + v * PASS // 2, PASS + (v + 1) * PASS // 2)
            nc.sync.dma_start(
                out=wu_last[v][:].rearrange("p (i r) -> p i r", i=PACK),
                in_=wu[PASS : 2 * PASS, cols].rearrange("(p i) r -> p i r", i=PACK),
            )

        def load_wg(s):
            words = wg_words[:, :, s * PASS : (s + 1) * PASS, :].rearrange("a p r i -> p a (r i)")
            tile = (wg_first, wg_second)[s]
            nc.sync.dma_start(out=tile[:].rearrange("p (a r) -> p a r", a=2), in_=words.bitcast(I32))

        def load_scale_rows(tile, shift, rows):
            passes = rows.shape[0]
            for q in range(4):
                nc.gpsimd.dma_start(
                    out=tile[32 * q + shift : 32 * q + shift + 4 * passes, :].bitcast(I32),
                    in_=rows[:, 4 * q : 4 * q + 4, :].bitcast(I32),
                )

        make_identity(nc, identity[:])
        nc.gpsimd.memset(wg_sc_raw[:].bitcast(I32), 0)
        nc.gpsimd.memset(no_bias[:], 0.0)
        load_scale_rows(wg_sc_raw, SCALE_SHIFT, wg_scales)
        for page in pages:
            nc.gpsimd.memset(page[:], 0.0)
        nc.gpsimd.memset(wd_sc[:].bitcast(I32), 0)
        load_scale_rows(wd_sc, 3 * SCALE_SHIFT, wd8_scales)
        load_scale_rows(wd_sc, 0, wd4_scales)

        for w, rows in enumerate((wgt, wgo)):
            nc.sync.dma_start(
                out=packed[w * P // 2 : (w + 1) * P // 2, :],
                in_=rows.rearrange("p (h j) -> (p h) j", h=2)[0 : 2 * P : GROUP + 1].rearrange("x (b c) -> x b c", c=P),
            )
        load_x(0, 0)
        nc.sync.dma_start(pick_list[:], offs)
        load_x(0, 1)
        load_x(0, 2)
        load_x(0, 3)
        load_wu(0, 0)
        load_x(1, 0)
        load_x(1, 1)
        load_wu(1, 0)
        load_x(1, 2)
        load_wu(0, 1)
        load_wu_last(0)
        load_x(1, 3)
        load_wg(0)
        load_wg(1)
        load_wu_last(1)
        nc.sync.dma_start(out=wd8_codes[:], in_=wd8_words[0].rearrange("p n i -> p (n i)").bitcast(I32))
        nc.sync.dma_start(out=wd4_codes[:].bitcast(I32), in_=wd4_words[0].bitcast(I32))
        with nc.allow_non_contiguous_dma(reason="one bias value for each partition and page"):
            nc.sync.dma_start(out=bias[:], in_=b.rearrange("(n p) -> p n", p=P))
        nc.sync.dma_start(place_list[:], offs2)

        def spread(copy, source, target, w, first, last):
            by_run = source[:, 0:P].rearrange("p (w g b) -> p w b g", w=2, b=RUNS)[:, w, first:last, :]
            copy(
                out=repeated[:, first * P : last * P].rearrange("p (b g r) -> p b g r", g=GROUPS, r=GROUP),
                in_=by_run.unsqueeze(3).to_broadcast([P, last - first, GROUPS, GROUP]),
            )
            for k in range(last - first):
                run = repeated[:, (first + k) * P : (first + k + 1) * P]
                nc.tensor.transpose(target[:, k * P : (k + 1) * P], run, identity[:])
            copy(out=weights[:, w * J + first * P : w * J + last * P], in_=target[:, 0 : (last - first) * P])

        def spread_weights():
            for v in range(2):
                nc.tensor.transpose(banks[v][:, 0:P], packed[:], identity[:])
            spread(nc.scalar.copy, banks[0], banks[2], 0, 0, 2)
            spread(nc.vector.tensor_copy, banks[1], banks[3], 0, 2, 4)
            spread(nc.scalar.copy, banks[0], banks[4], 0, 4, RUNS)
            spread(nc.scalar.copy, banks[0], banks[5], 1, 0, 4)
            spread(nc.scalar.copy, banks[0], banks[6], 1, 4, RUNS)

        def picks(a, lo, hi):
            return picked[a][:].rearrange("p (i j) -> p i j", i=PACK)[:, :, lo:hi]

        def gather(a, i, lo, hi):
            nc.vector.tensor_tensor(
                picks(a, lo, hi)[:, i, :],
                planes[a][i][:].indirect(pick_list[:, lo // GROUP : hi // GROUP]),
                wgt_sb[:, lo:hi],
                MULT,
            )

        def round_x(a, lo, hi):
            nc.scalar.copy(
                out=x_rounded(a, lo, hi).rearrange("p (g e i) -> p g i e", e=4, i=PACK),
                in_=picks(a, lo, hi).rearrange("p i (g e) -> p g i e", e=4),
            )

        def round_x_on_gpsimd(a, lo, hi):
            nc.gpsimd.tensor_scalar(
                x_rounded(a, lo, hi).rearrange("p (j i) -> p j i", i=PACK),
                picks(a, lo, hi).rearrange("p i j -> p j i"),
                1.0,
                0.0,
                MULT,
                ADD,
            )

        def x_words(a, lo, hi):
            if a == 0:
                return x0_codes[:, lo:hi]
            if lo >= HALF:
                return x1_late[:, lo - HALF : hi - HALF]
            start = lo // CHUNK * CHUNK
            return x1_codes[lo // CHUNK][:, lo - start : hi - start]

        def quantise_x(a, lo, hi):
            nc.vector.quantize_mx(
                out=x_words(a, lo, hi).bitcast(FP8X4), scales=x_sc[a][:, lo:hi], in_=x_rounded(a, lo, hi)
            )

        def round_wu(a, s):
            nc.scalar.copy(
                out=wu_rounded(a, s).rearrange("p (t q i) -> p q i t", q=P, i=PACK),
                in_=wu_raw[a, s][:].rearrange("p (i q t) -> p q i t", i=PACK, t=PACK),
            )

        def round_wu_last(v, copy):
            copy(
                out=wu_rounded(1, 1).rearrange("p (t q i) -> p q i t", q=P, i=PACK)[:, v * P // 2 : (v + 1) * P // 2],
                in_=wu_last[v][:].rearrange("p (i q t) -> p q i t", i=PACK, t=PACK),
            )

        def quantise_wu(a, s):
            nc.vector.quantize_mx(out=wu_codes[a, s][:].bitcast(FP8X4), scales=wu_sc[a, s], in_=wu_rounded(a, s))

        def deal_wg_words(dealt, raw):
            nc.vector.tensor_copy(
                out=dealt.rearrange("p (a t q) -> p a q t", t=PACK, q=P),
                in_=raw.rearrange("p (a q t) -> p a q t", t=PACK, q=P),
            )

        def deal_wg_scales():
            nc.vector.tensor_copy(
                out=wg_sc[:].rearrange("p (s t q) -> p s t q", t=PACK, q=P),
                in_=wg_sc_raw[:].rearrange("p (s q t) -> p s t q", t=PACK, q=P),
            )

        def first_products(turn, u, stationary):
            chunk, place = divmod(turn, BANKS)
            if chunk == 0 or place == LAST_GATE:
                bank = banks[place]
            else:
                bank = banks[((BANKS - 1) * (chunk - 1) + place - (place > LAST_GATE)) % SUM_BANKS]
            by_t = bank[:].rearrange("p (t j) -> p t j", t=PACK)
            cols = slice(u * UNIT, (u + 1) * UNIT)
            for a in range(2):
                for t in range(PACK):
                    codes, scales = stationary(a, t)
                    nc.tensor.matmul_mx(
                        out=by_t[:, t, :],
                        lhsT=codes.bitcast(FP8X4),
                        lhsT_scale=scales,
                        rhs=x_words(a, u * UNIT, (u + 1) * UNIT).bitcast(FP8X4),
                        rhs_scale=x_sc[a][:, cols],
                        start=(a == 0 and t == 0),
                        stop=(a == 1 and t == PACK - 1),
                    )
            return by_t.rearrange("p t j -> p j t")

        def factors(chunk, quarter):
            s, u = quarter // 2, 2 * chunk + quarter % 2
            step = 4 * chunk + quarter

            def wg_stationary(a, t):
                word, scale = a * PASS + t * P, s * PASS + t * P
                return wg_codes[s][:, word : word + P], wg_sc[SCALE_SHIFT * (a + 1) :, scale : scale + P]

            def wu_stationary(a, t):
                return wu_codes[a, s][:, t * P : (t + 1) * P], wu_sc[a, s][:, t * P : (t + 1) * P]

            slot = slice(step % SLOTS * PASS, (step % SLOTS + 1) * PASS)
            gated = first_gated[quarter] if chunk == 0 else gated_slots[:, slot]
            gate = first_products(2 * step, u, wg_stationary)
            nc.scalar.activation(
                out=gated.rearrange("p (j t) -> p j t", t=PACK), in_=gate, func=ACT.Tanh, bias=no_bias[:]
            )
            up = first_products(2 * step + 1, u, wu_stationary)
            if chunk == 0 or (chunk, quarter) == (1, 3):
                return nc.vector, up, gated.rearrange("p (j t) -> p j t", t=PACK)
            moved = held_place(1) if (chunk, quarter) == (2, 3) else moved_slots[:, slot]
            nc.scalar.copy(out=moved.rearrange("p (j t) -> p j t", t=PACK), in_=up)
            return nc.gpsimd, moved.rearrange("p (j t) -> p j t", t=PACK), gated.rearrange("p (j t) -> p j t", t=PACK)

        def hidden_chunk(chunk, ahead=()):
            for quarter in range(4):
                engine, up, gated = ahead[quarter] if quarter < len(ahead) else factors(chunk, quarter)
                product = h_rounded(chunk)[:, quarter * PACK * UNIT : (quarter + 1) * PACK * UNIT]
                engine.tensor_tensor(product.rearrange("p (j t) -> p j t", t=PACK), up, gated, MULT)
            codes, scales = h_codes(chunk)
            nc.vector.quantize_mx(out=codes.bitcast(FP8X4), scales=scales, in_=h_rounded(chunk))

        def output_sums(chunk, n, bank, side):
            codes, scales = h_codes(chunk)
            rows = slice(n * P, (n + 1) * P)
            acc = bank[:, side * CHUNK : (side + 1) * CHUNK]
            below, above = slice(0, CHUNK), slice(CHUNK, 2 * CHUNK)
            nc.tensor.matmul_mx(
                out=acc,
                lhsT=wd8_codes[:, rows].bitcast(FP8X4),
                lhsT_scale=wd8_sc[:, rows],
                rhs=codes[:, below].bitcast(FP8X4),
                rhs_scale=scales[:, below],
                start=True,
                stop=False,
            )
            nc.tensor.matmul_mx(
                out=acc,
                lhsT=wd4_codes[:, 2 * n * P : 2 * (n + 1) * P].bitcast(FP4X4),
                lhsT_scale=wd4_sc[:, rows],
                rhs=codes[:, above].bitcast(FP8X4),
                rhs_scale=scales[:, above],
                start=False,
                stop=True,
            )
            return acc

        def places(chunk, n):
            return pages[n][:].indirect(place_list[:, chunk * CHUNK // GROUP : (chunk + 1) * CHUNK // GROUP])

        def wgo_of(chunk):
            return wgo_sb[:, chunk * CHUNK : (chunk + 1) * CHUNK]

        def weigh_on_vector(chunk, n, acc, staged):
            nc.vector.scalar_tensor_tensor(staged, acc, bias[:, n : n + 1], wgo_of(chunk), ADD, MULT)

        def add_bias(n, acc, staged):
            nc.scalar.activation(out=staged, in_=acc, func=ACT.Identity, bias=bias[:, n : n + 1])

        def scatter(chunk, n, staged):
            nc.vector.tensor_copy(places(chunk, n), staged)

        def early_place(chunk, n):
            first = (2 * chunk + n) * CHUNK
            return early_staged[:, first : first + CHUNK]

        def scatter_by_gpsimd(chunk, n, acc):
            staged = early_place(chunk, n)
            biased = late_rounded.bitcast(F32)[:, (2 + n) * CHUNK : (3 + n) * CHUNK]
            add_bias(n, acc, biased)
            nc.gpsimd.tensor_tensor(staged, biased, wgo_of(chunk), MULT)
            scatter(chunk, n, staged)

        def scatter_held(chunk):
            staged = {n: held_place(chunk)[:, (n - 2) * CHUNK : (n - 1) * CHUNK] for n in (2, 3)}
            held = {n: output_sums(chunk, n, bank_b, n % 2) for n in (2, 3)}
            for n in (2, 3):
                weigh_on_vector(chunk, n, held[n], staged[n])
            for n in (2, 3):
                scatter(chunk, n, staged[n])

        def scatter_fused(chunk, n, acc, staged):
            add_bias(n, acc, staged)
            nc.vector.tensor_tensor(places(chunk, n), staged, wgo_of(chunk), MULT)

        def store(n):
            nc.sync.dma_start(out=out[n * P : (n + 1) * P, :], in_=pages[n][:])

        spread_weights()
        for i in range(PACK):
            if i == 0:
                gather(0, i, 0, HALF)
                gather(0, i, HALF, J)
            else:
                gather(0, i, 0, J)
        round_wu(0, 0)
        round_x(0, 0, J)
        quantise_wu(0, 0)
        gather(1, 0, 0, J)
        gather(1, 1, 0, J)
        quantise_x(0, 0, J)
        round_wu(1, 0)
        gather(1, 2, 0, J)
        quantise_wu(1, 0)
        deal_wg_scales()
        round_wu(0, 1)
        quantise_wu(0, 1)
        round_wu_last(0, nc.scalar.copy)
        gather(1, 3, 0, CHUNK)
        gather(1, 3, CHUNK, HALF)
        deal_wg_words(wg_codes[0][:], wg_first[:])
        round_x(1, 0, CHUNK)
        quantise_x(1, 0, CHUNK)
        gather(1, 3, HALF, J)
        round_x(1, CHUNK, HALF)
        round_wu_last(1, nc.scalar.copy)
        quantise_x(1, CHUNK, HALF)
        deal_wg_words(wg_codes[1][:], wg_second[:])
        quantise_wu(1, 1)
        round_x_on_gpsimd(1, HALF, J - UNIT)
        hidden_chunk(0)
        round_x(1, J - UNIT, J)
        quantise_x(1, HALF, J)

        sums = [output_sums(0, 0, bank_a, 0), output_sums(0, 1, bank_c, 0)]
        for n in range(2):
            weigh_on_vector(0, n, sums[n], early_place(0, n))
        for n in range(2):
            scatter(0, n, early_place(0, n))
        hidden_chunk(1)
        scatter_held(0)

        ahead = [factors(2, quarter) for quarter in range(2)]
        sums = [output_sums(1, n, bank_c, n) for n in range(2)]
        for n in range(2):
            scatter_by_gpsimd(1, n, sums[n])
        hidden_chunk(2, ahead)
        scatter_held(1)

        ahead = [factors(3, quarter) for quarter in range(3)]
        sums = [output_sums(2, n, bank_c, n) for n in range(2)] + [output_sums(2, 2, bank_a, 0)]
        for n in range(2):
            scatter_by_gpsimd(2, n, sums[n])
        hidden_chunk(3, ahead)
        last_slot = (SLOTS - 1) * PASS
        scatter_fused(2, 2, sums[2], moved_slots[:, last_slot : last_slot + CHUNK])

        staged = [last_staged[:, n * CHUNK : (n + 1) * CHUNK] for n in range(PAGES - 1)]
        for n, bank in enumerate((bank_b, banks[0])):
            scatter_fused(3, n, output_sums(3, n, bank, 0), staged[n])
            store(n)
        scatter_fused(3, 2, output_sums(3, 2, bank_c, 0), staged[2])
        store(2)
        both = last_staged[:, PAGES * CHUNK : (PAGES + 2) * CHUNK]
        for side in range(2):
            output_sums(2 + side, 3, banks[1], side)
        add_bias(3, banks[1][:], both)
        nc.vector.tensor_tensor(pages[3][:].indirect(place_list[:, HALF // GROUP :]), both, wgo_sb[:, HALF:], MULT)
        store(3)
